import numpy as np
import ml_dtypes


def mxq(x, axis, fmt="e4m3"):
    dtype, down = {"e4m3": (ml_dtypes.float8_e4m3fn, 7), "e5m2": (ml_dtypes.float8_e5m2, 14)}[fmt]
    v = np.moveaxis(np.asarray(x, np.float32).astype(ml_dtypes.bfloat16).astype(np.float64), axis, -1)
    blocks = v.reshape(v.shape[:-1] + (-1, 32))
    amax = np.abs(blocks).max(-1, keepdims=True)
    byte = np.maximum(np.where(amax > 0, np.frexp(amax)[1] - 1 + 127, 0) - down, 1)
    scale = np.exp2(byte - 127.0)
    codes = (blocks / scale).astype(np.float32).astype(dtype).astype(np.float64)
    return np.moveaxis((codes * scale).reshape(v.shape), -1, axis)


WIDE = False


def mx_kscale(k):
    if not WIDE:
        return np.ones(k)
    levels = np.array([10, -10, 5, -5, 0])
    if k % 512:
        return np.exp2(np.random.permutation(np.resize(levels, k // 32))).repeat(32)
    a = np.empty((k // 512, 16))
    for p in range(k // 512):
        a[p, :8] = np.random.permutation(np.resize(levels, 8))
        for g in range(8):
            far = levels[np.abs(levels - a[p, g]) >= 10]
            a[p, g + 8] = far[np.random.randint(len(far))]
    return np.exp2(a.ravel()).repeat(32)


def f64(x):
    return np.asarray(x).astype(np.float64)


def striped(idx):
    return np.tile(idx.reshape(-1, 16).T, (8, 1)).astype(np.uint16)


def unstriped(offs):
    return offs[:16].T.reshape(-1).astype(np.int64)


def pack_weight(w):
    k, n = w.shape
    w = f64(np.asarray(w, np.float32).astype(ml_dtypes.bfloat16)).reshape(k // 32, 32, n)
    amax = np.abs(w).max(1)
    byte = np.clip(np.where(amax > 0, np.frexp(amax)[1] - 1 + 127 - 7, 1), 1, 254)
    scaled = (w * np.exp2(127.0 - byte)[:, None, :]).reshape(k, n).astype(np.float32)
    words = np.ascontiguousarray(scaled.reshape(k // 512, 128, 4, n).transpose(0, 1, 3, 2)).astype(ml_dtypes.float8_e4m3fn).view(np.uint8)
    return words, np.ascontiguousarray(byte.astype(np.uint8).reshape(k // 512, 16, n))


def unpack_weight(words, scales):
    g, p, n, _ = words.shape
    vals = np.ascontiguousarray(words).view(ml_dtypes.float8_e4m3fn).astype(np.float64) * np.repeat(np.exp2(scales.astype(np.float64) - 127.0), 8, axis=1)[..., None]
    return vals.transpose(0, 1, 3, 2).reshape(g * 512, n)


def sigmoid(v):
    return 1.0 / (1.0 + np.exp(-np.maximum(v, -700.0)))


K, T, S, V, U, D = 1024, 2048, 512, 512, 256, 4
P = 2 ** 7


def setup_inputs():
    n = np.random.standard_normal
    s = mx_kscale(K)[:, None]
    packed_xT = pack_weight(n((K, T)) * s)
    return {
        "x_words": packed_xT[0],
        "x_scales": packed_xT[1],
        "hT": (n((K, V)) / np.sqrt(K) / s).astype(np.float32),
        "turn": (np.tile(np.where(np.random.uniform(size=(D, 1, U)) < 0.5, 1.0, -1.0), (1, P, 1))).astype(np.float32),
        "offs": striped(np.random.permutation(T)[:S]),
        "pos1": striped(np.random.randint(0, S, U)),
        "pos2": striped(np.random.randint(0, S, U)),
        "pos3": striped(np.random.randint(0, S, U)),
        "pos4": striped(np.random.randint(0, S, U)),
    }


def reference(x_words, x_scales, hT, turn, offs, pos1, pos2, pos3, pos4):
    hTq = mxq(f64(hT), 0, "e4m3")
    xq = unpack_weight(x_words, x_scales)[:, unstriped(offs)]
    y = hTq.T @ xq
    z0 = y[:, unstriped(pos1)] * f64(turn)[0, :1]
    z1 = y[:, unstriped(pos2)] * f64(turn)[1, :1]
    z2 = y[:, unstriped(pos3)] * f64(turn)[2, :1]
    z3 = y[:, unstriped(pos4)] * f64(turn)[3, :1]
    return ((sigmoid(z0) * sigmoid(z1)) * sigmoid(z2)) * sigmoid(z3)

@@ -1,0 +1,203 @@
+from contextlib import ExitStack
+
+import concourse.mybir as mybir
+from concourse.masks import make_identity
+
+K, T, S, V, U, D = 1024, 2048, 512, 512, 256, 4
+FLOPS = 2 * K * V * S
+
+F32 = mybir.dt.float32
+BF16 = mybir.dt.bfloat16
+I32 = mybir.dt.int32
+U32 = mybir.dt.uint32
+U16 = mybir.dt.uint16
+U8 = mybir.dt.uint8
+FP8X4 = mybir.dt.float8_e4m3fn_x4
+MULT = mybir.AluOpType.mult
+ADD = mybir.AluOpType.add
+SIGMOID = mybir.ActivationFunctionType.Sigmoid
+
+P = 128
+PACK = 4
+PASSES = K // (P * PACK)
+BLOCKS = V // P
+HALVES = U // P
+RUNS = P // 4
+VECTOR_RUNS = 20
+SCALAR_LISTS = (2,2,2,2)
+SCALAR_ROUNDS = (0,0,0,0)
+H_LOADS = ((0, 1), (1, 1), (2, 2))
+
+
+def tile_picked_yhs_prob_p_kernel(tc, x_words, x_scales, hT, turn, offs, pos1, pos2, pos3, pos4, out):
+    nc = tc.nc
+    with ExitStack() as ctx:
+        keep = ctx.enter_context(tc.tile_pool(name="keep", bufs=1))
+        work = ctx.enter_context(tc.tile_pool(name="work", bufs=2))
+        psum = ctx.enter_context(tc.psum_pool(name="psum", bufs=1))
+
+        node_list = keep.tile([P, S // 16], U16, name="node_list")
+        path_lists = [keep.tile([P, U // 16], U16, name="path_list%d" % d) for d in range(D)]
+        word_table = [keep.tile([P, T], U32, name="word_table%d" % o) for o in range(PASSES)]
+        scale_table = keep.tile([P, T], U8, name="scale_table")
+        node_words = [keep.tile([P, S], U32, name="node_words%d" % o, align_bytes=64) for o in range(PASSES)]
+        node_scales = keep.tile([P, S], U8, name="node_scales", align_bytes=64)
+        identity = keep.tile([P, P], F32, name="identity")
+        turn_rows = keep.tile([P, P], F32, name="turn_rows")
+        turn_cols = keep.tile([P, D * HALVES], F32, name="turn_cols")
+        turns = keep.tile([P, D, U], F32, name="turns")
+        h_bf16 = [keep.tile([P, PASSES, P * PACK], BF16, name="h_bf16_%d" % b, align_bytes=64) for b in range(BLOCKS)]
+        h_words = [keep.tile([P, PASSES, P], U32, name="h_words%d" % b, align_bytes=64) for b in range(BLOCKS)]
+        h_scales = [keep.tile([P, PASSES, P], U8, name="h_scales%d" % b, align_bytes=64) for b in range(BLOCKS)]
+        h_raw = {}
+
+        def load_words(o):
+            nc.sync.dma_start(
+                out=word_table[o][:].bitcast(I32),
+                in_=x_words[o].rearrange("p n r -> p (n r)").bitcast(I32),
+            )
+
+        def load_h(first, count):
+            raw = keep.tile([P, PASSES, PACK, count * P], F32, name="h_raw", tag="h_raw%d" % first)
+            for o in range(PASSES):
+                rows = hT[o * P * PACK : (o + 1) * P * PACK, first * P : (first + count) * P]
+                nc.sync.dma_start(out=raw[:, o], in_=rows.rearrange("(p j) t -> p j t", j=PACK))
+            for b in range(count):
+                h_raw[first + b] = raw[:, :, :, b * P : (b + 1) * P]
+
+        def woven(b):
+            return (
+                h_bf16[b][:].rearrange("p o (c i j) -> p o c j i", i=4, j=PACK),
+                h_raw[b].rearrange("p o j (c i) -> p o c j i", i=4),
+            )
+
+        nc.vector.memset(scale_table[:].bitcast(I32), 0)
+        nc.vector.memset(turn_rows[:], 0.0)
+        nc.sync.dma_start(node_list[:], offs)
+        for q in range(4):
+            nc.sync.dma_start(
+                out=scale_table[32 * q : 32 * q + 4 * PASSES, :].bitcast(I32),
+                in_=x_scales[:, 4 * q : 4 * q + 4, :].bitcast(I32),
+            )
+        load_words(0)
+        nc.sync.dma_start(path_lists[0][:], pos1)
+        nc.sync.dma_start(path_lists[1][:], pos2)
+        load_words(1)
+        nc.scalar.dma_start(
+            out=turn_rows[0 : D * HALVES, :],
+            in_=turn[:, 0, :].rearrange("d (h c) -> d h c", h=HALVES),
+        )
+        load_h(*H_LOADS[0])
+        nc.sync.dma_start(path_lists[2][:], pos3)
+        nc.sync.dma_start(path_lists[3][:], pos4)
+        for first, count in H_LOADS[1:]:
+            load_h(first, count)
+
+        make_identity(nc, identity[:])
+        turned = psum.tile([P, P], F32, name="turned", tag="bank_t")
+        nc.tensor.transpose(turned[:], turn_rows[:], identity[:])
+        nc.scalar.copy(out=turn_cols[:], in_=turned[:, 0 : D * HALVES])
+        for pair in range(D // 2):
+            spread = psum.tile([P, 2 * HALVES, P], F32, name="spread", tag="bank_s%d" % pair)
+            for j in range(2 * HALVES):
+                col = 2 * HALVES * pair + j
+                nc.tensor.transpose(spread[:, j, :], turn_cols[:, col : col + 1].to_broadcast([P, P]), identity[:])
+            nc.scalar.copy(
+                out=turns[:, 2 * pair : 2 * pair + 2, :].rearrange("p d u -> p (d u)"),
+                in_=spread[:].rearrange("p j c -> p (j c)"),
+            )
+
+        nc.vector.tensor_copy(node_words[0][:], word_table[0][:].indirect(node_list[:]))
+        nc.vector.tensor_copy(node_scales[:], scale_table[:].indirect(node_list[:]))
+        nc.vector.tensor_copy(node_words[1][:], word_table[1][:].indirect(node_list[:]))
+
+        def product(acc, b, o, cols):
+            nc.tensor.matmul_mx(
+                out=acc,
+                lhsT=h_words[b][:, o, :].bitcast(FP8X4),
+                lhsT_scale=h_scales[b][:, o, :],
+                rhs=node_words[o][:, cols].bitcast(FP8X4),
+                rhs_scale=node_scales[4 * o : P, cols],
+                start=(o == 0),
+                stop=(o == PASSES - 1),
+            )
+
+        def first_scores():
+            dst, src = woven(0)
+            nc.scalar.copy(out=dst[:, 0], in_=src[:, 0])
+            nc.vector.tensor_copy(out=dst[:, 1, 0:VECTOR_RUNS], in_=src[:, 1, 0:VECTOR_RUNS])
+            nc.scalar.copy(out=dst[:, 1, VECTOR_RUNS:RUNS], in_=src[:, 1, VECTOR_RUNS:RUNS])
+            halves = [psum.tile([P, S // 2], F32, name="acc_half", tag="bank_y0_%d" % n) for n in range(2)]
+            cols = [slice(n * S // 2, (n + 1) * S // 2) for n in range(2)]
+            for o in range(PASSES):
+                nc.vector.quantize_mx(out=h_words[0][:, o, :].bitcast(FP8X4), scales=h_scales[0][:, o, :], in_=h_bf16[0][:, o, :])
+                for n in range(2):
+                    product(halves[n][:], 0, o, cols[n])
+            y = keep.tile([P, S], F32, name="y0")
+            nc.scalar.copy(out=y[:, cols[0]], in_=halves[0][:])
+            nc.vector.tensor_copy(out=y[:, cols[1]], in_=halves[1][:])
+            return y
+
+        def round_h(b):
+            dst, src = woven(b)
+            copy = nc.scalar.copy if SCALAR_ROUNDS[b] else nc.vector.tensor_copy
+            copy(out=dst, in_=src)
+
+        def quantize_h(b):
+            nc.vector.quantize_mx(
+                out=h_words[b][:].rearrange("p o t -> p (o t)").bitcast(FP8X4),
+                scales=h_scales[b][:].rearrange("p o t -> p (o t)"),
+                in_=h_bf16[b][:].rearrange("p o t -> p (o t)"),
+            )
+
+        def scores(b):
+            acc = psum.tile([P, S], F32, name="acc", tag="bank_y%d" % b)
+            for o in range(PASSES):
+                product(acc[:], b, o, slice(0, S))
+            y = keep.tile([P, S], F32, name="y%d" % b)
+            nc.scalar.copy(out=y[:], in_=acc[:])
+            return y
+
+        def paths(b, y):
+            on_scalar = SCALAR_LISTS[b]
+            on_vector = D - on_scalar
+            held = [first for first, count in H_LOADS if first == b + 1]
+            z_tag = "h_raw%d" % held[0] if held else "z%d" % b
+            z = keep.tile([P, on_vector, U], F32, name="z", tag=z_tag)
+            plain = work.tile([P, on_scalar, U], F32, name="plain")
+            exact = work.tile([P, on_vector, U], F32, name="exact")
+            centred = work.tile([P, on_scalar, U], F32, name="centred")
+            steps = work.tile([P, 2, U], F32, name="steps")
+            prob = work.tile([P, U], F32, name="prob")
+            for d in range(on_vector):
+                nc.vector.tensor_tensor(z[:, d, :], y[:].indirect(path_lists[d][:]), turns[:, d, :], MULT)
+            if on_scalar == 2:
+                for d in range(on_scalar):
+                    nc.scalar.activation(plain[:, d, :], y[:].indirect(path_lists[on_vector + d][:]), SIGMOID)
+                nc.scalar.activation(exact[:], z[:], SIGMOID)
+                nc.vector.scalar_tensor_tensor(centred[:], plain[:], -0.5, turns[:, on_vector:D, :], ADD, MULT)
+                nc.vector.scalar_tensor_tensor(steps[:], centred[:], 0.5, exact[:], ADD, MULT)
+                nc.vector.tensor_tensor(prob[:], steps[:, 0, :], steps[:, 1, :], MULT)
+            else:
+                so_far = exact[:, 0, :]
+                for d in range(on_scalar):
+                    nc.scalar.activation(plain[:, d, :], y[:].indirect(path_lists[on_vector + d][:]), SIGMOID)
+                    if d == 0:
+                        nc.scalar.activation(exact[:], z[:], SIGMOID)
+                    nc.vector.scalar_tensor_tensor(centred[:, d, :], plain[:, d, :], -0.5, turns[:, on_vector + d, :], ADD, MULT)
+                    target = prob[:] if d == on_scalar - 1 else steps[:, d, :]
+                    nc.vector.scalar_tensor_tensor(target, centred[:, d, :], 0.5, so_far, ADD, MULT)
+                    so_far = target
+            nc.sync.dma_start(out=out[b * P : (b + 1) * P, :], in_=prob[:])
+
+        ys = {0: first_scores()}
+        for b in range(BLOCKS):
+            for first, count in H_LOADS:
+                if first == b + 1:
+                    for n in range(first, first + count):
+                        round_h(n)
+                    for n in range(first, first + count):
+                        quantize_h(n)
+            if b + 1 < BLOCKS:
+                ys[b + 1] = scores(b + 1)
+            paths(b, ys[b])

@@ -26,14 +26,14 @@ RUNS = P // 4
 VECTOR_RUNS = 20
 SCALAR_LISTS = (2,2,2,2)
 SCALAR_ROUNDS = (0,0,0,0)
-H_LOADS = ((0, 1), (1, 1), (2, 2))
+H_LOADS = ((0, 1), (1, 1), (2, 1), (3, 1))
 
 
 def tile_picked_yhs_prob_p_kernel(tc, x_words, x_scales, hT, turn, offs, pos1, pos2, pos3, pos4, out):
     nc = tc.nc
     with ExitStack() as ctx:
         keep = ctx.enter_context(tc.tile_pool(name="keep", bufs=1))
-        work = ctx.enter_context(tc.tile_pool(name="work", bufs=2))
+        work = ctx.enter_context(tc.tile_pool(name="work", bufs=4))
         psum = ctx.enter_context(tc.psum_pool(name="psum", bufs=1))
 
         node_list = keep.tile([P, S // 16], U16, name="node_list")
@@ -51,11 +51,11 @@ def tile_picked_yhs_prob_p_kernel(tc, x_words, x_scales, hT, turn, offs, pos1, p
         h_scales = [keep.tile([P, PASSES, P], U8, name="h_scales%d" % b, align_bytes=64) for b in range(BLOCKS)]
         h_raw = {}
 
-        def load_words(o):
-            nc.sync.dma_start(
-                out=word_table[o][:].bitcast(I32),
-                in_=x_words[o].rearrange("p n r -> p (n r)").bitcast(I32),
-            )
+        def load_words(o, pieces):
+            words = x_words[o].rearrange("p n r -> p (n r)").bitcast(I32)
+            for n in range(pieces):
+                cols = slice(n * T // pieces, (n + 1) * T // pieces)
+                nc.sync.dma_start(out=word_table[o][:, cols].bitcast(I32), in_=words[:, cols])
 
         def load_h(first, count):
             raw = keep.tile([P, PASSES, PACK, count * P], F32, name="h_raw", tag="h_raw%d" % first)
@@ -72,22 +72,22 @@ def tile_picked_yhs_prob_p_kernel(tc, x_words, x_scales, hT, turn, offs, pos1, p
             )
 
         nc.vector.memset(scale_table[:].bitcast(I32), 0)
-        nc.vector.memset(turn_rows[:], 0.0)
+        nc.gpsimd.memset(turn_rows[:], 0.0)
         nc.sync.dma_start(node_list[:], offs)
         for q in range(4):
             nc.sync.dma_start(
                 out=scale_table[32 * q : 32 * q + 4 * PASSES, :].bitcast(I32),
                 in_=x_scales[:, 4 * q : 4 * q + 4, :].bitcast(I32),
             )
-        load_words(0)
+        load_words(0, 1)
         nc.sync.dma_start(path_lists[0][:], pos1)
-        nc.sync.dma_start(path_lists[1][:], pos2)
-        load_words(1)
-        nc.scalar.dma_start(
+        nc.sync.dma_start(
             out=turn_rows[0 : D * HALVES, :],
             in_=turn[:, 0, :].rearrange("d (h c) -> d h c", h=HALVES),
         )
+        load_words(1, 1)
         load_h(*H_LOADS[0])
+        nc.sync.dma_start(path_lists[1][:], pos2)
         nc.sync.dma_start(path_lists[2][:], pos3)
         nc.sync.dma_start(path_lists[3][:], pos4)
         for first, count in H_LOADS[1:]:
@@ -135,13 +135,17 @@ def tile_picked_yhs_prob_p_kernel(tc, x_words, x_scales, hT, turn, offs, pos1, p
                     product(halves[n][:], 0, o, cols[n])
             y = keep.tile([P, S], F32, name="y0")
             nc.scalar.copy(out=y[:, cols[0]], in_=halves[0][:])
-            nc.vector.tensor_copy(out=y[:, cols[1]], in_=halves[1][:])
+            nc.scalar.copy(out=y[:, cols[1]], in_=halves[1][:])
             return y
 
         def round_h(b):
             dst, src = woven(b)
-            copy = nc.scalar.copy if SCALAR_ROUNDS[b] else nc.vector.tensor_copy
-            copy(out=dst, in_=src)
+            if b == 3:
+                nc.vector.tensor_copy(out=dst, in_=src)
+            else:
+                copy = nc.scalar.copy if b == 2 else nc.vector.tensor_copy
+                for o in range(PASSES):
+                    copy(out=dst[:, o], in_=src[:, o])
 
         def quantize_h(b):
             nc.vector.quantize_mx(
@@ -158,46 +162,55 @@ def tile_picked_yhs_prob_p_kernel(tc, x_words, x_scales, hT, turn, offs, pos1, p
             nc.scalar.copy(out=y[:], in_=acc[:])
             return y
 
-        def paths(b, y):
-            on_scalar = SCALAR_LISTS[b]
-            on_vector = D - on_scalar
-            held = [first for first, count in H_LOADS if first == b + 1]
-            z_tag = "h_raw%d" % held[0] if held else "z%d" % b
-            z = keep.tile([P, on_vector, U], F32, name="z", tag=z_tag)
-            plain = work.tile([P, on_scalar, U], F32, name="plain")
-            exact = work.tile([P, on_vector, U], F32, name="exact")
-            centred = work.tile([P, on_scalar, U], F32, name="centred")
-            steps = work.tile([P, 2, U], F32, name="steps")
+        ys, zs, plains, exacts, centreds, pairs = {}, {}, {}, {}, {}, {}
+
+        def signed_score(b, d):
+            if d == 0:
+                zs[b] = work.tile([P, 2, U], F32, name="z")
+            nc.vector.tensor_tensor(zs[b][:, d, :], ys[b][:].indirect(path_lists[d][:]), turns[:, d, :], MULT)
+
+        def plain_sigmoids(b):
+            plains[b] = work.tile([P, 2, U], F32, name="plain")
+            for d in range(2):
+                nc.scalar.activation(plains[b][:, d, :], ys[b][:].indirect(path_lists[2 + d][:]), SIGMOID)
+
+        def exact_sigmoids(b):
+            exacts[b] = work.tile([P, 2, U], F32, name="exact")
+            nc.scalar.activation(exacts[b][:], zs[b][:], SIGMOID)
+
+        def centre(b):
+            centreds[b] = work.tile([P, 2, U], F32, name="centred")
+            nc.vector.scalar_tensor_tensor(centreds[b][:], plains[b][:], -0.5, turns[:, 2:D, :], ADD, MULT)
+
+        def pair_up(b):
+            pairs[b] = work.tile([P, 2, U], F32, name="pairs")
+            nc.vector.scalar_tensor_tensor(pairs[b][:], centreds[b][:], 0.5, exacts[b][:], ADD, MULT)
+
+        def finish(b):
             prob = work.tile([P, U], F32, name="prob")
-            for d in range(on_vector):
-                nc.vector.tensor_tensor(z[:, d, :], y[:].indirect(path_lists[d][:]), turns[:, d, :], MULT)
-            if on_scalar == 2:
-                for d in range(on_scalar):
-                    nc.scalar.activation(plain[:, d, :], y[:].indirect(path_lists[on_vector + d][:]), SIGMOID)
-                nc.scalar.activation(exact[:], z[:], SIGMOID)
-                nc.vector.scalar_tensor_tensor(centred[:], plain[:], -0.5, turns[:, on_vector:D, :], ADD, MULT)
-                nc.vector.scalar_tensor_tensor(steps[:], centred[:], 0.5, exact[:], ADD, MULT)
-                nc.vector.tensor_tensor(prob[:], steps[:, 0, :], steps[:, 1, :], MULT)
-            else:
-                so_far = exact[:, 0, :]
-                for d in range(on_scalar):
-                    nc.scalar.activation(plain[:, d, :], y[:].indirect(path_lists[on_vector + d][:]), SIGMOID)
-                    if d == 0:
-                        nc.scalar.activation(exact[:], z[:], SIGMOID)
-                    nc.vector.scalar_tensor_tensor(centred[:, d, :], plain[:, d, :], -0.5, turns[:, on_vector + d, :], ADD, MULT)
-                    target = prob[:] if d == on_scalar - 1 else steps[:, d, :]
-                    nc.vector.scalar_tensor_tensor(target, centred[:, d, :], 0.5, so_far, ADD, MULT)
-                    so_far = target
+            nc.vector.tensor_tensor(prob[:], pairs[b][:, 0, :], pairs[b][:, 1, :], MULT)
             nc.sync.dma_start(out=out[b * P : (b + 1) * P, :], in_=prob[:])
 
-        ys = {0: first_scores()}
+        ys[0] = first_scores()
+        round_h(1)
+        quantize_h(1)
         for b in range(BLOCKS):
-            for first, count in H_LOADS:
-                if first == b + 1:
-                    for n in range(first, first + count):
-                        round_h(n)
-                    for n in range(first, first + count):
-                        quantize_h(n)
+            signed_score(b, 0)
+            plain_sigmoids(b)
+            if b > 0:
+                pair_up(b - 1)
+            signed_score(b, 1)
+            if b > 0:
+                finish(b - 1)
+            else:
+                round_h(3)
             if b + 1 < BLOCKS:
                 ys[b + 1] = scores(b + 1)
-            paths(b, ys[b])
+            exact_sigmoids(b)
+            centre(b)
+            if b == 0:
+                round_h(2)
+                quantize_h(2)
+                quantize_h(3)
+        pair_up(BLOCKS - 1)
+        finish(BLOCKS - 1)

@@ -140,12 +140,11 @@ def tile_picked_yhs_prob_p_kernel(tc, x_words, x_scales, hT, turn, offs, pos1, p
 
         def round_h(b):
             dst, src = woven(b)
-            if b == 3:
+            if b > 1:
                 nc.vector.tensor_copy(out=dst, in_=src)
             else:
-                copy = nc.scalar.copy if b == 2 else nc.vector.tensor_copy
                 for o in range(PASSES):
-                    copy(out=dst[:, o], in_=src[:, o])
+                    nc.vector.tensor_copy(out=dst[:, o], in_=src[:, o])
 
         def quantize_h(b):
             nc.vector.quantize_mx(
@@ -162,55 +161,48 @@ def tile_picked_yhs_prob_p_kernel(tc, x_words, x_scales, hT, turn, offs, pos1, p
             nc.scalar.copy(out=y[:], in_=acc[:])
             return y
 
-        ys, zs, plains, exacts, centreds, pairs = {}, {}, {}, {}, {}, {}
+        ys, zs, plains, centreds, so_far = {}, {}, {}, {}, {}
 
-        def signed_score(b, d):
-            if d == 0:
-                zs[b] = work.tile([P, 2, U], F32, name="z")
-            nc.vector.tensor_tensor(zs[b][:, d, :], ys[b][:].indirect(path_lists[d][:]), turns[:, d, :], MULT)
+        def signed_score(b):
+            zs[b] = work.tile([P, U], F32, name="z")
+            nc.vector.tensor_tensor(zs[b][:], ys[b][:].indirect(path_lists[0][:]), turns[:, 0, :], MULT)
 
-        def plain_sigmoids(b):
-            plains[b] = work.tile([P, 2, U], F32, name="plain")
-            for d in range(2):
-                nc.scalar.activation(plains[b][:, d, :], ys[b][:].indirect(path_lists[2 + d][:]), SIGMOID)
+        def signed_sigmoid(b):
+            so_far[b] = work.tile([P, U], F32, name="first")
+            nc.scalar.activation(so_far[b][:], zs[b][:], SIGMOID)
 
-        def exact_sigmoids(b):
-            exacts[b] = work.tile([P, 2, U], F32, name="exact")
-            nc.scalar.activation(exacts[b][:], zs[b][:], SIGMOID)
+        def plain_sigmoid(b, d):
+            plains[b, d] = work.tile([P, U], F32, name="plain%d" % d)
+            nc.scalar.activation(plains[b, d][:], ys[b][:].indirect(path_lists[d][:]), SIGMOID)
 
-        def centre(b):
-            centreds[b] = work.tile([P, 2, U], F32, name="centred")
-            nc.vector.scalar_tensor_tensor(centreds[b][:], plains[b][:], -0.5, turns[:, 2:D, :], ADD, MULT)
+        def centre(b, d):
+            centreds[b, d] = work.tile([P, U], F32, name="centred%d" % d)
+            nc.vector.scalar_tensor_tensor(centreds[b, d][:], plains[b, d][:], -0.5, turns[:, d, :], ADD, MULT)
 
-        def pair_up(b):
-            pairs[b] = work.tile([P, 2, U], F32, name="pairs")
-            nc.vector.scalar_tensor_tensor(pairs[b][:], centreds[b][:], 0.5, exacts[b][:], ADD, MULT)
-
-        def finish(b):
-            prob = work.tile([P, U], F32, name="prob")
-            nc.vector.tensor_tensor(prob[:], pairs[b][:, 0, :], pairs[b][:, 1, :], MULT)
-            nc.sync.dma_start(out=out[b * P : (b + 1) * P, :], in_=prob[:])
+        def multiply(b, d):
+            longer = work.tile([P, U], F32, name="longer%d" % d)
+            nc.vector.scalar_tensor_tensor(longer[:], centreds[b, d][:], 0.5, so_far[b][:], ADD, MULT)
+            so_far[b] = longer
+            if d == D - 1:
+                nc.sync.dma_start(out=out[b * P : (b + 1) * P, :], in_=longer[:])
 
         ys[0] = first_scores()
         round_h(1)
         quantize_h(1)
         for b in range(BLOCKS):
-            signed_score(b, 0)
-            plain_sigmoids(b)
-            if b > 0:
-                pair_up(b - 1)
-            signed_score(b, 1)
-            if b > 0:
-                finish(b - 1)
-            else:
-                round_h(3)
+            signed_score(b)
+            for d in range(1, D):
+                plain_sigmoid(b, d)
+                if d == 2:
+                    signed_sigmoid(b)
+                if b > 0:
+                    multiply(b - 1, d)
+                elif d < 3:
+                    round_h(d + 1)
+                centre(b, d)
+                if b == 0 and d < 3:
+                    quantize_h(d + 1)
             if b + 1 < BLOCKS:
                 ys[b + 1] = scores(b + 1)
-            exact_sigmoids(b)
-            centre(b)
-            if b == 0:
-                round_h(2)
-                quantize_h(2)
-                quantize_h(3)
-        pair_up(BLOCKS - 1)
-        finish(BLOCKS - 1)
+        for d in range(1, D):
+            multiply(BLOCKS - 1, d)

@@ -20,20 +20,21 @@ SIGMOID = mybir.ActivationFunctionType.Sigmoid
 P = 128
 PACK = 4
 PASSES = K // (P * PACK)
+QUADRANTS = 4
+SCALE_ROWS = 4
 BLOCKS = V // P
-HALVES = U // P
-RUNS = P // 4
+LAST = BLOCKS - 1
+TURN_ROWS = D * U // P
+RUN = 4
+RUNS = P // RUN
 VECTOR_RUNS = 20
-SCALAR_LISTS = (2,2,2,2)
-SCALAR_ROUNDS = (0,0,0,0)
-H_LOADS = ((0, 1), (1, 1), (2, 1), (3, 1))
+VECTOR_BANK = 2
 
 
 def tile_picked_yhs_prob_p_kernel(tc, x_words, x_scales, hT, turn, offs, pos1, pos2, pos3, pos4, out):
     nc = tc.nc
     with ExitStack() as ctx:
         keep = ctx.enter_context(tc.tile_pool(name="keep", bufs=1))
-        work = ctx.enter_context(tc.tile_pool(name="work", bufs=4))
         psum = ctx.enter_context(tc.psum_pool(name="psum", bufs=1))
 
         node_list = keep.tile([P, S // 16], U16, name="node_list")
@@ -44,107 +45,75 @@ def tile_picked_yhs_prob_p_kernel(tc, x_words, x_scales, hT, turn, offs, pos1, p
         node_scales = keep.tile([P, S], U8, name="node_scales", align_bytes=64)
         identity = keep.tile([P, P], F32, name="identity")
         turn_rows = keep.tile([P, P], F32, name="turn_rows")
-        turn_cols = keep.tile([P, D * HALVES], F32, name="turn_cols")
+        turn_cols = keep.tile([P, TURN_ROWS], F32, name="turn_cols")
         turns = keep.tile([P, D, U], F32, name="turns")
-        h_bf16 = [keep.tile([P, PASSES, P * PACK], BF16, name="h_bf16_%d" % b, align_bytes=64) for b in range(BLOCKS)]
+        h_raw = [
+            keep.tile([P, PASSES, PACK, P], F32, name="h_raw", tag="h_raw%d" % b, align_bytes=64)
+            for b in range(BLOCKS)
+        ]
+        h_bf16 = [
+            keep.tile([P, PASSES, P * PACK], BF16, name="h_bf16", tag="h_bf16_%d" % b, align_bytes=64)
+            for b in range(BLOCKS)
+        ]
         h_words = [keep.tile([P, PASSES, P], U32, name="h_words%d" % b, align_bytes=64) for b in range(BLOCKS)]
         h_scales = [keep.tile([P, PASSES, P], U8, name="h_scales%d" % b, align_bytes=64) for b in range(BLOCKS)]
-        h_raw = {}
 
-        def load_words(o, pieces):
+        def load_words(o):
             words = x_words[o].rearrange("p n r -> p (n r)").bitcast(I32)
-            for n in range(pieces):
-                cols = slice(n * T // pieces, (n + 1) * T // pieces)
-                nc.sync.dma_start(out=word_table[o][:, cols].bitcast(I32), in_=words[:, cols])
+            nc.sync.dma_start(out=word_table[o][:].bitcast(I32), in_=words)
 
-        def load_h(first, count):
-            raw = keep.tile([P, PASSES, PACK, count * P], F32, name="h_raw", tag="h_raw%d" % first)
+        def load_h(b):
             for o in range(PASSES):
-                rows = hT[o * P * PACK : (o + 1) * P * PACK, first * P : (first + count) * P]
-                nc.sync.dma_start(out=raw[:, o], in_=rows.rearrange("(p j) t -> p j t", j=PACK))
-            for b in range(count):
-                h_raw[first + b] = raw[:, :, :, b * P : (b + 1) * P]
-
-        def woven(b):
-            return (
-                h_bf16[b][:].rearrange("p o (c i j) -> p o c j i", i=4, j=PACK),
-                h_raw[b].rearrange("p o j (c i) -> p o c j i", i=4),
-            )
+                rows = hT[o * P * PACK : (o + 1) * P * PACK, b * P : (b + 1) * P]
+                nc.sync.dma_start(out=h_raw[b][:, o], in_=rows.rearrange("(p j) t -> p j t", j=PACK))
 
         nc.vector.memset(scale_table[:].bitcast(I32), 0)
         nc.gpsimd.memset(turn_rows[:], 0.0)
         nc.sync.dma_start(node_list[:], offs)
-        for q in range(4):
+        for q in range(QUADRANTS):
             nc.sync.dma_start(
-                out=scale_table[32 * q : 32 * q + 4 * PASSES, :].bitcast(I32),
-                in_=x_scales[:, 4 * q : 4 * q + 4, :].bitcast(I32),
+                out=scale_table[32 * q : 32 * q + SCALE_ROWS * PASSES, :].bitcast(I32),
+                in_=x_scales[:, SCALE_ROWS * q : SCALE_ROWS * (q + 1), :].bitcast(I32),
             )
-        load_words(0, 1)
+        load_words(0)
         nc.sync.dma_start(path_lists[0][:], pos1)
         nc.sync.dma_start(
-            out=turn_rows[0 : D * HALVES, :],
-            in_=turn[:, 0, :].rearrange("d (h c) -> d h c", h=HALVES),
+            out=turn_rows[0:TURN_ROWS, :],
+            in_=turn[:, 0, :].rearrange("d (h c) -> d h c", c=P),
         )
-        load_words(1, 1)
-        load_h(*H_LOADS[0])
-        nc.sync.dma_start(path_lists[1][:], pos2)
-        nc.sync.dma_start(path_lists[2][:], pos3)
-        nc.sync.dma_start(path_lists[3][:], pos4)
-        for first, count in H_LOADS[1:]:
-            load_h(first, count)
+        load_words(1)
+        load_h(0)
+        for path_list, pos in zip(path_lists[1:], (pos2, pos3, pos4)):
+            nc.sync.dma_start(path_list[:], pos)
+        for b in range(1, BLOCKS):
+            load_h(b)
 
         make_identity(nc, identity[:])
-        turned = psum.tile([P, P], F32, name="turned", tag="bank_t")
+        warm_up = keep.tile([P, 1], F32, name="warm_up")
+        nc.scalar.activation(warm_up[:], identity[:, 0:1], SIGMOID)
+
+        turned = psum.tile([P, P], F32, name="turned")
         nc.tensor.transpose(turned[:], turn_rows[:], identity[:])
-        nc.scalar.copy(out=turn_cols[:], in_=turned[:, 0 : D * HALVES])
+        nc.scalar.copy(out=turn_cols[:], in_=turned[:, 0:TURN_ROWS])
         for pair in range(D // 2):
-            spread = psum.tile([P, 2 * HALVES, P], F32, name="spread", tag="bank_s%d" % pair)
-            for j in range(2 * HALVES):
-                col = 2 * HALVES * pair + j
-                nc.tensor.transpose(spread[:, j, :], turn_cols[:, col : col + 1].to_broadcast([P, P]), identity[:])
+            spread = psum.tile([P, TURN_ROWS // 2, P], F32, name="spread%d" % pair)
+            for n in range(TURN_ROWS // 2):
+                col = pair * TURN_ROWS // 2 + n
+                nc.tensor.transpose(spread[:, n, :], turn_cols[:, col : col + 1].to_broadcast([P, P]), identity[:])
             nc.scalar.copy(
                 out=turns[:, 2 * pair : 2 * pair + 2, :].rearrange("p d u -> p (d u)"),
-                in_=spread[:].rearrange("p j c -> p (j c)"),
+                in_=spread[:].rearrange("p n c -> p (n c)"),
             )
 
         nc.vector.tensor_copy(node_words[0][:], word_table[0][:].indirect(node_list[:]))
         nc.vector.tensor_copy(node_scales[:], scale_table[:].indirect(node_list[:]))
         nc.vector.tensor_copy(node_words[1][:], word_table[1][:].indirect(node_list[:]))
 
-        def product(acc, b, o, cols):
-            nc.tensor.matmul_mx(
-                out=acc,
-                lhsT=h_words[b][:, o, :].bitcast(FP8X4),
-                lhsT_scale=h_scales[b][:, o, :],
-                rhs=node_words[o][:, cols].bitcast(FP8X4),
-                rhs_scale=node_scales[4 * o : P, cols],
-                start=(o == 0),
-                stop=(o == PASSES - 1),
+        def rounding_views(b):
+            return (
+                h_bf16[b][:].rearrange("p o (c i j) -> p o c j i", i=RUN, j=PACK),
+                h_raw[b][:].rearrange("p o j (c i) -> p o c j i", i=RUN),
             )
-
-        def first_scores():
-            dst, src = woven(0)
-            nc.scalar.copy(out=dst[:, 0], in_=src[:, 0])
-            nc.vector.tensor_copy(out=dst[:, 1, 0:VECTOR_RUNS], in_=src[:, 1, 0:VECTOR_RUNS])
-            nc.scalar.copy(out=dst[:, 1, VECTOR_RUNS:RUNS], in_=src[:, 1, VECTOR_RUNS:RUNS])
-            halves = [psum.tile([P, S // 2], F32, name="acc_half", tag="bank_y0_%d" % n) for n in range(2)]
-            cols = [slice(n * S // 2, (n + 1) * S // 2) for n in range(2)]
-            for o in range(PASSES):
-                nc.vector.quantize_mx(out=h_words[0][:, o, :].bitcast(FP8X4), scales=h_scales[0][:, o, :], in_=h_bf16[0][:, o, :])
-                for n in range(2):
-                    product(halves[n][:], 0, o, cols[n])
-            y = keep.tile([P, S], F32, name="y0")
-            nc.scalar.copy(out=y[:, cols[0]], in_=halves[0][:])
-            nc.scalar.copy(out=y[:, cols[1]], in_=halves[1][:])
-            return y
-
-        def round_h(b):
-            dst, src = woven(b)
-            if b > 1:
-                nc.vector.tensor_copy(out=dst, in_=src)
-            else:
-                for o in range(PASSES):
-                    nc.vector.tensor_copy(out=dst[:, o], in_=src[:, o])
 
         def quantize_h(b):
             nc.vector.quantize_mx(
@@ -153,56 +122,86 @@ def tile_picked_yhs_prob_p_kernel(tc, x_words, x_scales, hT, turn, offs, pos1, p
                 in_=h_bf16[b][:].rearrange("p o t -> p (o t)"),
             )
 
+        def product(acc, b, o, cols):
+            nc.tensor.matmul_mx(
+                out=acc,
+                lhsT=h_words[b][:, o, :].bitcast(FP8X4),
+                lhsT_scale=h_scales[b][:, o, :],
+                rhs=node_words[o][:, cols].bitcast(FP8X4),
+                rhs_scale=node_scales[SCALE_ROWS * o : P, cols],
+                start=(o == 0),
+                stop=(o == PASSES - 1),
+            )
+
+        def first_scores():
+            dst, src = rounding_views(0)
+            nc.scalar.copy(out=dst[:, 0], in_=src[:, 0])
+            nc.vector.tensor_copy(out=dst[:, 1, 0:VECTOR_RUNS], in_=src[:, 1, 0:VECTOR_RUNS])
+            nc.scalar.copy(out=dst[:, 1, VECTOR_RUNS:RUNS], in_=src[:, 1, VECTOR_RUNS:RUNS])
+            halves = [psum.tile([P, S // 2], F32, name="acc_half%d" % n) for n in range(2)]
+            cols = [slice(n * S // 2, (n + 1) * S // 2) for n in range(2)]
+            for o in range(PASSES):
+                nc.vector.quantize_mx(
+                    out=h_words[0][:, o, :].bitcast(FP8X4), scales=h_scales[0][:, o, :], in_=h_bf16[0][:, o, :]
+                )
+                for n in range(2):
+                    product(halves[n][:], 0, o, cols[n])
+            y = keep.tile([P, S], F32, name="y0")
+            for n in range(2):
+                nc.scalar.copy(out=y[:, cols[n]], in_=halves[n][:])
+            return y
+
         def scores(b):
-            acc = psum.tile([P, S], F32, name="acc", tag="bank_y%d" % b)
+            dst, src = rounding_views(b)
+            if b == 1:
+                for o in range(PASSES):
+                    nc.vector.tensor_copy(out=dst[:, o], in_=src[:, o])
+            else:
+                nc.vector.tensor_copy(out=dst, in_=src)
+            quantize_h(b)
+            acc = psum.tile([P, S], F32, name="acc%d" % b)
             for o in range(PASSES):
                 product(acc[:], b, o, slice(0, S))
             y = keep.tile([P, S], F32, name="y%d" % b)
-            nc.scalar.copy(out=y[:], in_=acc[:])
+            copy = nc.vector.tensor_copy if b == VECTOR_BANK else nc.scalar.copy
+            copy(out=y[:], in_=acc[:])
             return y
 
-        ys, zs, plains, centreds, so_far = {}, {}, {}, {}, {}
+        slots = {
+            "centred01": "h_raw3",
+            "centred2": "h_raw2",
+            "centred3": "h_bf16_2",
+            "product0": "product0",
+            "product1": "h_bf16_3",
+            "product2": "product2",
+        }
 
-        def signed_score(b):
-            zs[b] = work.tile([P, U], F32, name="z")
-            nc.vector.tensor_tensor(zs[b][:], ys[b][:].indirect(path_lists[0][:]), turns[:, 0, :], MULT)
+        def step_tile(kind, shape, slot):
+            return keep.tile(shape, F32, name=kind, tag=slot, align_bytes=64)
 
-        def signed_sigmoid(b):
-            so_far[b] = work.tile([P, U], F32, name="first")
-            nc.scalar.activation(so_far[b][:], zs[b][:], SIGMOID)
-
-        def plain_sigmoid(b, d):
-            plains[b, d] = work.tile([P, U], F32, name="plain%d" % d)
-            nc.scalar.activation(plains[b, d][:], ys[b][:].indirect(path_lists[d][:]), SIGMOID)
-
-        def centre(b, d):
-            centreds[b, d] = work.tile([P, U], F32, name="centred%d" % d)
-            nc.vector.scalar_tensor_tensor(centreds[b, d][:], plains[b, d][:], -0.5, turns[:, d, :], ADD, MULT)
-
-        def multiply(b, d):
-            longer = work.tile([P, U], F32, name="longer%d" % d)
-            nc.vector.scalar_tensor_tensor(longer[:], centreds[b, d][:], 0.5, so_far[b][:], ADD, MULT)
-            so_far[b] = longer
-            if d == D - 1:
-                nc.sync.dma_start(out=out[b * P : (b + 1) * P, :], in_=longer[:])
-
-        ys[0] = first_scores()
-        round_h(1)
-        quantize_h(1)
-        for b in range(BLOCKS):
-            signed_score(b)
+        def paths(b, y):
+            plain = keep.tile([P, D, U], F32, name="plain%d" % b)
+            for d in range(D):
+                nc.scalar.activation(plain[:, d, :], y[:].indirect(path_lists[d][:]), SIGMOID)
+            centred01 = step_tile("centred01", [P, 2, U], slots["centred01"])
+            nc.vector.scalar_tensor_tensor(centred01[:], plain[:, 0:2, :], -0.5, turns[:, 0:2, :], ADD, MULT)
+            so_far = step_tile("product0", [P, U], slots["product0"])
+            nc.vector.tensor_scalar_add(so_far[:], centred01[:, 0, :], 0.5)
             for d in range(1, D):
-                plain_sigmoid(b, d)
-                if d == 2:
-                    signed_sigmoid(b)
-                if b > 0:
-                    multiply(b - 1, d)
-                elif d < 3:
-                    round_h(d + 1)
-                centre(b, d)
-                if b == 0 and d < 3:
-                    quantize_h(d + 1)
-            if b + 1 < BLOCKS:
-                ys[b + 1] = scores(b + 1)
-        for d in range(1, D):
-            multiply(BLOCKS - 1, d)
+                if d == 1:
+                    centred = centred01[:, 1, :]
+                else:
+                    very_last = b == LAST and d == D - 1
+                    slot = slots["product1" if very_last else "centred%d" % d]
+                    centred_tile = step_tile("centred%d" % d, [P, U], slot)
+                    centred = centred_tile[:]
+                    nc.vector.scalar_tensor_tensor(centred, plain[:, d, :], -0.5, turns[:, d, :], ADD, MULT)
+                slot = slots["product%d" % d] if d < D - 1 else "result%d" % b
+                longer = step_tile("product%d" % d, [P, U], slot)
+                nc.vector.scalar_tensor_tensor(longer[:], centred, 0.5, so_far[:], ADD, MULT)
+                so_far = longer
+            nc.sync.dma_start(out=out[b * P : (b + 1) * P, :], in_=so_far[:])
+
+        ys = [first_scores()] + [scores(b) for b in range(1, BLOCKS)]
+        for b in range(BLOCKS):
+            paths(b, ys[b])

@@ -15,6 +15,8 @@ U8 = mybir.dt.uint8
 FP8X4 = mybir.dt.float8_e4m3fn_x4
 MULT = mybir.AluOpType.mult
 ADD = mybir.AluOpType.add
+SUBTRACT = mybir.AluOpType.subtract
+COPY = mybir.ActivationFunctionType.Copy
 SIGMOID = mybir.ActivationFunctionType.Sigmoid
 
 P = 128
@@ -28,35 +30,38 @@ TURN_ROWS = D * U // P
 RUN = 4
 RUNS = P // RUN
 VECTOR_RUNS = 20
-VECTOR_BANK = 2
+KIB = 1024
 
 
 def tile_picked_yhs_prob_p_kernel(tc, x_words, x_scales, hT, turn, offs, pos1, pos2, pos3, pos4, out):
     nc = tc.nc
     with ExitStack() as ctx:
         keep = ctx.enter_context(tc.tile_pool(name="keep", bufs=1))
+        reused = ctx.enter_context(tc.tile_pool(name="reused", bufs=1))
         psum = ctx.enter_context(tc.psum_pool(name="psum", bufs=1))
+
+        def placed(shape, dtype, name, kib):
+            if kib is None:
+                return keep.tile(shape, dtype, name=name, align_bytes=64)
+            return reused.tile(shape, dtype, name=name, offset=int(kib * KIB), align_bytes=64)
 
         node_list = keep.tile([P, S // 16], U16, name="node_list")
         path_lists = [keep.tile([P, U // 16], U16, name="path_list%d" % d) for d in range(D)]
-        word_table = [keep.tile([P, T], U32, name="word_table%d" % o) for o in range(PASSES)]
-        scale_table = keep.tile([P, T], U8, name="scale_table")
-        node_words = [keep.tile([P, S], U32, name="node_words%d" % o, align_bytes=64) for o in range(PASSES)]
+        word_table = [placed([P, T], U32, "word_table0", None), placed([P, T], U32, "word_table1", 0)]
+        scale_table = placed([P, T], U8, "scale_table", 16)
         node_scales = keep.tile([P, S], U8, name="node_scales", align_bytes=64)
         identity = keep.tile([P, P], F32, name="identity")
         turn_rows = keep.tile([P, P], F32, name="turn_rows")
         turn_cols = keep.tile([P, TURN_ROWS], F32, name="turn_cols")
-        turns = keep.tile([P, D, U], F32, name="turns")
-        h_raw = [
-            keep.tile([P, PASSES, PACK, P], F32, name="h_raw", tag="h_raw%d" % b, align_bytes=64)
-            for b in range(BLOCKS)
-        ]
-        h_bf16 = [
-            keep.tile([P, PASSES, P * PACK], BF16, name="h_bf16", tag="h_bf16_%d" % b, align_bytes=64)
-            for b in range(BLOCKS)
-        ]
-        h_words = [keep.tile([P, PASSES, P], U32, name="h_words%d" % b, align_bytes=64) for b in range(BLOCKS)]
-        h_scales = [keep.tile([P, PASSES, P], U8, name="h_scales%d" % b, align_bytes=64) for b in range(BLOCKS)]
+        h_raw = {}
+        for b in range(2):
+            for o in range(PASSES):
+                h_raw[b, o] = keep.tile([P, PACK, P], F32, name="h_raw%d_%d" % (b, o))[:]
+        h_whole = {}
+        for b in range(2, BLOCKS):
+            h_whole[b] = placed([P, PASSES, PACK, P], F32, "h_raw%d" % b, 8 + 4 * (b - 2))
+            for o in range(PASSES):
+                h_raw[b, o] = h_whole[b][:, o]
 
         def load_words(o):
             words = x_words[o].rearrange("p n r -> p (n r)").bitcast(I32)
@@ -65,143 +70,185 @@ def tile_picked_yhs_prob_p_kernel(tc, x_words, x_scales, hT, turn, offs, pos1, p
         def load_h(b):
             for o in range(PASSES):
                 rows = hT[o * P * PACK : (o + 1) * P * PACK, b * P : (b + 1) * P]
-                nc.sync.dma_start(out=h_raw[b][:, o], in_=rows.rearrange("(p j) t -> p j t", j=PACK))
+                nc.sync.dma_start(out=h_raw[b, o], in_=rows.rearrange("(p j) t -> p j t", j=PACK))
+
+        def load_scales(q, queue):
+            queue.dma_start(
+                out=scale_table[32 * q : 32 * q + SCALE_ROWS * PASSES, :].bitcast(I32),
+                in_=x_scales[:, SCALE_ROWS * q : SCALE_ROWS * (q + 1), :].bitcast(I32),
+            )
+
+        def load_turn(queue):
+            queue.dma_start(out=turn_rows[0:TURN_ROWS, :], in_=turn[:, 0, :].rearrange("d (h c) -> d h c", c=P))
+
+        def load_path(d):
+            nc.sync.dma_start(path_lists[d][:], (pos1, pos2, pos3, pos4)[d])
 
         nc.vector.memset(scale_table[:].bitcast(I32), 0)
         nc.gpsimd.memset(turn_rows[:], 0.0)
         nc.sync.dma_start(node_list[:], offs)
         for q in range(QUADRANTS):
-            nc.sync.dma_start(
-                out=scale_table[32 * q : 32 * q + SCALE_ROWS * PASSES, :].bitcast(I32),
-                in_=x_scales[:, SCALE_ROWS * q : SCALE_ROWS * (q + 1), :].bitcast(I32),
-            )
+            load_scales(q, nc.sync)
         load_words(0)
-        nc.sync.dma_start(path_lists[0][:], pos1)
-        nc.sync.dma_start(
-            out=turn_rows[0:TURN_ROWS, :],
-            in_=turn[:, 0, :].rearrange("d (h c) -> d h c", c=P),
-        )
+        load_path(0)
+        load_turn(nc.sync)
         load_words(1)
         load_h(0)
-        for path_list, pos in zip(path_lists[1:], (pos2, pos3, pos4)):
-            nc.sync.dma_start(path_list[:], pos)
-        for b in range(1, BLOCKS):
-            load_h(b)
+        load_path(1)
+        load_h(1)
+        load_path(2)
+        load_path(3)
+        load_h(2)
+        load_h(3)
 
         make_identity(nc, identity[:])
+        warm_in = keep.tile([P, 1], F32, name="warm_in")
         warm_up = keep.tile([P, 1], F32, name="warm_up")
-        nc.scalar.activation(warm_up[:], identity[:, 0:1], SIGMOID)
+        nc.vector.memset(warm_in[:], 0.0)
+        nc.scalar.activation(warm_up[:], warm_in[:], SIGMOID)
 
-        turned = psum.tile([P, P], F32, name="turned")
+        turned = psum.tile([P, P], F32, name="turned", tag="turned")
         nc.tensor.transpose(turned[:], turn_rows[:], identity[:])
         nc.scalar.copy(out=turn_cols[:], in_=turned[:, 0:TURN_ROWS])
-        for pair in range(D // 2):
-            spread = psum.tile([P, TURN_ROWS // 2, P], F32, name="spread%d" % pair)
-            for n in range(TURN_ROWS // 2):
-                col = pair * TURN_ROWS // 2 + n
-                nc.tensor.transpose(spread[:, n, :], turn_cols[:, col : col + 1].to_broadcast([P, P]), identity[:])
-            nc.scalar.copy(
-                out=turns[:, 2 * pair : 2 * pair + 2, :].rearrange("p d u -> p (d u)"),
-                in_=spread[:].rearrange("p n c -> p (n c)"),
-            )
+        base_cols = keep.tile([P, TURN_ROWS], F32, name="base_cols")
+        nc.scalar.activation(base_cols[:], turned[:, 0:TURN_ROWS], COPY, bias=0.5, scale=-0.5)
+        pair_cols = keep.tile([P, 4], F32, name="pair_cols")
+        nc.gpsimd.tensor_tensor(pair_cols[:], turn_cols[:, 0:4], turn_cols[:, 4:8], MULT)
+        sign_cols = keep.tile([P, 2], F32, name="sign_cols")
+        nc.gpsimd.tensor_tensor(sign_cols[:], pair_cols[:, 0:2], pair_cols[:, 2:4], MULT)
 
+        def spread(bank, columns, count):
+            for n in range(count):
+                nc.tensor.transpose(bank[:, n * P : (n + 1) * P], columns[:, n : n + 1].to_broadcast([P, P]), identity[:])
+
+        bases = [psum.tile([P, 2, U], F32, name="bases%d" % pair) for pair in range(D // 2)]
+        for pair in range(D // 2):
+            spread(bases[pair][:].rearrange("p d u -> p (d u)"), base_cols[:, 4 * pair : 4 * pair + 4], 4)
+        signs = psum.tile([P, U], F32, name="signs", tag="turned")
+        spread(signs[:], sign_cols[:], 2)
+        signs_sb = keep.tile([P, U], F32, name="signs_sb")
+        nc.scalar.copy(out=signs_sb[:], in_=signs[:])
+
+        node_words = [placed([P, S], U32, "node_words0", None), placed([P, S], U32, "node_words1", 16)]
         nc.vector.tensor_copy(node_words[0][:], word_table[0][:].indirect(node_list[:]))
         nc.vector.tensor_copy(node_scales[:], scale_table[:].indirect(node_list[:]))
         nc.vector.tensor_copy(node_words[1][:], word_table[1][:].indirect(node_list[:]))
 
-        def rounding_views(b):
+        bf16_at = {(0, 0): None, (0, 1): 1, (1, 0): 2, (1, 1): 3, (2, None): 4, (3, None): 6}
+        h_bf16, h_words, h_scales = {}, {}, {}
+        for piece, kib in bf16_at.items():
+            width = P * (PASSES if piece[1] is None else 1)
+            name = "%s_%s" % piece
+            h_bf16[piece] = placed([P, width * PACK], BF16, "h_bf16" + name, kib)
+            h_words[piece] = placed([P, width], U32, "h_words" + name, 0 if piece == (0, 0) else None)
+            h_scales[piece] = placed([P, width], U8, "h_scales" + name, None)
+
+        def rounding_views(b, o):
+            if o is None:
+                return (
+                    h_bf16[b, o][:].rearrange("p (o c i j) -> p o c j i", o=PASSES, i=RUN, j=PACK),
+                    h_whole[b][:].rearrange("p o j (c i) -> p o c j i", i=RUN),
+                )
             return (
-                h_bf16[b][:].rearrange("p o (c i j) -> p o c j i", i=RUN, j=PACK),
-                h_raw[b][:].rearrange("p o j (c i) -> p o c j i", i=RUN),
+                h_bf16[b, o][:].rearrange("p (c i j) -> p c j i", i=RUN, j=PACK),
+                h_raw[b, o].rearrange("p j (c i) -> p c j i", i=RUN),
             )
 
-        def quantize_h(b):
-            nc.vector.quantize_mx(
-                out=h_words[b][:].rearrange("p o t -> p (o t)").bitcast(FP8X4),
-                scales=h_scales[b][:].rearrange("p o t -> p (o t)"),
-                in_=h_bf16[b][:].rearrange("p o t -> p (o t)"),
-            )
+        def round_h(b, o):
+            dst, src = rounding_views(b, o)
+            nc.vector.tensor_copy(out=dst, in_=src)
+
+        def quantize_h(b, o):
+            nc.vector.quantize_mx(out=h_words[b, o][:].bitcast(FP8X4), scales=h_scales[b, o][:], in_=h_bf16[b, o][:])
 
         def product(acc, b, o, cols):
+            piece, at = ((b, o), slice(0, P)) if b < 2 else ((b, None), slice(o * P, (o + 1) * P))
             nc.tensor.matmul_mx(
                 out=acc,
-                lhsT=h_words[b][:, o, :].bitcast(FP8X4),
-                lhsT_scale=h_scales[b][:, o, :],
+                lhsT=h_words[piece][:, at].bitcast(FP8X4),
+                lhsT_scale=h_scales[piece][:, at],
                 rhs=node_words[o][:, cols].bitcast(FP8X4),
                 rhs_scale=node_scales[SCALE_ROWS * o : P, cols],
                 start=(o == 0),
                 stop=(o == PASSES - 1),
             )
 
-        def first_scores():
-            dst, src = rounding_views(0)
-            nc.scalar.copy(out=dst[:, 0], in_=src[:, 0])
-            nc.vector.tensor_copy(out=dst[:, 1, 0:VECTOR_RUNS], in_=src[:, 1, 0:VECTOR_RUNS])
-            nc.scalar.copy(out=dst[:, 1, VECTOR_RUNS:RUNS], in_=src[:, 1, VECTOR_RUNS:RUNS])
-            halves = [psum.tile([P, S // 2], F32, name="acc_half%d" % n) for n in range(2)]
-            cols = [slice(n * S // 2, (n + 1) * S // 2) for n in range(2)]
+        ys = [placed([P, S], F32, "y%d" % b, {1: 8, 2: 12}.get(b)) for b in range(BLOCKS)]
+        accs = [None] + [psum.tile([P, S], F32, name="acc%d" % b) for b in range(1, BLOCKS)]
+        halves = [psum.tile([P, S // 2], F32, name="acc_half%d" % n) for n in range(2)]
+        cols = [slice(n * S // 2, (n + 1) * S // 2) for n in range(2)]
+        plain = [keep.tile([P, D, U], F32, name="plain%d" % b) for b in range(BLOCKS)]
+        signed = [
+            [placed([P, 2, U], F32, "signed%d_%d" % (b, pair), {(0, 0): 10, (0, 1): 4, (1, 0): 6, (1, 1): 14}.get((b, pair))) for pair in range(2)]
+            for b in range(BLOCKS)
+        ]
+        partial = [keep.tile([P, 3, U], F32, name="partial%d" % b) for b in range(BLOCKS)]
+        result = [placed([P, U], F32, "result%d" % b, {}.get(b)) for b in range(BLOCKS)]
+
+        def scores(b, copy):
             for o in range(PASSES):
-                nc.vector.quantize_mx(
-                    out=h_words[0][:, o, :].bitcast(FP8X4), scales=h_scales[0][:, o, :], in_=h_bf16[0][:, o, :]
-                )
-                for n in range(2):
-                    product(halves[n][:], 0, o, cols[n])
-            y = keep.tile([P, S], F32, name="y0")
-            for n in range(2):
-                nc.scalar.copy(out=y[:, cols[n]], in_=halves[n][:])
-            return y
+                if b > 1:
+                    product(accs[b][:], b, o, slice(0, S))
+            copy(out=ys[b][:], in_=accs[b][:])
+            gathers(b)
 
-        def scores(b):
-            dst, src = rounding_views(b)
-            if b == 1:
-                for o in range(PASSES):
-                    nc.vector.tensor_copy(out=dst[:, o], in_=src[:, o])
-            else:
-                nc.vector.tensor_copy(out=dst, in_=src)
-            quantize_h(b)
-            acc = psum.tile([P, S], F32, name="acc%d" % b)
-            for o in range(PASSES):
-                product(acc[:], b, o, slice(0, S))
-            y = keep.tile([P, S], F32, name="y%d" % b)
-            copy = nc.vector.tensor_copy if b == VECTOR_BANK else nc.scalar.copy
-            copy(out=y[:], in_=acc[:])
-            return y
-
-        slots = {
-            "centred01": "h_raw3",
-            "centred2": "h_raw2",
-            "centred3": "h_bf16_2",
-            "product0": "product0",
-            "product1": "h_bf16_3",
-            "product2": "product2",
-        }
-
-        def step_tile(kind, shape, slot):
-            return keep.tile(shape, F32, name=kind, tag=slot, align_bytes=64)
-
-        def paths(b, y):
-            plain = keep.tile([P, D, U], F32, name="plain%d" % b)
+        def gathers(b):
             for d in range(D):
-                nc.scalar.activation(plain[:, d, :], y[:].indirect(path_lists[d][:]), SIGMOID)
-            centred01 = step_tile("centred01", [P, 2, U], slots["centred01"])
-            nc.vector.scalar_tensor_tensor(centred01[:], plain[:, 0:2, :], -0.5, turns[:, 0:2, :], ADD, MULT)
-            so_far = step_tile("product0", [P, U], slots["product0"])
-            nc.vector.tensor_scalar_add(so_far[:], centred01[:, 0, :], 0.5)
-            for d in range(1, D):
-                if d == 1:
-                    centred = centred01[:, 1, :]
-                else:
-                    very_last = b == LAST and d == D - 1
-                    slot = slots["product1" if very_last else "centred%d" % d]
-                    centred_tile = step_tile("centred%d" % d, [P, U], slot)
-                    centred = centred_tile[:]
-                    nc.vector.scalar_tensor_tensor(centred, plain[:, d, :], -0.5, turns[:, d, :], ADD, MULT)
-                slot = slots["product%d" % d] if d < D - 1 else "result%d" % b
-                longer = step_tile("product%d" % d, [P, U], slot)
-                nc.vector.scalar_tensor_tensor(longer[:], centred, 0.5, so_far[:], ADD, MULT)
-                so_far = longer
-            nc.sync.dma_start(out=out[b * P : (b + 1) * P, :], in_=so_far[:])
+                nc.scalar.activation(plain[b][:, d, :], ys[b][:].indirect(path_lists[d][:]), SIGMOID)
 
-        ys = [first_scores()] + [scores(b) for b in range(1, BLOCKS)]
-        for b in range(BLOCKS):
-            paths(b, ys[b])
+        def shift(b, lo, hi):
+            at_pair = slice(lo % 2, lo % 2 + hi - lo)
+            nc.vector.tensor_tensor(
+                signed[b][lo // 2][:, at_pair, :], plain[b][:, lo:hi, :], bases[lo // 2][:, at_pair, :], SUBTRACT
+            )
+            if b < LAST:
+                pair = lo // 2
+                nc.gpsimd.tensor_tensor(partial[b][:, pair, :], signed[b][pair][:, 0, :], signed[b][pair][:, 1, :], MULT)
+                if pair == 0:
+                    nc.gpsimd.tensor_tensor(partial[b][:, 2, :], partial[b][:, 0, :], signs_sb[:], MULT)
+                else:
+                    nc.gpsimd.tensor_tensor(result[b][:], partial[b][:, 2, :], partial[b][:, 1, :], MULT)
+                    nc.sync.dma_start(out=out[b * P : (b + 1) * P, :], in_=result[b][:])
+
+        def last_factor(d):
+            factor = signed[LAST][d // 2][:, d % 2, :]
+            so_far = signs[:] if d == 0 else partial[LAST][:, d - 1, :]
+            target = result[LAST][:] if d == D - 1 else partial[LAST][:, d, :]
+            nc.vector.tensor_tensor(target, factor, so_far, MULT)
+            if d == D - 1:
+                nc.sync.dma_start(out=out[LAST * P : (LAST + 1) * P, :], in_=result[LAST][:])
+
+        dst, src = rounding_views(0, 0)
+        nc.scalar.copy(out=dst, in_=src)
+        quantize_h(0, 0)
+        for n in range(2):
+            product(halves[n][:], 0, 0, cols[n])
+        dst, src = rounding_views(0, 1)
+        nc.vector.tensor_copy(out=dst[:, 0:VECTOR_RUNS], in_=src[:, 0:VECTOR_RUNS])
+        nc.scalar.copy(out=dst[:, VECTOR_RUNS:RUNS], in_=src[:, VECTOR_RUNS:RUNS])
+        quantize_h(0, 1)
+        for n in range(2):
+            product(halves[n][:], 0, 1, cols[n])
+        nc.scalar.copy(out=ys[0][:, cols[0]], in_=halves[0][:])
+        nc.vector.tensor_copy(out=ys[0][:, cols[1]], in_=halves[1][:])
+        gathers(0)
+        for o in range(PASSES):
+            round_h(1, o)
+            quantize_h(1, o)
+            product(accs[1][:], 1, o, slice(0, S))
+        round_h(2, None)
+        shift(0, 0, 2)
+        scores(1, nc.vector.tensor_copy)
+        quantize_h(2, None)
+        shift(0, 2, 4)
+        round_h(3, None)
+        scores(2, nc.vector.tensor_copy)
+        quantize_h(3, None)
+        shift(1, 0, 2)
+        shift(1, 2, 4)
+        scores(3, nc.vector.tensor_copy)
+        shift(2, 0, 2)
+        shift(2, 2, 4)
+        for d in range(D):
+            shift(LAST, d, d + 1)
+            last_factor(d)

@@ -179,7 +179,7 @@ def tile_picked_yhs_prob_p_kernel(tc, x_words, x_scales, hT, turn, offs, pos1, p
         cols = [slice(n * S // 2, (n + 1) * S // 2) for n in range(2)]
         plain = [keep.tile([P, D, U], F32, name="plain%d" % b) for b in range(BLOCKS)]
         signed = [
-            [placed([P, 2, U], F32, "signed%d_%d" % (b, pair), {(0, 0): 10, (0, 1): 4, (1, 0): 6, (1, 1): 14}.get((b, pair))) for pair in range(2)]
+            [placed([P, 2, U], F32, "signed%d_%d" % (b, pair), {(0, 0): 10, (0, 1): 4, (1, 0): 14, (1, 1): 6}.get((b, pair))) for pair in range(2)]
             for b in range(BLOCKS)
         ]
         partial = [keep.tile([P, 3, U], F32, name="partial%d" % b) for b in range(BLOCKS)]
@@ -201,14 +201,20 @@ def tile_picked_yhs_prob_p_kernel(tc, x_words, x_scales, hT, turn, offs, pos1, p
             nc.vector.tensor_tensor(
                 signed[b][lo // 2][:, at_pair, :], plain[b][:, lo:hi, :], bases[lo // 2][:, at_pair, :], SUBTRACT
             )
-            if b < LAST:
-                pair = lo // 2
-                nc.gpsimd.tensor_tensor(partial[b][:, pair, :], signed[b][pair][:, 0, :], signed[b][pair][:, 1, :], MULT)
-                if pair == 0:
-                    nc.gpsimd.tensor_tensor(partial[b][:, 2, :], partial[b][:, 0, :], signs_sb[:], MULT)
-                else:
-                    nc.gpsimd.tensor_tensor(result[b][:], partial[b][:, 2, :], partial[b][:, 1, :], MULT)
-                    nc.sync.dma_start(out=out[b * P : (b + 1) * P, :], in_=result[b][:])
+
+        def first_pair(b, sign_on_vector):
+            low, high = signed[b][0][:, 0, :], signed[b][0][:, 1, :]
+            if sign_on_vector:
+                nc.vector.tensor_tensor(partial[b][:, 0, :], low, signs[:], MULT)
+                nc.gpsimd.tensor_tensor(partial[b][:, 2, :], partial[b][:, 0, :], high, MULT)
+            else:
+                nc.gpsimd.tensor_tensor(partial[b][:, 0, :], low, high, MULT)
+                nc.gpsimd.tensor_tensor(partial[b][:, 2, :], partial[b][:, 0, :], signs_sb[:], MULT)
+
+        def second_pair(b):
+            nc.gpsimd.tensor_tensor(partial[b][:, 1, :], signed[b][1][:, 0, :], signed[b][1][:, 1, :], MULT)
+            nc.gpsimd.tensor_tensor(result[b][:], partial[b][:, 2, :], partial[b][:, 1, :], MULT)
+            nc.sync.dma_start(out=out[b * P : (b + 1) * P, :], in_=result[b][:])
 
         def last_factor(d):
             factor = signed[LAST][d // 2][:, d % 2, :]
@@ -238,17 +244,23 @@ def tile_picked_yhs_prob_p_kernel(tc, x_words, x_scales, hT, turn, offs, pos1, p
             product(accs[1][:], 1, o, slice(0, S))
         round_h(2, None)
         shift(0, 0, 2)
+        first_pair(0, False)
         scores(1, nc.vector.tensor_copy)
         quantize_h(2, None)
         shift(0, 2, 4)
+        second_pair(0)
         round_h(3, None)
         scores(2, nc.vector.tensor_copy)
-        quantize_h(3, None)
         shift(1, 0, 2)
+        quantize_h(3, None)
+        first_pair(1, True)
         shift(1, 2, 4)
+        second_pair(1)
         scores(3, nc.vector.tensor_copy)
         shift(2, 0, 2)
+        first_pair(2, True)
         shift(2, 2, 4)
+        second_pair(2)
         for d in range(D):
             shift(LAST, d, d + 1)
             last_factor(d)

@@ -54,11 +54,11 @@ def tile_picked_yhs_prob_p_kernel(tc, x_words, x_scales, hT, turn, offs, pos1, p
         turn_rows = keep.tile([P, P], F32, name="turn_rows")
         turn_cols = keep.tile([P, TURN_ROWS], F32, name="turn_cols")
         h_raw = {}
-        for b in range(2):
+        for b in range(LAST):
             for o in range(PASSES):
-                h_raw[b, o] = keep.tile([P, PACK, P], F32, name="h_raw%d_%d" % (b, o))[:]
+                h_raw[b, o] = placed([P, PACK, P], F32, "h_raw%d_%d" % (b, o), 8 + 2 * o if b == 2 else None)[:]
         h_whole = {}
-        for b in range(2, BLOCKS):
+        for b in range(LAST, BLOCKS):
             h_whole[b] = placed([P, PASSES, PACK, P], F32, "h_raw%d" % b, 8 + 4 * (b - 2))
             for o in range(PASSES):
                 h_raw[b, o] = h_whole[b][:, o]
@@ -67,8 +67,8 @@ def tile_picked_yhs_prob_p_kernel(tc, x_words, x_scales, hT, turn, offs, pos1, p
             words = x_words[o].rearrange("p n r -> p (n r)").bitcast(I32)
             nc.sync.dma_start(out=word_table[o][:].bitcast(I32), in_=words)
 
-        def load_h(b):
-            for o in range(PASSES):
+        def load_h(b, passes=range(PASSES)):
+            for o in passes:
                 rows = hT[o * P * PACK : (o + 1) * P * PACK, b * P : (b + 1) * P]
                 nc.sync.dma_start(out=h_raw[b, o], in_=rows.rearrange("(p j) t -> p j t", j=PACK))
 
@@ -94,11 +94,12 @@ def tile_picked_yhs_prob_p_kernel(tc, x_words, x_scales, hT, turn, offs, pos1, p
         load_turn(nc.sync)
         load_words(1)
         load_h(0)
-        load_path(1)
         load_h(1)
+        load_path(1)
+        load_h(2, [0])
         load_path(2)
         load_path(3)
-        load_h(2)
+        load_h(2, [1])
         load_h(3)
 
         make_identity(nc, identity[:])
@@ -134,7 +135,7 @@ def tile_picked_yhs_prob_p_kernel(tc, x_words, x_scales, hT, turn, offs, pos1, p
         nc.vector.tensor_copy(node_scales[:], scale_table[:].indirect(node_list[:]))
         nc.vector.tensor_copy(node_words[1][:], word_table[1][:].indirect(node_list[:]))
 
-        bf16_at = {(0, 0): None, (0, 1): 1, (1, 0): 2, (1, 1): 3, (2, None): 4, (3, None): 6}
+        bf16_at = {(0, 0): None, (0, 1): 1, (1, 0): 2, (1, 1): 3, (2, 0): 4, (2, 1): 5, (3, None): 6}
         h_bf16, h_words, h_scales = {}, {}, {}
         for piece, kib in bf16_at.items():
             width = P * (PASSES if piece[1] is None else 1)
@@ -162,7 +163,7 @@ def tile_picked_yhs_prob_p_kernel(tc, x_words, x_scales, hT, turn, offs, pos1, p
             nc.vector.quantize_mx(out=h_words[b, o][:].bitcast(FP8X4), scales=h_scales[b, o][:], in_=h_bf16[b, o][:])
 
         def product(acc, b, o, cols):
-            piece, at = ((b, o), slice(0, P)) if b < 2 else ((b, None), slice(o * P, (o + 1) * P))
+            piece, at = ((b, o), slice(0, P)) if b < LAST else ((b, None), slice(o * P, (o + 1) * P))
             nc.tensor.matmul_mx(
                 out=acc,
                 lhsT=h_words[piece][:, at].bitcast(FP8X4),
@@ -173,13 +174,13 @@ def tile_picked_yhs_prob_p_kernel(tc, x_words, x_scales, hT, turn, offs, pos1, p
                 stop=(o == PASSES - 1),
             )
 
-        ys = [placed([P, S], F32, "y%d" % b, {1: 8, 2: 12}.get(b)) for b in range(BLOCKS)]
+        ys = [placed([P, S], F32, "y%d" % b, {2: 12}.get(b)) for b in range(BLOCKS)]
         accs = [None] + [psum.tile([P, S], F32, name="acc%d" % b) for b in range(1, BLOCKS)]
         halves = [psum.tile([P, S // 2], F32, name="acc_half%d" % n) for n in range(2)]
         cols = [slice(n * S // 2, (n + 1) * S // 2) for n in range(2)]
         plain = [keep.tile([P, D, U], F32, name="plain%d" % b) for b in range(BLOCKS)]
         signed = [
-            [placed([P, 2, U], F32, "signed%d_%d" % (b, pair), {(0, 0): 10, (0, 1): 4, (1, 0): 14, (1, 1): 6}.get((b, pair))) for pair in range(2)]
+            [placed([P, 2, U], F32, "signed%d_%d" % (b, pair), {(0, 0): 8, (0, 1): 10, (1, 0): 5, (1, 1): 7}.get((b, pair))) for pair in range(2)]
             for b in range(BLOCKS)
         ]
         partial = [keep.tile([P, 3, U], F32, name="partial%d" % b) for b in range(BLOCKS)]
@@ -187,7 +188,7 @@ def tile_picked_yhs_prob_p_kernel(tc, x_words, x_scales, hT, turn, offs, pos1, p
 
         def scores(b, copy):
             for o in range(PASSES):
-                if b > 1:
+                if b == LAST:
                     product(accs[b][:], b, o, slice(0, S))
             copy(out=ys[b][:], in_=accs[b][:])
             gathers(b)
@@ -242,19 +243,23 @@ def tile_picked_yhs_prob_p_kernel(tc, x_words, x_scales, hT, turn, offs, pos1, p
             round_h(1, o)
             quantize_h(1, o)
             product(accs[1][:], 1, o, slice(0, S))
-        round_h(2, None)
+        round_h(2, 0)
         shift(0, 0, 2)
         first_pair(0, False)
         scores(1, nc.vector.tensor_copy)
-        quantize_h(2, None)
+        quantize_h(2, 0)
+        product(accs[2][:], 2, 0, slice(0, S))
+        round_h(2, 1)
         shift(0, 2, 4)
         second_pair(0)
+        quantize_h(2, 1)
+        product(accs[2][:], 2, 1, slice(0, S))
         round_h(3, None)
         scores(2, nc.vector.tensor_copy)
-        shift(1, 0, 2)
         quantize_h(3, None)
-        first_pair(1, True)
+        shift(1, 0, 2)
         shift(1, 2, 4)
+        first_pair(1, True)
         second_pair(1)
         scores(3, nc.vector.tensor_copy)
         shift(2, 0, 2)

@@ -111,24 +111,14 @@ def tile_picked_yhs_prob_p_kernel(tc, x_words, x_scales, hT, turn, offs, pos1, p
         turned = psum.tile([P, P], F32, name="turned", tag="turned")
         nc.tensor.transpose(turned[:], turn_rows[:], identity[:])
         nc.scalar.copy(out=turn_cols[:], in_=turned[:, 0:TURN_ROWS])
-        base_cols = keep.tile([P, TURN_ROWS], F32, name="base_cols")
-        nc.scalar.activation(base_cols[:], turned[:, 0:TURN_ROWS], COPY, bias=0.5, scale=-0.5)
-        pair_cols = keep.tile([P, 4], F32, name="pair_cols")
-        nc.gpsimd.tensor_tensor(pair_cols[:], turn_cols[:, 0:4], turn_cols[:, 4:8], MULT)
-        sign_cols = keep.tile([P, 2], F32, name="sign_cols")
-        nc.gpsimd.tensor_tensor(sign_cols[:], pair_cols[:, 0:2], pair_cols[:, 2:4], MULT)
 
         def spread(bank, columns, count):
             for n in range(count):
                 nc.tensor.transpose(bank[:, n * P : (n + 1) * P], columns[:, n : n + 1].to_broadcast([P, P]), identity[:])
 
-        bases = [psum.tile([P, 2, U], F32, name="bases%d" % pair) for pair in range(D // 2)]
+        turns = [psum.tile([P, 2, U], F32, name="turns%d" % pair) for pair in range(D // 2)]
         for pair in range(D // 2):
-            spread(bases[pair][:].rearrange("p d u -> p (d u)"), base_cols[:, 4 * pair : 4 * pair + 4], 4)
-        signs = psum.tile([P, U], F32, name="signs", tag="turned")
-        spread(signs[:], sign_cols[:], 2)
-        signs_sb = keep.tile([P, U], F32, name="signs_sb")
-        nc.scalar.copy(out=signs_sb[:], in_=signs[:])
+            spread(turns[pair][:].rearrange("p d u -> p (d u)"), turn_cols[:, 4 * pair : 4 * pair + 4], 4)
 
         node_words = [placed([P, S], U32, "node_words0", None), placed([P, S], U32, "node_words1", 16)]
         nc.vector.tensor_copy(node_words[0][:], word_table[0][:].indirect(node_list[:]))
@@ -180,11 +170,10 @@ def tile_picked_yhs_prob_p_kernel(tc, x_words, x_scales, hT, turn, offs, pos1, p
         cols = [slice(n * S // 2, (n + 1) * S // 2) for n in range(2)]
         plain = [keep.tile([P, D, U], F32, name="plain%d" % b) for b in range(BLOCKS)]
         signed = [
-            [placed([P, 2, U], F32, "signed%d_%d" % (b, pair), {(0, 0): 8, (0, 1): 10, (1, 0): 5, (1, 1): 7}.get((b, pair))) for pair in range(2)]
+            [placed([P, 2, U], F32, "signed%d_%d" % (b, pair), {(0, 0): 8, (0, 1): 4, (1, 0): 14, (1, 1): 6}.get((b, pair))) for pair in range(2)]
             for b in range(BLOCKS)
         ]
-        partial = [keep.tile([P, 3, U], F32, name="partial%d" % b) for b in range(BLOCKS)]
-        result = [placed([P, U], F32, "result%d" % b, {}.get(b)) for b in range(BLOCKS)]
+        so_far = [[placed([P, U], F32, "so_far%d_%d" % (b, d), {(0, 0): 10}.get((b, d))) for d in range(D)] for b in range(BLOCKS)]
 
         def scores(b, copy):
             for o in range(PASSES):
@@ -197,33 +186,20 @@ def tile_picked_yhs_prob_p_kernel(tc, x_words, x_scales, hT, turn, offs, pos1, p
             for d in range(D):
                 nc.scalar.activation(plain[b][:, d, :], ys[b][:].indirect(path_lists[d][:]), SIGMOID)
 
-        def shift(b, lo, hi):
+        def centre(b, lo, hi):
             at_pair = slice(lo % 2, lo % 2 + hi - lo)
-            nc.vector.tensor_tensor(
-                signed[b][lo // 2][:, at_pair, :], plain[b][:, lo:hi, :], bases[lo // 2][:, at_pair, :], SUBTRACT
+            nc.vector.scalar_tensor_tensor(
+                signed[b][lo // 2][:, at_pair, :], plain[b][:, lo:hi, :], -0.5, turns[lo // 2][:, at_pair, :], ADD, MULT
             )
 
-        def first_pair(b, sign_on_vector):
-            low, high = signed[b][0][:, 0, :], signed[b][0][:, 1, :]
-            if sign_on_vector:
-                nc.vector.tensor_tensor(partial[b][:, 0, :], low, signs[:], MULT)
-                nc.gpsimd.tensor_tensor(partial[b][:, 2, :], partial[b][:, 0, :], high, MULT)
+        def factor(b, d):
+            centred = signed[b][d // 2][:, d % 2, :]
+            if d == 0:
+                nc.vector.tensor_scalar_add(so_far[b][0][:], centred, 0.5)
             else:
-                nc.gpsimd.tensor_tensor(partial[b][:, 0, :], low, high, MULT)
-                nc.gpsimd.tensor_tensor(partial[b][:, 2, :], partial[b][:, 0, :], signs_sb[:], MULT)
-
-        def second_pair(b):
-            nc.gpsimd.tensor_tensor(partial[b][:, 1, :], signed[b][1][:, 0, :], signed[b][1][:, 1, :], MULT)
-            nc.gpsimd.tensor_tensor(result[b][:], partial[b][:, 2, :], partial[b][:, 1, :], MULT)
-            nc.sync.dma_start(out=out[b * P : (b + 1) * P, :], in_=result[b][:])
-
-        def last_factor(d):
-            factor = signed[LAST][d // 2][:, d % 2, :]
-            so_far = signs[:] if d == 0 else partial[LAST][:, d - 1, :]
-            target = result[LAST][:] if d == D - 1 else partial[LAST][:, d, :]
-            nc.vector.tensor_tensor(target, factor, so_far, MULT)
+                nc.vector.scalar_tensor_tensor(so_far[b][d][:], centred, 0.5, so_far[b][d - 1][:], ADD, MULT)
             if d == D - 1:
-                nc.sync.dma_start(out=out[LAST * P : (LAST + 1) * P, :], in_=result[LAST][:])
+                nc.sync.dma_start(out=out[b * P : (b + 1) * P, :], in_=so_far[b][d][:])
 
         dst, src = rounding_views(0, 0)
         nc.scalar.copy(out=dst, in_=src)
@@ -244,28 +220,35 @@ def tile_picked_yhs_prob_p_kernel(tc, x_words, x_scales, hT, turn, offs, pos1, p
             quantize_h(1, o)
             product(accs[1][:], 1, o, slice(0, S))
         round_h(2, 0)
-        shift(0, 0, 2)
-        first_pair(0, False)
+        centre(0, 0, 2)
         scores(1, nc.vector.tensor_copy)
         quantize_h(2, 0)
         product(accs[2][:], 2, 0, slice(0, S))
         round_h(2, 1)
-        shift(0, 2, 4)
-        second_pair(0)
+        factor(0, 0)
         quantize_h(2, 1)
         product(accs[2][:], 2, 1, slice(0, S))
+        centre(0, 2, 4)
         round_h(3, None)
         scores(2, nc.vector.tensor_copy)
         quantize_h(3, None)
-        shift(1, 0, 2)
-        shift(1, 2, 4)
-        first_pair(1, True)
-        second_pair(1)
+        factor(0, 1)
+        centre(1, 0, 2)
+        factor(0, 2)
+        factor(1, 0)
         scores(3, nc.vector.tensor_copy)
-        shift(2, 0, 2)
-        first_pair(2, True)
-        shift(2, 2, 4)
-        second_pair(2)
-        for d in range(D):
-            shift(LAST, d, d + 1)
-            last_factor(d)
+        factor(0, 3)
+        factor(1, 1)
+        centre(1, 2, 4)
+        for b in range(2, BLOCKS):
+            centre(b, 0, 2)
+            factor(b - 1, 2)
+            factor(b, 0)
+            factor(b - 1, 3)
+            factor(b, 1)
+            if b < LAST:
+                centre(b, 2, 4)
+        centre(LAST, 2, 3)
+        factor(LAST, 2)
+        centre(LAST, 3, 4)
+        factor(LAST, 3)

@@ -45,6 +45,9 @@ def tile_picked_yhs_prob_p_kernel(tc, x_words, x_scales, hT, turn, offs, pos1, p
                 return keep.tile(shape, dtype, name=name, align_bytes=64)
             return reused.tile(shape, dtype, name=name, offset=int(kib * KIB), align_bytes=64)
 
+        def bank(shape, name, first):
+            return psum.tile(shape, F32, name=name, offset=first * 2 * KIB)
+
         node_list = keep.tile([P, S // 16], U16, name="node_list")
         path_lists = [keep.tile([P, U // 16], U16, name="path_list%d" % d) for d in range(D)]
         word_table = [placed([P, T], U32, "word_table0", None), placed([P, T], U32, "word_table1", 0)]
@@ -59,7 +62,7 @@ def tile_picked_yhs_prob_p_kernel(tc, x_words, x_scales, hT, turn, offs, pos1, p
                 h_raw[b, o] = placed([P, PACK, P], F32, "h_raw%d_%d" % (b, o), 8 + 2 * o if b == 2 else None)[:]
         h_whole = {}
         for b in range(LAST, BLOCKS):
-            h_whole[b] = placed([P, PASSES, PACK, P], F32, "h_raw%d" % b, 8 + 4 * (b - 2))
+            h_whole[b] = placed([P, PASSES, PACK, P], F32, "h_raw%d" % b, 20)
             for o in range(PASSES):
                 h_raw[b, o] = h_whole[b][:, o]
 
@@ -108,17 +111,24 @@ def tile_picked_yhs_prob_p_kernel(tc, x_words, x_scales, hT, turn, offs, pos1, p
         nc.vector.memset(warm_in[:], 0.0)
         nc.scalar.activation(warm_up[:], warm_in[:], SIGMOID)
 
-        turned = psum.tile([P, P], F32, name="turned", tag="turned")
+        turned = bank([P, P], "turned", 7)
         nc.tensor.transpose(turned[:], turn_rows[:], identity[:])
         nc.scalar.copy(out=turn_cols[:], in_=turned[:, 0:TURN_ROWS])
 
-        def spread(bank, columns, count):
-            for n in range(count):
-                nc.tensor.transpose(bank[:, n * P : (n + 1) * P], columns[:, n : n + 1].to_broadcast([P, P]), identity[:])
-
-        turns = [psum.tile([P, 2, U], F32, name="turns%d" % pair) for pair in range(D // 2)]
+        base_cols = keep.tile([P, TURN_ROWS], F32, name="base_cols")
+        nc.scalar.activation(base_cols[:], turned[:, 0:TURN_ROWS], COPY, bias=0.5, scale=-0.5)
+        pair_cols = keep.tile([P, 2], F32, name="pair_cols")
+        nc.gpsimd.tensor_tensor(pair_cols[:], turn_cols[:, 0:2], turn_cols[:, 2:4], MULT)
+        sign_cols = keep.tile([P, 2], F32, name="sign_cols")
+        nc.gpsimd.tensor_tensor(sign_cols[:], pair_cols[:], turn_cols[:, 4:6], MULT)
+        turns = [keep.tile([P, 2, U], F32, name="turns%d" % pair) for pair in range(D // 2)]
         for pair in range(D // 2):
-            spread(turns[pair][:].rearrange("p d u -> p (d u)"), turn_cols[:, 4 * pair : 4 * pair + 4], 4)
+            spread = bank([P, 2, U], "spread%d" % pair, 2 + pair)
+            flat = spread[:].rearrange("p d u -> p (d u)")
+            for n in range(4):
+                column = turn_cols[:, 4 * pair + n : 4 * pair + n + 1].to_broadcast([P, P])
+                nc.tensor.transpose(flat[:, n * P : (n + 1) * P], column, identity[:])
+            nc.scalar.copy(out=turns[pair][:], in_=spread[:])
 
         node_words = [placed([P, S], U32, "node_words0", None), placed([P, S], U32, "node_words1", 16)]
         nc.vector.tensor_copy(node_words[0][:], word_table[0][:].indirect(node_list[:]))
@@ -149,6 +159,14 @@ def tile_picked_yhs_prob_p_kernel(tc, x_words, x_scales, hT, turn, offs, pos1, p
             dst, src = rounding_views(b, o)
             nc.vector.tensor_copy(out=dst, in_=src)
 
+        def round_on_gpsimd(b, o):
+            dst, src = rounding_views(b, o)
+            if o is None:
+                for n in range(PASSES):
+                    nc.gpsimd.tensor_scalar(dst[:, n], src[:, n], 1.0, 0.0, MULT, ADD)
+            else:
+                nc.gpsimd.tensor_scalar(dst, src, 1.0, 0.0, MULT, ADD)
+
         def quantize_h(b, o):
             nc.vector.quantize_mx(out=h_words[b, o][:].bitcast(FP8X4), scales=h_scales[b, o][:], in_=h_bf16[b, o][:])
 
@@ -164,27 +182,62 @@ def tile_picked_yhs_prob_p_kernel(tc, x_words, x_scales, hT, turn, offs, pos1, p
                 stop=(o == PASSES - 1),
             )
 
-        ys = [placed([P, S], F32, "y%d" % b, {2: 12}.get(b)) for b in range(BLOCKS)]
-        accs = [None] + [psum.tile([P, S], F32, name="acc%d" % b) for b in range(1, BLOCKS)]
-        halves = [psum.tile([P, S // 2], F32, name="acc_half%d" % n) for n in range(2)]
+        ys = [placed([P, S], F32, "y%d" % b, {1: 9, 2: 6}.get(b)) for b in range(BLOCKS)]
+        accs = [None, bank([P, D - 1, S], "acc1", 4)[:, 0, :], bank([P, S], "acc2", 2)[:], bank([P, S], "acc3", 3)[:]]
+        halves = [bank([P, S // 2], "acc_half%d" % n, n) for n in range(2)]
         cols = [slice(n * S // 2, (n + 1) * S // 2) for n in range(2)]
         plain = [keep.tile([P, D, U], F32, name="plain%d" % b) for b in range(BLOCKS)]
         signed = [
-            [placed([P, 2, U], F32, "signed%d_%d" % (b, pair), {(0, 0): 8, (0, 1): 4, (1, 0): 14, (1, 1): 6}.get((b, pair))) for pair in range(2)]
+            [placed([P, 2, U], F32, "signed%d_%d" % (b, pair), {(0, 1): 22, (1, 1): 11}.get((b, pair))) for pair in range(2)]
             for b in range(BLOCKS)
         ]
-        so_far = [[placed([P, U], F32, "so_far%d_%d" % (b, d), {(0, 0): 10}.get((b, d))) for d in range(D)] for b in range(BLOCKS)]
+        so_far = [[placed([P, U], F32, "so_far%d_%d" % (b, d), {}.get((b, d))) for d in range(D)] for b in range(BLOCKS)]
 
         def scores(b, copy):
-            for o in range(PASSES):
-                if b == LAST:
-                    product(accs[b][:], b, o, slice(0, S))
-            copy(out=ys[b][:], in_=accs[b][:])
+            copy(out=ys[b][:], in_=accs[b])
             gathers(b)
 
         def gathers(b):
             for d in range(D):
-                nc.scalar.activation(plain[b][:, d, :], ys[b][:].indirect(path_lists[d][:]), SIGMOID)
+                if (b, d) == (LAST, D - 1):
+                    for n in range(2):
+                        half_list = path_lists[d][:, n * U // 32 : (n + 1) * U // 32]
+                        nc.scalar.activation(plain[b][:, d, n * P : (n + 1) * P], ys[b][:].indirect(half_list), SIGMOID)
+                else:
+                    nc.scalar.activation(plain[b][:, d, :], ys[b][:].indirect(path_lists[d][:]), SIGMOID)
+
+        flipped = [[bank([P, 2, P], "flipped%d_%d" % (b, d), ((4, 5, 6), (0, 1, 7), (4, 5, 6))[b][d]) for d in range(D - 1)] for b in range(LAST)]
+        chain = [[placed([P, 2, P], F32, "chain%d_%d" % (b, d), {(0, 0): 20, (0, 1): 21}.get((b, d))) for d in range(D - 1)] for b in range(LAST)]
+        back = [bank([P, U], "back%d" % b, (2, 3, 0)[b]) for b in range(LAST)]
+
+        def link(b, d):
+            for half in range(2):
+                nc.tensor.transpose(flipped[b][d][:, half, :], plain[b][:, d, half * P : (half + 1) * P], identity[:])
+            for half in range(2):
+                source = flipped[b][d][:, half, :]
+                base = base_cols[:, 2 * d + half : 2 * d + half + 1]
+                target = chain[b][d][:, half, :]
+                if d == 0:
+                    nc.vector.tensor_scalar(target, source, base, sign_cols[:, half : half + 1], SUBTRACT, MULT)
+                else:
+                    nc.vector.scalar_tensor_tensor(target, source, base, chain[b][d - 1][:, half, :], SUBTRACT, MULT)
+                if d == D - 2:
+                    nc.tensor.transpose(back[b][:, half * P : (half + 1) * P], target, identity[:])
+
+        def finish(b):
+            nc.vector.scalar_tensor_tensor(so_far[b][D - 1][:], signed[b][1][:, 1, :], 0.5, back[b][:], ADD, MULT)
+            nc.sync.dma_start(out=out[b * P : (b + 1) * P, :], in_=so_far[b][D - 1][:])
+
+        def last_half(n):
+            at = slice(n * P, (n + 1) * P)
+            centred = signed[LAST][1][:, 1, at]
+            nc.vector.scalar_tensor_tensor(centred, plain[LAST][:, D - 1, at], -0.5, turns[1][:, 1, at], ADD, MULT)
+
+        def finish_half(n):
+            at = slice(n * P, (n + 1) * P)
+            result = so_far[LAST][D - 1][:, at]
+            nc.vector.scalar_tensor_tensor(result, signed[LAST][1][:, 1, at], 0.5, so_far[LAST][D - 2][:, at], ADD, MULT)
+            nc.sync.dma_start(out=out[LAST * P : (LAST + 1) * P, at], in_=result)
 
         def centre(b, lo, hi):
             at_pair = slice(lo % 2, lo % 2 + hi - lo)
@@ -218,37 +271,42 @@ def tile_picked_yhs_prob_p_kernel(tc, x_words, x_scales, hT, turn, offs, pos1, p
         for o in range(PASSES):
             round_h(1, o)
             quantize_h(1, o)
-            product(accs[1][:], 1, o, slice(0, S))
+            product(accs[1], 1, o, slice(0, S))
         round_h(2, 0)
-        centre(0, 0, 2)
-        scores(1, nc.vector.tensor_copy)
         quantize_h(2, 0)
-        product(accs[2][:], 2, 0, slice(0, S))
+        product(accs[2], 2, 0, slice(0, S))
         round_h(2, 1)
-        factor(0, 0)
         quantize_h(2, 1)
-        product(accs[2][:], 2, 1, slice(0, S))
-        centre(0, 2, 4)
+        product(accs[2], 2, 1, slice(0, S))
+        scores(1, nc.vector.tensor_copy)
         round_h(3, None)
-        scores(2, nc.vector.tensor_copy)
+        link(0, 0)
         quantize_h(3, None)
-        factor(0, 1)
-        centre(1, 0, 2)
-        factor(0, 2)
-        factor(1, 0)
+        for o in range(PASSES):
+            product(accs[3], 3, o, slice(0, S))
+        scores(2, nc.vector.tensor_copy)
+        link(0, 1)
+        centre(0, 3, 4)
+        link(0, 2)
+        link(1, 0)
         scores(3, nc.vector.tensor_copy)
-        factor(0, 3)
-        factor(1, 1)
-        centre(1, 2, 4)
-        for b in range(2, BLOCKS):
-            centre(b, 0, 2)
-            factor(b - 1, 2)
-            factor(b, 0)
-            factor(b - 1, 3)
-            factor(b, 1)
-            if b < LAST:
-                centre(b, 2, 4)
-        centre(LAST, 2, 3)
-        factor(LAST, 2)
-        centre(LAST, 3, 4)
-        factor(LAST, 3)
+        link(1, 1)
+        finish(0)
+        link(1, 2)
+        centre(1, 3, 4)
+        link(2, 0)
+        finish(1)
+        link(2, 1)
+        centre(2, 3, 4)
+        link(2, 2)
+        centre(3, 0, 1)
+        factor(3, 0)
+        centre(3, 1, 2)
+        finish(2)
+        factor(3, 1)
+        centre(3, 2, 3)
+        last_half(0)
+        factor(3, 2)
+        last_half(1)
+        finish_half(0)
+        finish_half(1)

@@ -59,7 +59,7 @@ def tile_picked_yhs_prob_p_kernel(tc, x_words, x_scales, hT, turn, offs, pos1, p
         h_raw = {}
         for b in range(LAST):
             for o in range(PASSES):
-                h_raw[b, o] = placed([P, PACK, P], F32, "h_raw%d_%d" % (b, o), 8 + 2 * o if b == 2 else None)[:]
+                h_raw[b, o] = placed([P, PACK, P], F32, "h_raw%d_%d" % (b, o), 8 + 2 * o if b == 2 else 34 if (b, o) == (0, 0) else None)[:]
         h_whole = {}
         for b in range(LAST, BLOCKS):
             h_whole[b] = placed([P, PASSES, PACK, P], F32, "h_raw%d" % b, 20)
@@ -117,10 +117,10 @@ def tile_picked_yhs_prob_p_kernel(tc, x_words, x_scales, hT, turn, offs, pos1, p
 
         base_cols = keep.tile([P, TURN_ROWS], F32, name="base_cols")
         nc.scalar.activation(base_cols[:], turned[:, 0:TURN_ROWS], COPY, bias=0.5, scale=-0.5)
-        pair_cols = keep.tile([P, 2], F32, name="pair_cols")
-        nc.gpsimd.tensor_tensor(pair_cols[:], turn_cols[:, 0:2], turn_cols[:, 2:4], MULT)
+        pair_cols = keep.tile([P, 4], F32, name="pair_cols")
+        nc.gpsimd.tensor_tensor(pair_cols[:], turn_cols[:, 0:4], turn_cols[:, 4:8], MULT)
         sign_cols = keep.tile([P, 2], F32, name="sign_cols")
-        nc.gpsimd.tensor_tensor(sign_cols[:], pair_cols[:], turn_cols[:, 4:6], MULT)
+        nc.gpsimd.tensor_tensor(sign_cols[:], pair_cols[:, 0:2], pair_cols[:, 2:4], MULT)
         turns = [keep.tile([P, 2, U], F32, name="turns%d" % pair) for pair in range(D // 2)]
         for pair in range(D // 2):
             spread = bank([P, 2, U], "spread%d" % pair, 2 + pair)
@@ -182,16 +182,16 @@ def tile_picked_yhs_prob_p_kernel(tc, x_words, x_scales, hT, turn, offs, pos1, p
                 stop=(o == PASSES - 1),
             )
 
-        ys = [placed([P, S], F32, "y%d" % b, {1: 9, 2: 6}.get(b)) for b in range(BLOCKS)]
+        ys = [placed([P, S], F32, "y%d" % b, {1: 9, 2: 4.5}.get(b)) for b in range(BLOCKS)]
         accs = [None, bank([P, D - 1, S], "acc1", 4)[:, 0, :], bank([P, S], "acc2", 2)[:], bank([P, S], "acc3", 3)[:]]
         halves = [bank([P, S // 2], "acc_half%d" % n, n) for n in range(2)]
         cols = [slice(n * S // 2, (n + 1) * S // 2) for n in range(2)]
         plain = [keep.tile([P, D, U], F32, name="plain%d" % b) for b in range(BLOCKS)]
         signed = [
-            [placed([P, 2, U], F32, "signed%d_%d" % (b, pair), {(0, 1): 22, (1, 1): 11}.get((b, pair))) for pair in range(2)]
+            [placed([P, 2, U], F32, "signed%d_%d" % (b, pair), {(0, 1): 6.5, (3, 0): 24.5, (3, 1): 27}.get((b, pair))) for pair in range(2)]
             for b in range(BLOCKS)
         ]
-        so_far = [[placed([P, U], F32, "so_far%d_%d" % (b, d), {}.get((b, d))) for d in range(D)] for b in range(BLOCKS)]
+        so_far = [[placed([P, U], F32, "so_far%d_%d" % (b, d), {(0, 3): 32, (1, 3): 23.5}.get((b, d))) for d in range(D)] for b in range(BLOCKS)]
 
         def scores(b, copy):
             copy(out=ys[b][:], in_=accs[b])
@@ -207,7 +207,7 @@ def tile_picked_yhs_prob_p_kernel(tc, x_words, x_scales, hT, turn, offs, pos1, p
                     nc.scalar.activation(plain[b][:, d, :], ys[b][:].indirect(path_lists[d][:]), SIGMOID)
 
         flipped = [[bank([P, 2, P], "flipped%d_%d" % (b, d), ((4, 5, 6), (0, 1, 7), (4, 5, 6))[b][d]) for d in range(D - 1)] for b in range(LAST)]
-        chain = [[placed([P, 2, P], F32, "chain%d_%d" % (b, d), {(0, 0): 20, (0, 1): 21}.get((b, d))) for d in range(D - 1)] for b in range(LAST)]
+        chain = [[placed([P, 2, P], F32, "chain%d_%d" % (b, d), {(0, 0): 20, (0, 1): 21, (1, 1): 32, (2, 0): 24, (2, 1): 27}.get((b, d))) for d in range(D - 1)] for b in range(LAST)]
         back = [bank([P, U], "back%d" % b, (2, 3, 0)[b]) for b in range(LAST)]
 
         def link(b, d):
@@ -224,8 +224,11 @@ def tile_picked_yhs_prob_p_kernel(tc, x_words, x_scales, hT, turn, offs, pos1, p
                 if d == D - 2:
                     nc.tensor.transpose(back[b][:, half * P : (half + 1) * P], target, identity[:])
 
+        def shift(b):
+            nc.gpsimd.tensor_tensor(signed[b][1][:, 1, :], plain[b][:, D - 1, :], last_base[:], SUBTRACT)
+
         def finish(b):
-            nc.vector.scalar_tensor_tensor(so_far[b][D - 1][:], signed[b][1][:, 1, :], 0.5, back[b][:], ADD, MULT)
+            nc.vector.tensor_tensor(so_far[b][D - 1][:], signed[b][1][:, 1, :], back[b][:], MULT)
             nc.sync.dma_start(out=out[b * P : (b + 1) * P, :], in_=so_far[b][D - 1][:])
 
         def last_half(n):
@@ -265,6 +268,8 @@ def tile_picked_yhs_prob_p_kernel(tc, x_words, x_scales, hT, turn, offs, pos1, p
         quantize_h(0, 1)
         for n in range(2):
             product(halves[n][:], 0, 1, cols[n])
+        last_base = placed([P, U], F32, "last_base", 34)
+        nc.scalar.activation(last_base[:], spread[:, 1, :], COPY, bias=0.5, scale=-0.5)
         nc.scalar.copy(out=ys[0][:, cols[0]], in_=halves[0][:])
         nc.vector.tensor_copy(out=ys[0][:, cols[1]], in_=halves[1][:])
         gathers(0)
@@ -286,23 +291,23 @@ def tile_picked_yhs_prob_p_kernel(tc, x_words, x_scales, hT, turn, offs, pos1, p
             product(accs[3], 3, o, slice(0, S))
         scores(2, nc.vector.tensor_copy)
         link(0, 1)
-        centre(0, 3, 4)
+        shift(0)
         link(0, 2)
         link(1, 0)
         scores(3, nc.vector.tensor_copy)
         link(1, 1)
-        finish(0)
+        shift(1)
         link(1, 2)
-        centre(1, 3, 4)
         link(2, 0)
-        finish(1)
+        finish(0)
         link(2, 1)
-        centre(2, 3, 4)
+        shift(2)
         link(2, 2)
         centre(3, 0, 1)
+        finish(1)
         factor(3, 0)
-        centre(3, 1, 2)
         finish(2)
+        centre(3, 1, 2)
         factor(3, 1)
         centre(3, 2, 3)
         last_half(0)

@@ -24,13 +24,25 @@ PACK = 4
 PASSES = K // (P * PACK)
 QUADRANTS = 4
 SCALE_ROWS = 4
-BLOCKS = V // P
-LAST = BLOCKS - 1
-TURN_ROWS = D * U // P
+BANDS = V // P
+LAST = BANDS - 1
+HALVES = U // P
+TURN_ROWS = D * HALVES
+LINKS = D - 1
 RUN = 4
 RUNS = P // RUN
 VECTOR_RUNS = 20
 KIB = 1024
+BANK = 2 * KIB
+
+WORDS_1 = 0
+RAW_LATE = 8 * KIB
+SCALES = 16 * KIB
+CHAIN_2_0 = 24 * KIB
+CHAIN_2_1 = 27 * KIB
+CHAIN_1_1 = 32 * KIB
+RAW_0 = 34 * KIB
+ROUNDED_3 = WORDS_1 + 6 * KIB
 
 
 def tile_picked_yhs_prob_p_kernel(tc, x_words, x_scales, hT, turn, offs, pos1, pos2, pos3, pos4, out):
@@ -40,49 +52,39 @@ def tile_picked_yhs_prob_p_kernel(tc, x_words, x_scales, hT, turn, offs, pos1, p
         reused = ctx.enter_context(tc.tile_pool(name="reused", bufs=1))
         psum = ctx.enter_context(tc.psum_pool(name="psum", bufs=1))
 
-        def placed(shape, dtype, name, kib):
-            if kib is None:
+        def placed(shape, dtype, name, start=None):
+            if start is None:
                 return keep.tile(shape, dtype, name=name, align_bytes=64)
-            return reused.tile(shape, dtype, name=name, offset=int(kib * KIB), align_bytes=64)
+            return reused.tile(shape, dtype, name=name, offset=start, align_bytes=64)
 
-        def bank(shape, name, first):
-            return psum.tile(shape, F32, name=name, offset=first * 2 * KIB)
+        def in_bank(shape, name, bank):
+            return psum.tile(shape, F32, name=name, offset=bank * BANK)
+
+        def half(n):
+            return slice(n * P, (n + 1) * P)
 
         node_list = keep.tile([P, S // 16], U16, name="node_list")
         path_lists = [keep.tile([P, U // 16], U16, name="path_list%d" % d) for d in range(D)]
-        word_table = [placed([P, T], U32, "word_table0", None), placed([P, T], U32, "word_table1", 0)]
-        scale_table = placed([P, T], U8, "scale_table", 16)
-        node_scales = keep.tile([P, S], U8, name="node_scales", align_bytes=64)
+        word_table = [placed([P, T], U32, "word_table0"), placed([P, T], U32, "word_table1", WORDS_1)]
+        scale_table = placed([P, T], U8, "scale_table", SCALES)
         identity = keep.tile([P, P], F32, name="identity")
         turn_rows = keep.tile([P, P], F32, name="turn_rows")
-        turn_cols = keep.tile([P, TURN_ROWS], F32, name="turn_cols")
-        h_raw = {}
-        for b in range(LAST):
-            for o in range(PASSES):
-                h_raw[b, o] = placed([P, PACK, P], F32, "h_raw%d_%d" % (b, o), 8 + 2 * o if b == 2 else 34 if (b, o) == (0, 0) else None)[:]
-        h_whole = {}
-        for b in range(LAST, BLOCKS):
-            h_whole[b] = placed([P, PASSES, PACK, P], F32, "h_raw%d" % b, 20)
-            for o in range(PASSES):
-                h_raw[b, o] = h_whole[b][:, o]
+        h_raw = {
+            (b, o): placed([P, PACK, P], F32, "h_raw%d_%d" % (b, o), RAW_0 if (b, o) == (0, 0) else None)[:]
+            for b in range(2)
+            for o in range(PASSES)
+        }
+        late_raw = placed([P, PASSES, PACK, 2 * P], F32, "late_raw", RAW_LATE)
+        for o in range(PASSES):
+            h_raw[2, o] = late_raw[:, o, :, half(0)]
 
         def load_words(o):
             words = x_words[o].rearrange("p n r -> p (n r)").bitcast(I32)
             nc.sync.dma_start(out=word_table[o][:].bitcast(I32), in_=words)
 
-        def load_h(b, passes=range(PASSES)):
-            for o in passes:
-                rows = hT[o * P * PACK : (o + 1) * P * PACK, b * P : (b + 1) * P]
-                nc.sync.dma_start(out=h_raw[b, o], in_=rows.rearrange("(p j) t -> p j t", j=PACK))
-
-        def load_scales(q, queue):
-            queue.dma_start(
-                out=scale_table[32 * q : 32 * q + SCALE_ROWS * PASSES, :].bitcast(I32),
-                in_=x_scales[:, SCALE_ROWS * q : SCALE_ROWS * (q + 1), :].bitcast(I32),
-            )
-
-        def load_turn(queue):
-            queue.dma_start(out=turn_rows[0:TURN_ROWS, :], in_=turn[:, 0, :].rearrange("d (h c) -> d h c", c=P))
+        def load_h(target, o, positions):
+            rows = hT[o * P * PACK : (o + 1) * P * PACK, positions]
+            nc.sync.dma_start(out=target, in_=rows.rearrange("(p j) t -> p j t", j=PACK))
 
         def load_path(d):
             nc.sync.dma_start(path_lists[d][:], (pos1, pos2, pos3, pos4)[d])
@@ -91,19 +93,22 @@ def tile_picked_yhs_prob_p_kernel(tc, x_words, x_scales, hT, turn, offs, pos1, p
         nc.gpsimd.memset(turn_rows[:], 0.0)
         nc.sync.dma_start(node_list[:], offs)
         for q in range(QUADRANTS):
-            load_scales(q, nc.sync)
+            nc.sync.dma_start(
+                out=scale_table[32 * q : 32 * q + SCALE_ROWS * PASSES, :].bitcast(I32),
+                in_=x_scales[:, SCALE_ROWS * q : SCALE_ROWS * (q + 1), :].bitcast(I32),
+            )
         load_words(0)
         load_path(0)
-        load_turn(nc.sync)
+        nc.sync.dma_start(out=turn_rows[0:TURN_ROWS, :], in_=turn[:, 0, :].rearrange("d (h c) -> d h c", c=P))
         load_words(1)
-        load_h(0)
-        load_h(1)
+        for b in range(2):
+            for o in range(PASSES):
+                load_h(h_raw[b, o], o, half(b))
         load_path(1)
-        load_h(2, [0])
         load_path(2)
+        load_h(late_raw[:, 0], 0, slice(2 * P, V))
         load_path(3)
-        load_h(2, [1])
-        load_h(3)
+        load_h(late_raw[:, 1], 1, slice(2 * P, V))
 
         make_identity(nc, identity[:])
         warm_in = keep.tile([P, 1], F32, name="warm_in")
@@ -111,190 +116,184 @@ def tile_picked_yhs_prob_p_kernel(tc, x_words, x_scales, hT, turn, offs, pos1, p
         nc.vector.memset(warm_in[:], 0.0)
         nc.scalar.activation(warm_up[:], warm_in[:], SIGMOID)
 
-        turned = bank([P, P], "turned", 7)
+        turned = in_bank([P, P], "turned", 7)
         nc.tensor.transpose(turned[:], turn_rows[:], identity[:])
+        turn_cols = keep.tile([P, TURN_ROWS], F32, name="turn_cols")
         nc.scalar.copy(out=turn_cols[:], in_=turned[:, 0:TURN_ROWS])
-
         base_cols = keep.tile([P, TURN_ROWS], F32, name="base_cols")
         nc.scalar.activation(base_cols[:], turned[:, 0:TURN_ROWS], COPY, bias=0.5, scale=-0.5)
-        pair_cols = keep.tile([P, 4], F32, name="pair_cols")
-        nc.gpsimd.tensor_tensor(pair_cols[:], turn_cols[:, 0:4], turn_cols[:, 4:8], MULT)
-        sign_cols = keep.tile([P, 2], F32, name="sign_cols")
-        nc.gpsimd.tensor_tensor(sign_cols[:], pair_cols[:, 0:2], pair_cols[:, 2:4], MULT)
-        turns = [keep.tile([P, 2, U], F32, name="turns%d" % pair) for pair in range(D // 2)]
+        pair_cols = keep.tile([P, 2 * HALVES], F32, name="pair_cols")
+        nc.gpsimd.tensor_tensor(pair_cols[:], turn_cols[:, 0 : 2 * HALVES], turn_cols[:, 2 * HALVES : TURN_ROWS], MULT)
+        sign_cols = keep.tile([P, HALVES], F32, name="sign_cols")
+        nc.gpsimd.tensor_tensor(sign_cols[:], pair_cols[:, 0:HALVES], pair_cols[:, HALVES : 2 * HALVES], MULT)
+        spread = [in_bank([P, 2, U], "spread%d" % pair, 5 + pair) for pair in range(D // 2)]
+        turn_pairs = [keep.tile([P, 2, U], F32, name="turn_pair%d" % pair) for pair in range(D // 2)]
         for pair in range(D // 2):
-            spread = bank([P, 2, U], "spread%d" % pair, 2 + pair)
-            flat = spread[:].rearrange("p d u -> p (d u)")
-            for n in range(4):
-                column = turn_cols[:, 4 * pair + n : 4 * pair + n + 1].to_broadcast([P, P])
-                nc.tensor.transpose(flat[:, n * P : (n + 1) * P], column, identity[:])
-            nc.scalar.copy(out=turns[pair][:], in_=spread[:])
+            flat = spread[pair][:].rearrange("p d u -> p (d u)")
+            for n in range(2 * HALVES):
+                col = 2 * HALVES * pair + n
+                nc.tensor.transpose(flat[:, half(n)], turn_cols[:, col : col + 1].to_broadcast([P, P]), identity[:])
+            nc.scalar.copy(out=turn_pairs[pair][:], in_=spread[pair][:])
+        turns = [turn_pairs[d // 2][:, d % 2, :] for d in range(D)]
 
-        node_words = [placed([P, S], U32, "node_words0", None), placed([P, S], U32, "node_words1", 16)]
+        node_words = [placed([P, S], U32, "node_words0"), placed([P, S], U32, "node_words1", SCALES)]
+        node_scales = placed([P, S], U8, "node_scales")
         nc.vector.tensor_copy(node_words[0][:], word_table[0][:].indirect(node_list[:]))
         nc.vector.tensor_copy(node_scales[:], scale_table[:].indirect(node_list[:]))
         nc.vector.tensor_copy(node_words[1][:], word_table[1][:].indirect(node_list[:]))
 
-        bf16_at = {(0, 0): None, (0, 1): 1, (1, 0): 2, (1, 1): 3, (2, 0): 4, (2, 1): 5, (3, None): 6}
+        words_start = {(0, 0): WORDS_1, (0, 1): WORDS_1 + 3 * KIB}
         h_bf16, h_words, h_scales = {}, {}, {}
-        for piece, kib in bf16_at.items():
-            width = P * (PASSES if piece[1] is None else 1)
-            name = "%s_%s" % piece
-            h_bf16[piece] = placed([P, width * PACK], BF16, "h_bf16" + name, kib)
-            h_words[piece] = placed([P, width], U32, "h_words" + name, 0 if piece == (0, 0) else None)
-            h_scales[piece] = placed([P, width], U8, "h_scales" + name, None)
+        for b in range(LAST):
+            for o in range(PASSES):
+                start = WORDS_1 + (PASSES * b + o) * KIB
+                first = (b, o) == (0, 0)
+                h_bf16[b, o] = placed([P, P * PACK], BF16, "h_bf16_%d_%d" % (b, o), None if first else start)
+                h_words[b, o] = placed([P, P], U32, "h_words%d_%d" % (b, o), words_start.get((b, o)))[:]
+                h_scales[b, o] = placed([P, P], U8, "h_scales%d_%d" % (b, o))[:]
+        last_bf16 = placed([P, PASSES * P * PACK], BF16, "last_bf16", ROUNDED_3)
+        last_words = placed([P, PASSES * P], U32, "last_words")
+        last_scales = placed([P, PASSES * P], U8, "last_scales")
+        for o in range(PASSES):
+            h_words[LAST, o] = last_words[:, half(o)]
+            h_scales[LAST, o] = last_scales[:, half(o)]
 
         def rounding_views(b, o):
-            if o is None:
-                return (
-                    h_bf16[b, o][:].rearrange("p (o c i j) -> p o c j i", o=PASSES, i=RUN, j=PACK),
-                    h_whole[b][:].rearrange("p o j (c i) -> p o c j i", i=RUN),
-                )
             return (
                 h_bf16[b, o][:].rearrange("p (c i j) -> p c j i", i=RUN, j=PACK),
                 h_raw[b, o].rearrange("p j (c i) -> p c j i", i=RUN),
             )
 
-        def round_h(b, o):
-            dst, src = rounding_views(b, o)
-            nc.vector.tensor_copy(out=dst, in_=src)
-
-        def round_on_gpsimd(b, o):
-            dst, src = rounding_views(b, o)
-            if o is None:
-                for n in range(PASSES):
-                    nc.gpsimd.tensor_scalar(dst[:, n], src[:, n], 1.0, 0.0, MULT, ADD)
-            else:
-                nc.gpsimd.tensor_scalar(dst, src, 1.0, 0.0, MULT, ADD)
-
         def quantize_h(b, o):
-            nc.vector.quantize_mx(out=h_words[b, o][:].bitcast(FP8X4), scales=h_scales[b, o][:], in_=h_bf16[b, o][:])
+            nc.vector.quantize_mx(out=h_words[b, o].bitcast(FP8X4), scales=h_scales[b, o], in_=h_bf16[b, o][:])
 
         def product(acc, b, o, cols):
-            piece, at = ((b, o), slice(0, P)) if b < LAST else ((b, None), slice(o * P, (o + 1) * P))
             nc.tensor.matmul_mx(
                 out=acc,
-                lhsT=h_words[piece][:, at].bitcast(FP8X4),
-                lhsT_scale=h_scales[piece][:, at],
+                lhsT=h_words[b, o].bitcast(FP8X4),
+                lhsT_scale=h_scales[b, o],
                 rhs=node_words[o][:, cols].bitcast(FP8X4),
                 rhs_scale=node_scales[SCALE_ROWS * o : P, cols],
                 start=(o == 0),
                 stop=(o == PASSES - 1),
             )
 
-        ys = [placed([P, S], F32, "y%d" % b, {1: 9, 2: 4.5}.get(b)) for b in range(BLOCKS)]
-        accs = [None, bank([P, D - 1, S], "acc1", 4)[:, 0, :], bank([P, S], "acc2", 2)[:], bank([P, S], "acc3", 3)[:]]
-        halves = [bank([P, S // 2], "acc_half%d" % n, n) for n in range(2)]
-        cols = [slice(n * S // 2, (n + 1) * S // 2) for n in range(2)]
-        plain = [keep.tile([P, D, U], F32, name="plain%d" % b) for b in range(BLOCKS)]
-        signed = [
-            [placed([P, 2, U], F32, "signed%d_%d" % (b, pair), {(0, 1): 6.5, (3, 0): 24.5, (3, 1): 27}.get((b, pair))) for pair in range(2)]
-            for b in range(BLOCKS)
+        node_halves = [slice(n * S // 2, (n + 1) * S // 2) for n in range(2)]
+        first_accs = [in_bank([P, S // 2], "first_acc%d" % n, n) for n in range(2)]
+        accs = {
+            1: in_bank([P, LINKS, S], "acc1", 2)[:, 0, :],
+            2: in_bank([P, S], "acc2", 5)[:],
+            3: in_bank([P, S], "acc3", 6)[:],
+        }
+        y_start = {1: WORDS_1 + 5 * KIB // 2, 2: ROUNDED_3 - 3 * KIB // 2}
+        ys = [placed([P, S], F32, "y%d" % b, y_start.get(b)) for b in range(BANDS)]
+
+        def round_h(b, o):
+            dst, src = rounding_views(b, o)
+            nc.vector.tensor_copy(out=dst, in_=src)
+
+        def quantize_multiply(b, o):
+            quantize_h(b, o)
+            product(accs[b], b, o, slice(0, S))
+
+        def empty(b):
+            nc.vector.tensor_copy(out=ys[b][:], in_=accs[b])
+
+        sigmoids = [placed([P, D, U], F32, "sigmoids%d" % b) for b in range(BANDS)]
+        flip_banks = ((2, 3, 4), (0, 1, 2), (3, 4, 7))
+        back_banks = (5, 6, 0)
+        first_span = psum.tile([P, LINKS, S], F32, name="first_span", offset=0)
+        flipped = [
+            [
+                first_span[:, LINKS - 1, 0:U].rearrange("p (h t) -> p h t", h=HALVES)
+                if (b, d) == (0, 0)
+                else in_bank([P, HALVES, P], "flipped%d_%d" % (b, d), flip_banks[b][d])[:]
+                for d in range(LINKS)
+            ]
+            for b in range(LAST)
         ]
-        so_far = [[placed([P, U], F32, "so_far%d_%d" % (b, d), {(0, 3): 32, (1, 3): 23.5}.get((b, d))) for d in range(D)] for b in range(BLOCKS)]
+        back = [in_bank([P, U], "back%d" % b, back_banks[b]) for b in range(LAST)]
+        chain_start = {(0, 0): RAW_LATE + 2 * KIB, (0, 1): RAW_LATE + 3 * KIB, (1, 1): CHAIN_1_1, (2, 0): CHAIN_2_0, (2, 1): CHAIN_2_1}
+        chain = [
+            [placed([P, HALVES, P], F32, "chain%d_%d" % (b, d), chain_start.get((b, d))) for d in range(LINKS)]
+            for b in range(LAST)
+        ]
+        shifted_start = {0: ROUNDED_3 + KIB // 2}
+        shifted = [placed([P, U], F32, "shifted%d" % b, shifted_start.get(b)) for b in range(LAST)]
+        result_start = {0: CHAIN_1_1, 1: CHAIN_2_0 - KIB // 2}
+        results = [placed([P, U], F32, "result%d" % b, result_start.get(b)) for b in range(BANDS)]
 
-        def scores(b, copy):
-            copy(out=ys[b][:], in_=accs[b])
-            gathers(b)
-
-        def gathers(b):
+        def gather_sigmoids(b):
             for d in range(D):
-                if (b, d) == (LAST, D - 1):
-                    for n in range(2):
-                        half_list = path_lists[d][:, n * U // 32 : (n + 1) * U // 32]
-                        nc.scalar.activation(plain[b][:, d, n * P : (n + 1) * P], ys[b][:].indirect(half_list), SIGMOID)
-                else:
-                    nc.scalar.activation(plain[b][:, d, :], ys[b][:].indirect(path_lists[d][:]), SIGMOID)
-
-        flipped = [[bank([P, 2, P], "flipped%d_%d" % (b, d), ((4, 5, 6), (0, 1, 7), (4, 5, 6))[b][d]) for d in range(D - 1)] for b in range(LAST)]
-        chain = [[placed([P, 2, P], F32, "chain%d_%d" % (b, d), {(0, 0): 20, (0, 1): 21, (1, 1): 32, (2, 0): 24, (2, 1): 27}.get((b, d))) for d in range(D - 1)] for b in range(LAST)]
-        back = [bank([P, U], "back%d" % b, (2, 3, 0)[b]) for b in range(LAST)]
+                pieces = HALVES if (b, d) == (LAST, D - 1) else 1
+                for n in range(pieces):
+                    words = slice(n * U // pieces, (n + 1) * U // pieces)
+                    offsets = path_lists[d][:, words.start // 16 : words.stop // 16]
+                    nc.scalar.activation(sigmoids[b][:, d, words], ys[b][:].indirect(offsets), SIGMOID)
 
         def link(b, d):
-            for half in range(2):
-                nc.tensor.transpose(flipped[b][d][:, half, :], plain[b][:, d, half * P : (half + 1) * P], identity[:])
-            for half in range(2):
-                source = flipped[b][d][:, half, :]
-                base = base_cols[:, 2 * d + half : 2 * d + half + 1]
-                target = chain[b][d][:, half, :]
+            for h in range(HALVES):
+                nc.tensor.transpose(flipped[b][d][:, h, :], sigmoids[b][:, d, half(h)], identity[:])
+            for h in range(HALVES):
+                base = base_cols[:, HALVES * d + h : HALVES * d + h + 1]
+                target = chain[b][d][:, h, :]
                 if d == 0:
-                    nc.vector.tensor_scalar(target, source, base, sign_cols[:, half : half + 1], SUBTRACT, MULT)
+                    nc.vector.tensor_scalar(target, flipped[b][d][:, h, :], base, sign_cols[:, h : h + 1], SUBTRACT, MULT)
                 else:
-                    nc.vector.scalar_tensor_tensor(target, source, base, chain[b][d - 1][:, half, :], SUBTRACT, MULT)
-                if d == D - 2:
-                    nc.tensor.transpose(back[b][:, half * P : (half + 1) * P], target, identity[:])
+                    nc.vector.scalar_tensor_tensor(
+                        target, flipped[b][d][:, h, :], base, chain[b][d - 1][:, h, :], SUBTRACT, MULT
+                    )
+                if d == LINKS - 1:
+                    nc.tensor.transpose(back[b][:, half(h)], target, identity[:])
 
         def shift(b):
-            nc.gpsimd.tensor_tensor(signed[b][1][:, 1, :], plain[b][:, D - 1, :], last_base[:], SUBTRACT)
+            nc.gpsimd.tensor_tensor(shifted[b][:], sigmoids[b][:, D - 1, :], last_base[:], SUBTRACT)
 
         def finish(b):
-            nc.vector.tensor_tensor(so_far[b][D - 1][:], signed[b][1][:, 1, :], back[b][:], MULT)
-            nc.sync.dma_start(out=out[b * P : (b + 1) * P, :], in_=so_far[b][D - 1][:])
-
-        def last_half(n):
-            at = slice(n * P, (n + 1) * P)
-            centred = signed[LAST][1][:, 1, at]
-            nc.vector.scalar_tensor_tensor(centred, plain[LAST][:, D - 1, at], -0.5, turns[1][:, 1, at], ADD, MULT)
-
-        def finish_half(n):
-            at = slice(n * P, (n + 1) * P)
-            result = so_far[LAST][D - 1][:, at]
-            nc.vector.scalar_tensor_tensor(result, signed[LAST][1][:, 1, at], 0.5, so_far[LAST][D - 2][:, at], ADD, MULT)
-            nc.sync.dma_start(out=out[LAST * P : (LAST + 1) * P, at], in_=result)
-
-        def centre(b, lo, hi):
-            at_pair = slice(lo % 2, lo % 2 + hi - lo)
-            nc.vector.scalar_tensor_tensor(
-                signed[b][lo // 2][:, at_pair, :], plain[b][:, lo:hi, :], -0.5, turns[lo // 2][:, at_pair, :], ADD, MULT
-            )
-
-        def factor(b, d):
-            centred = signed[b][d // 2][:, d % 2, :]
-            if d == 0:
-                nc.vector.tensor_scalar_add(so_far[b][0][:], centred, 0.5)
-            else:
-                nc.vector.scalar_tensor_tensor(so_far[b][d][:], centred, 0.5, so_far[b][d - 1][:], ADD, MULT)
-            if d == D - 1:
-                nc.sync.dma_start(out=out[b * P : (b + 1) * P, :], in_=so_far[b][d][:])
+            nc.vector.tensor_tensor(results[b][:], shifted[b][:], back[b][:], MULT)
+            nc.sync.dma_start(out=out[half(b), :], in_=results[b][:])
 
         dst, src = rounding_views(0, 0)
         nc.scalar.copy(out=dst, in_=src)
         quantize_h(0, 0)
         for n in range(2):
-            product(halves[n][:], 0, 0, cols[n])
+            product(first_accs[n][:], 0, 0, node_halves[n])
         dst, src = rounding_views(0, 1)
         nc.vector.tensor_copy(out=dst[:, 0:VECTOR_RUNS], in_=src[:, 0:VECTOR_RUNS])
         nc.scalar.copy(out=dst[:, VECTOR_RUNS:RUNS], in_=src[:, VECTOR_RUNS:RUNS])
         quantize_h(0, 1)
         for n in range(2):
-            product(halves[n][:], 0, 1, cols[n])
-        last_base = placed([P, U], F32, "last_base", 34)
-        nc.scalar.activation(last_base[:], spread[:, 1, :], COPY, bias=0.5, scale=-0.5)
-        nc.scalar.copy(out=ys[0][:, cols[0]], in_=halves[0][:])
-        nc.vector.tensor_copy(out=ys[0][:, cols[1]], in_=halves[1][:])
-        gathers(0)
-        for o in range(PASSES):
-            round_h(1, o)
-            quantize_h(1, o)
-            product(accs[1], 1, o, slice(0, S))
-        round_h(2, 0)
-        quantize_h(2, 0)
-        product(accs[2], 2, 0, slice(0, S))
+            product(first_accs[n][:], 0, 1, node_halves[n])
+        last_base = placed([P, U], F32, "last_base", RAW_0)
+        nc.scalar.activation(last_base[:], spread[1][:, 1, :], COPY, bias=0.5, scale=-0.5)
+        nc.scalar.copy(out=ys[0][:, node_halves[0]], in_=first_accs[0][:])
+        nc.vector.tensor_copy(out=ys[0][:, node_halves[1]], in_=first_accs[1][:])
+        gather_sigmoids(0)
+
+        for b, o in ((1, 0), (1, 1), (2, 0)):
+            round_h(b, o)
+            quantize_multiply(b, o)
+        empty(1)
+        gather_sigmoids(1)
         round_h(2, 1)
-        quantize_h(2, 1)
-        product(accs[2], 2, 1, slice(0, S))
-        scores(1, nc.vector.tensor_copy)
-        round_h(3, None)
+        nc.vector.tensor_copy(
+            out=last_bf16[:].rearrange("p (o c i j) -> p o c j i", o=PASSES, i=RUN, j=PACK),
+            in_=late_raw[:, :, :, half(1)].rearrange("p o j (c i) -> p o c j i", i=RUN),
+        )
+        quantize_multiply(2, 1)
         link(0, 0)
-        quantize_h(3, None)
+        nc.vector.quantize_mx(out=last_words[:].bitcast(FP8X4), scales=last_scales[:], in_=last_bf16[:])
         for o in range(PASSES):
-            product(accs[3], 3, o, slice(0, S))
-        scores(2, nc.vector.tensor_copy)
+            product(accs[LAST], LAST, o, slice(0, S))
+        empty(2)
+        gather_sigmoids(2)
+
         link(0, 1)
         shift(0)
         link(0, 2)
         link(1, 0)
-        scores(3, nc.vector.tensor_copy)
+        empty(LAST)
+        gather_sigmoids(LAST)
         link(1, 1)
         shift(1)
         link(1, 2)
@@ -303,15 +302,33 @@ def tile_picked_yhs_prob_p_kernel(tc, x_words, x_scales, hT, turn, offs, pos1, p
         link(2, 1)
         shift(2)
         link(2, 2)
-        centre(3, 0, 1)
+
+        centred_pairs = [
+            placed([P, 2, U], F32, "centred_pair0", CHAIN_2_0 + KIB // 2),
+            placed([P, 2, U], F32, "centred_pair1", CHAIN_2_1),
+        ]
+        centred = [centred_pairs[d // 2][:, d % 2, :] for d in range(D)]
+        so_far = [placed([P, U], F32, "so_far%d" % d) for d in range(D - 1)]
+
+        def centre(d, words):
+            nc.vector.scalar_tensor_tensor(
+                centred[d][:, words], sigmoids[LAST][:, d, words], -0.5, turns[d][:, words], ADD, MULT
+            )
+
+        def extend(target, d, words):
+            nc.vector.scalar_tensor_tensor(target[:, words], centred[d][:, words], 0.5, so_far[d - 1][:, words], ADD, MULT)
+
+        every = slice(0, U)
+        centre(0, every)
         finish(1)
-        factor(3, 0)
+        nc.vector.tensor_scalar_add(so_far[0][:], centred[0], 0.5)
         finish(2)
-        centre(3, 1, 2)
-        factor(3, 1)
-        centre(3, 2, 3)
-        last_half(0)
-        factor(3, 2)
-        last_half(1)
-        finish_half(0)
-        finish_half(1)
+        centre(1, every)
+        extend(so_far[1], 1, every)
+        centre(2, every)
+        centre(3, half(0))
+        extend(so_far[2], 2, every)
+        centre(3, half(1))
+        for h in range(HALVES):
+            extend(results[LAST], 3, half(h))
+            nc.sync.dma_start(out=out[half(LAST), half(h)], in_=results[LAST][:, half(h)])

@@ -146,13 +146,16 @@ def tile_picked_yhs_prob_p_kernel(tc, x_words, x_scales, hT, turn, offs, pos1, p
         h_bf16, h_words, h_scales = {}, {}, {}
         for b in range(LAST):
             for o in range(PASSES):
-                start = WORDS_1 + (PASSES * b + o) * KIB
+                start = WORDS_1 + (PASSES * b + o) * KIB + (2 * KIB if (b, o) == (2, 1) else 0)
                 first = (b, o) == (0, 0)
                 h_bf16[b, o] = placed([P, P * PACK], BF16, "h_bf16_%d_%d" % (b, o), None if first else start)
                 h_words[b, o] = placed([P, P], U32, "h_words%d_%d" % (b, o), words_start.get((b, o)))[:]
                 h_scales[b, o] = placed([P, P], U8, "h_scales%d_%d" % (b, o))[:]
-        last_bf16 = placed([P, PASSES * P * PACK], BF16, "last_bf16", ROUNDED_3)
-        last_words = placed([P, PASSES * P], U32, "last_words")
+        last_bf16 = [
+            placed([P, P * PACK], BF16, "last_bf16_0", WORDS_1 + 9 * KIB // 2),
+            placed([P, P * PACK], BF16, "last_bf16_1", ROUNDED_3),
+        ]
+        last_words = placed([P, PASSES * P], U32, "last_words", RAW_LATE)
         last_scales = placed([P, PASSES * P], U8, "last_scales")
         for o in range(PASSES):
             h_words[LAST, o] = last_words[:, half(o)]
@@ -224,12 +227,12 @@ def tile_picked_yhs_prob_p_kernel(tc, x_words, x_scales, hT, turn, offs, pos1, p
         results = [placed([P, U], F32, "result%d" % b, result_start.get(b)) for b in range(BANDS)]
 
         def gather_sigmoids(b):
-            for d in range(D):
-                pieces = HALVES if (b, d) == (LAST, D - 1) else 1
-                for n in range(pieces):
-                    words = slice(n * U // pieces, (n + 1) * U // pieces)
-                    offsets = path_lists[d][:, words.start // 16 : words.stop // 16]
-                    nc.scalar.activation(sigmoids[b][:, d, words], ys[b][:].indirect(offsets), SIGMOID)
+            whole = D if b < LAST else D - 2
+            steps = [(d, slice(0, U)) for d in range(whole)]
+            steps = steps + [(d, half(h)) for h in range(HALVES) for d in range(whole, D)]
+            for d, words in steps:
+                offsets = path_lists[d][:, words.start // 16 : words.stop // 16]
+                nc.scalar.activation(sigmoids[b][:, d, words], ys[b][:].indirect(offsets), SIGMOID)
 
         def link(b, d):
             for h in range(HALVES):
@@ -273,16 +276,25 @@ def tile_picked_yhs_prob_p_kernel(tc, x_words, x_scales, hT, turn, offs, pos1, p
         for b, o in ((1, 0), (1, 1), (2, 0)):
             round_h(b, o)
             quantize_multiply(b, o)
+        nc.gpsimd.tensor_scalar(
+            last_bf16[0][:].rearrange("p (t j) -> p t j", j=PACK),
+            late_raw[:, 0, :, half(1)].rearrange("p j t -> p t j"),
+            1.0,
+            0.0,
+            MULT,
+            ADD,
+        )
         empty(1)
         gather_sigmoids(1)
         round_h(2, 1)
         nc.vector.tensor_copy(
-            out=last_bf16[:].rearrange("p (o c i j) -> p o c j i", o=PASSES, i=RUN, j=PACK),
-            in_=late_raw[:, :, :, half(1)].rearrange("p o j (c i) -> p o c j i", i=RUN),
+            out=last_bf16[1][:].rearrange("p (c i j) -> p c j i", i=RUN, j=PACK),
+            in_=late_raw[:, 1, :, half(1)].rearrange("p j (c i) -> p c j i", i=RUN),
         )
         quantize_multiply(2, 1)
         link(0, 0)
-        nc.vector.quantize_mx(out=last_words[:].bitcast(FP8X4), scales=last_scales[:], in_=last_bf16[:])
+        nc.vector.quantize_mx(out=h_words[LAST, 0].bitcast(FP8X4), scales=h_scales[LAST, 0], in_=last_bf16[0][:])
+        nc.vector.quantize_mx(out=h_words[LAST, 1].bitcast(FP8X4), scales=h_scales[LAST, 1], in_=last_bf16[1][:])
         for o in range(PASSES):
             product(accs[LAST], LAST, o, slice(0, S))
         empty(2)
@@ -300,6 +312,7 @@ def tile_picked_yhs_prob_p_kernel(tc, x_words, x_scales, hT, turn, offs, pos1, p
         link(2, 0)
         finish(0)
         link(2, 1)
+        finish(1)
         shift(2)
         link(2, 2)
 
@@ -320,15 +333,17 @@ def tile_picked_yhs_prob_p_kernel(tc, x_words, x_scales, hT, turn, offs, pos1, p
 
         every = slice(0, U)
         centre(0, every)
-        finish(1)
-        nc.vector.tensor_scalar_add(so_far[0][:], centred[0], 0.5)
         finish(2)
+        nc.vector.tensor_scalar_add(so_far[0][:], centred[0], 0.5)
         centre(1, every)
         extend(so_far[1], 1, every)
-        centre(2, every)
+        centre(2, half(0))
         centre(3, half(0))
-        extend(so_far[2], 2, every)
+        extend(so_far[2], 2, half(0))
+        centre(2, half(1))
+        extend(results[LAST], 3, half(0))
+        nc.sync.dma_start(out=out[half(LAST), half(0)], in_=results[LAST][:, half(0)])
+        extend(so_far[2], 2, half(1))
         centre(3, half(1))
-        for h in range(HALVES):
-            extend(results[LAST], 3, half(h))
-            nc.sync.dma_start(out=out[half(LAST), half(h)], in_=results[LAST][:, half(h)])
+        extend(results[LAST], 3, half(1))
+        nc.sync.dma_start(out=out[half(LAST), half(1)], in_=results[LAST][:, half(1)])

@@ -30,19 +30,15 @@ HALVES = U // P
 TURN_ROWS = D * HALVES
 LINKS = D - 1
 RUN = 4
-RUNS = P // RUN
-VECTOR_RUNS = 20
 KIB = 1024
 BANK = 2 * KIB
 
 WORDS_1 = 0
-RAW_LATE = 8 * KIB
-SCALES = 16 * KIB
-CHAIN_2_0 = 24 * KIB
-CHAIN_2_1 = 27 * KIB
-CHAIN_1_1 = 32 * KIB
-RAW_0 = 34 * KIB
-ROUNDED_3 = WORDS_1 + 6 * KIB
+SCALES = 8 * KIB
+ROUNDED_FIRST = 10 * KIB
+RAW_LATE = 12 * KIB
+CHAIN_1_0 = 16 * KIB
+FOURTH = 20 * KIB
 
 
 def tile_picked_yhs_prob_p_kernel(tc, x_words, x_scales, hT, turn, offs, pos1, pos2, pos3, pos4, out):
@@ -69,14 +65,11 @@ def tile_picked_yhs_prob_p_kernel(tc, x_words, x_scales, hT, turn, offs, pos1, p
         scale_table = placed([P, T], U8, "scale_table", SCALES)
         identity = keep.tile([P, P], F32, name="identity")
         turn_rows = keep.tile([P, P], F32, name="turn_rows")
-        h_raw = {
-            (b, o): placed([P, PACK, P], F32, "h_raw%d_%d" % (b, o), RAW_0 if (b, o) == (0, 0) else None)[:]
-            for b in range(2)
-            for o in range(PASSES)
-        }
-        late_raw = placed([P, PASSES, PACK, 2 * P], F32, "late_raw", RAW_LATE)
+        h_raw = {(b, o): placed([P, PACK, P], F32, "h_raw%d_%d" % (b, o))[:] for b in range(2) for o in range(PASSES)}
+        late_raw = [placed([P, PACK, 2 * P], F32, "late_raw0", RAW_LATE), placed([P, PACK, 2 * P], F32, "late_raw1")]
         for o in range(PASSES):
-            h_raw[2, o] = late_raw[:, o, :, half(0)]
+            for b in range(2, BANDS):
+                h_raw[b, o] = late_raw[o][:, :, half(b - 2)]
 
         def load_words(o):
             words = x_words[o].rearrange("p n r -> p (n r)").bitcast(I32)
@@ -98,17 +91,18 @@ def tile_picked_yhs_prob_p_kernel(tc, x_words, x_scales, hT, turn, offs, pos1, p
                 in_=x_scales[:, SCALE_ROWS * q : SCALE_ROWS * (q + 1), :].bitcast(I32),
             )
         load_words(0)
-        load_path(0)
         nc.sync.dma_start(out=turn_rows[0:TURN_ROWS, :], in_=turn[:, 0, :].rearrange("d (h c) -> d h c", c=P))
+        load_h(h_raw[0, 0], 0, half(0))
         load_words(1)
-        for b in range(2):
-            for o in range(PASSES):
-                load_h(h_raw[b, o], o, half(b))
+        load_path(0)
+        load_h(h_raw[0, 1], 1, half(0))
+        for o in range(PASSES):
+            load_h(h_raw[1, o], o, half(1))
         load_path(1)
         load_path(2)
-        load_h(late_raw[:, 0], 0, slice(2 * P, V))
+        load_h(late_raw[0][:], 0, slice(2 * P, V))
         load_path(3)
-        load_h(late_raw[:, 1], 1, slice(2 * P, V))
+        load_h(late_raw[1][:], 1, slice(2 * P, V))
 
         make_identity(nc, identity[:])
         warm_in = keep.tile([P, 1], F32, name="warm_in")
@@ -116,65 +110,48 @@ def tile_picked_yhs_prob_p_kernel(tc, x_words, x_scales, hT, turn, offs, pos1, p
         nc.vector.memset(warm_in[:], 0.0)
         nc.scalar.activation(warm_up[:], warm_in[:], SIGMOID)
 
-        turned = in_bank([P, P], "turned", 7)
-        nc.tensor.transpose(turned[:], turn_rows[:], identity[:])
+        turned_span = in_bank([P, LINKS, S], "turned_span", 2)
+        turned = turned_span[:, 0, 0:P]
+        nc.tensor.transpose(turned, turn_rows[:], identity[:])
         turn_cols = keep.tile([P, TURN_ROWS], F32, name="turn_cols")
         nc.scalar.copy(out=turn_cols[:], in_=turned[:, 0:TURN_ROWS])
-        base_cols = keep.tile([P, TURN_ROWS], F32, name="base_cols")
-        nc.scalar.activation(base_cols[:], turned[:, 0:TURN_ROWS], COPY, bias=0.5, scale=-0.5)
         pair_cols = keep.tile([P, 2 * HALVES], F32, name="pair_cols")
         nc.gpsimd.tensor_tensor(pair_cols[:], turn_cols[:, 0 : 2 * HALVES], turn_cols[:, 2 * HALVES : TURN_ROWS], MULT)
         sign_cols = keep.tile([P, HALVES], F32, name="sign_cols")
         nc.gpsimd.tensor_tensor(sign_cols[:], pair_cols[:, 0:HALVES], pair_cols[:, HALVES : 2 * HALVES], MULT)
-        spread = [in_bank([P, 2, U], "spread%d" % pair, 5 + pair) for pair in range(D // 2)]
-        turn_pairs = [keep.tile([P, 2, U], F32, name="turn_pair%d" % pair) for pair in range(D // 2)]
-        for pair in range(D // 2):
-            flat = spread[pair][:].rearrange("p d u -> p (d u)")
-            for n in range(2 * HALVES):
-                col = 2 * HALVES * pair + n
-                nc.tensor.transpose(flat[:, half(n)], turn_cols[:, col : col + 1].to_broadcast([P, P]), identity[:])
-            nc.scalar.copy(out=turn_pairs[pair][:], in_=spread[pair][:])
-        turns = [turn_pairs[d // 2][:, d % 2, :] for d in range(D)]
+        spread = in_bank([P, U], "spread", 7)
+        for h in range(HALVES):
+            col = HALVES * LINKS + h
+            nc.tensor.transpose(spread[:, half(h)], turn_cols[:, col : col + 1].to_broadcast([P, P]), identity[:])
+        last_base = placed([P, U], F32, "last_base")
+        nc.scalar.activation(last_base[:], spread[:], COPY, bias=0.5, scale=-0.5)
 
-        node_words = [placed([P, S], U32, "node_words0"), placed([P, S], U32, "node_words1", SCALES)]
+        node_words = [placed([P, S], U32, "node_words0"), placed([P, S], U32, "node_words1", SCALES + KIB)]
         node_scales = placed([P, S], U8, "node_scales")
-        nc.vector.tensor_copy(node_words[0][:], word_table[0][:].indirect(node_list[:]))
-        nc.vector.tensor_copy(node_scales[:], scale_table[:].indirect(node_list[:]))
-        nc.vector.tensor_copy(node_words[1][:], word_table[1][:].indirect(node_list[:]))
 
-        words_start = {(0, 0): WORDS_1, (0, 1): WORDS_1 + 3 * KIB}
+        pieces = [(0, 1), (1, 0), (1, 1), (2, 0), (3, 0), (2, 1), (3, 1)]
+        rounded_start = {piece: WORDS_1 + n * KIB for n, piece in enumerate(pieces)}
+        rounded_start[0, 0] = ROUNDED_FIRST
         h_bf16, h_words, h_scales = {}, {}, {}
-        for b in range(LAST):
-            for o in range(PASSES):
-                start = WORDS_1 + (PASSES * b + o) * KIB + (2 * KIB if (b, o) == (2, 1) else 0)
-                first = (b, o) == (0, 0)
-                h_bf16[b, o] = placed([P, P * PACK], BF16, "h_bf16_%d_%d" % (b, o), None if first else start)
-                h_words[b, o] = placed([P, P], U32, "h_words%d_%d" % (b, o), words_start.get((b, o)))[:]
-                h_scales[b, o] = placed([P, P], U8, "h_scales%d_%d" % (b, o))[:]
-        last_bf16 = [
-            placed([P, P * PACK], BF16, "last_bf16_0", WORDS_1 + 9 * KIB // 2),
-            placed([P, P * PACK], BF16, "last_bf16_1", ROUNDED_3),
-        ]
-        last_words = placed([P, PASSES * P], U32, "last_words", RAW_LATE)
-        last_scales = placed([P, PASSES * P], U8, "last_scales")
-        for o in range(PASSES):
-            h_words[LAST, o] = last_words[:, half(o)]
-            h_scales[LAST, o] = last_scales[:, half(o)]
+        for (b, o), start in rounded_start.items():
+            h_bf16[b, o] = placed([P, P * PACK], BF16, "h_bf16_%d_%d" % (b, o), start)
+            h_words[b, o] = placed([P, P], U32, "h_words%d_%d" % (b, o))
+            h_scales[b, o] = placed([P, P], U8, "h_scales%d_%d" % (b, o))
 
-        def rounding_views(b, o):
-            return (
-                h_bf16[b, o][:].rearrange("p (c i j) -> p c j i", i=RUN, j=PACK),
-                h_raw[b, o].rearrange("p j (c i) -> p c j i", i=RUN),
+        def round_h(b, o):
+            nc.vector.tensor_copy(
+                out=h_bf16[b, o][:].rearrange("p (c i j) -> p c j i", i=RUN, j=PACK),
+                in_=h_raw[b, o].rearrange("p j (c i) -> p c j i", i=RUN),
             )
 
         def quantize_h(b, o):
-            nc.vector.quantize_mx(out=h_words[b, o].bitcast(FP8X4), scales=h_scales[b, o], in_=h_bf16[b, o][:])
+            nc.vector.quantize_mx(out=h_words[b, o][:].bitcast(FP8X4), scales=h_scales[b, o][:], in_=h_bf16[b, o][:])
 
         def product(acc, b, o, cols):
             nc.tensor.matmul_mx(
                 out=acc,
-                lhsT=h_words[b, o].bitcast(FP8X4),
-                lhsT_scale=h_scales[b, o],
+                lhsT=h_words[b, o][:].bitcast(FP8X4),
+                lhsT_scale=h_scales[b, o][:],
                 rhs=node_words[o][:, cols].bitcast(FP8X4),
                 rhs_scale=node_scales[SCALE_ROWS * o : P, cols],
                 start=(o == 0),
@@ -183,167 +160,161 @@ def tile_picked_yhs_prob_p_kernel(tc, x_words, x_scales, hT, turn, offs, pos1, p
 
         node_halves = [slice(n * S // 2, (n + 1) * S // 2) for n in range(2)]
         first_accs = [in_bank([P, S // 2], "first_acc%d" % n, n) for n in range(2)]
-        accs = {
-            1: in_bank([P, LINKS, S], "acc1", 2)[:, 0, :],
-            2: in_bank([P, S], "acc2", 5)[:],
-            3: in_bank([P, S], "acc3", 6)[:],
-        }
-        y_start = {1: WORDS_1 + 5 * KIB // 2, 2: ROUNDED_3 - 3 * KIB // 2}
-        ys = [placed([P, S], F32, "y%d" % b, y_start.get(b)) for b in range(BANDS)]
+        acc_banks = {1: 6, 2: 5, 3: 2}
+        accs = {b: in_bank([P, S], "acc%d" % b, bank) for b, bank in acc_banks.items()}
+        ys = [placed([P, S], F32, "y%d" % b, RAW_LATE if b == 1 else None) for b in range(BANDS)]
 
-        def round_h(b, o):
-            dst, src = rounding_views(b, o)
-            nc.vector.tensor_copy(out=dst, in_=src)
-
-        def quantize_multiply(b, o):
-            quantize_h(b, o)
-            product(accs[b], b, o, slice(0, S))
+        def multiply(b, o):
+            product(accs[b][:], b, o, slice(0, S))
 
         def empty(b):
-            nc.vector.tensor_copy(out=ys[b][:], in_=accs[b])
+            nc.vector.tensor_copy(out=ys[b][:], in_=accs[b][:])
 
-        sigmoids = [placed([P, D, U], F32, "sigmoids%d" % b) for b in range(BANDS)]
-        flip_banks = ((2, 3, 4), (0, 1, 2), (3, 4, 7))
-        back_banks = (5, 6, 0)
-        first_span = psum.tile([P, LINKS, S], F32, name="first_span", offset=0)
-        flipped = [
-            [
-                first_span[:, LINKS - 1, 0:U].rearrange("p (h t) -> p h t", h=HALVES)
-                if (b, d) == (0, 0)
-                else in_bank([P, HALVES, P], "flipped%d_%d" % (b, d), flip_banks[b][d])[:]
-                for d in range(LINKS)
-            ]
-            for b in range(LAST)
-        ]
-        back = [in_bank([P, U], "back%d" % b, back_banks[b]) for b in range(LAST)]
-        chain_start = {(0, 0): RAW_LATE + 2 * KIB, (0, 1): RAW_LATE + 3 * KIB, (1, 1): CHAIN_1_1, (2, 0): CHAIN_2_0, (2, 1): CHAIN_2_1}
-        chain = [
-            [placed([P, HALVES, P], F32, "chain%d_%d" % (b, d), chain_start.get((b, d))) for d in range(LINKS)]
-            for b in range(LAST)
-        ]
-        shifted_start = {0: ROUNDED_3 + KIB // 2}
-        shifted = [placed([P, U], F32, "shifted%d" % b, shifted_start.get(b)) for b in range(LAST)]
-        result_start = {0: CHAIN_1_1, 1: CHAIN_2_0 - KIB // 2}
-        results = [placed([P, U], F32, "result%d" % b, result_start.get(b)) for b in range(BANDS)]
+        sigmoid_start = {(0, 3): FOURTH, (1, 3): FOURTH + KIB, (2, 3): CHAIN_1_0 - KIB // 2}
+        sigmoids = {
+            (b, d): placed([P, U], F32, "sigmoids%d_%d" % (b, d), sigmoid_start.get((b, d)))[:]
+            for b in range(BANDS)
+            for d in range(D)
+            if (b, d) < (LAST, 2)
+        }
+        closing = placed([P, 2, U], F32, "closing", CHAIN_1_0 + KIB // 2)
+        for d in range(2, D):
+            sigmoids[LAST, d] = closing[:, d - 2, :]
 
-        def gather_sigmoids(b):
-            whole = D if b < LAST else D - 2
-            steps = [(d, slice(0, U)) for d in range(whole)]
-            steps = steps + [(d, half(h)) for h in range(HALVES) for d in range(whole, D)]
-            for d, words in steps:
-                offsets = path_lists[d][:, words.start // 16 : words.stop // 16]
-                nc.scalar.activation(sigmoids[b][:, d, words], ys[b][:].indirect(offsets), SIGMOID)
+        flip_banks = ((2, 3, 4), (5, 4, 2), (5, 4, 2), (5, 4))
+        flipped = {
+            (b, d): in_bank([P, HALVES, P], "flipped%d_%d" % (b, d), bank)
+            for b in range(BANDS)
+            for d, bank in enumerate(flip_banks[b])
+        }
+        closing_flipped = [in_bank([P, P], "closing_flipped%d" % h, bank) for h, bank in enumerate((2, 5))]
+        back = [in_bank([P, U], "back%d" % b, 3) for b in range(LAST)]
+        closing_back = [in_bank([P, P], "closing_back%d" % h, bank) for h, bank in enumerate((4, 6))]
+        chain_start = {(0, 0): rounded_start[2, 1], (1, 0): CHAIN_1_0}
+        chain = {
+            (b, d): placed([P, HALVES, P], F32, "chain%d_%d" % (b, d), chain_start.get((b, d)))
+            for b in range(BANDS)
+            for d in range(LINKS)
+        }
+        shifted_start = {0: rounded_start[3, 1], 1: FOURTH, 2: FOURTH + KIB}
+        shifted = [placed([P, U], F32, "shifted%d" % b, shifted_start.get(b)) for b in range(BANDS)]
+        results = [placed([P, U], F32, "result%d" % b) for b in range(BANDS)]
+        base_cols = placed([P, TURN_ROWS], F32, "base_cols", rounded_start[1, 1])
+
+        def gather(b, d, words=slice(0, U)):
+            offsets = path_lists[d][:, words.start // 16 : words.stop // 16]
+            nc.scalar.activation(sigmoids[b, d][:, words], ys[b][:].indirect(offsets), SIGMOID)
+
+        def flip(b, d):
+            for h in range(HALVES):
+                nc.tensor.transpose(flipped[b, d][:, h, :], sigmoids[b, d][:, half(h)], identity[:])
+
+        def link_half(b, d, h, source):
+            base = base_cols[:, HALVES * d + h : HALVES * d + h + 1]
+            target = chain[b, d][:, h, :]
+            if d == 0:
+                nc.vector.tensor_scalar(target, source, base, sign_cols[:, h : h + 1], SUBTRACT, MULT)
+            else:
+                nc.vector.scalar_tensor_tensor(target, source, base, chain[b, d - 1][:, h, :], SUBTRACT, MULT)
 
         def link(b, d):
             for h in range(HALVES):
-                nc.tensor.transpose(flipped[b][d][:, h, :], sigmoids[b][:, d, half(h)], identity[:])
+                link_half(b, d, h, flipped[b, d][:, h, :])
+
+        def turn_back(b):
             for h in range(HALVES):
-                base = base_cols[:, HALVES * d + h : HALVES * d + h + 1]
-                target = chain[b][d][:, h, :]
-                if d == 0:
-                    nc.vector.tensor_scalar(target, flipped[b][d][:, h, :], base, sign_cols[:, h : h + 1], SUBTRACT, MULT)
-                else:
-                    nc.vector.scalar_tensor_tensor(
-                        target, flipped[b][d][:, h, :], base, chain[b][d - 1][:, h, :], SUBTRACT, MULT
-                    )
-                if d == LINKS - 1:
-                    nc.tensor.transpose(back[b][:, half(h)], target, identity[:])
+                nc.tensor.transpose(back[b][:, half(h)], chain[b, LINKS - 1][:, h, :], identity[:])
 
         def shift(b):
-            nc.gpsimd.tensor_tensor(shifted[b][:], sigmoids[b][:, D - 1, :], last_base[:], SUBTRACT)
+            nc.gpsimd.tensor_tensor(shifted[b][:], sigmoids[b, D - 1], last_base[:], SUBTRACT)
 
         def finish(b):
             nc.vector.tensor_tensor(results[b][:], shifted[b][:], back[b][:], MULT)
             nc.sync.dma_start(out=out[half(b), :], in_=results[b][:])
 
-        dst, src = rounding_views(0, 0)
-        nc.scalar.copy(out=dst, in_=src)
+        nc.vector.tensor_copy(node_words[0][:], word_table[0][:].indirect(node_list[:]))
+        nc.vector.tensor_copy(node_scales[:], scale_table[:].indirect(node_list[:]))
+        round_h(0, 0)
         quantize_h(0, 0)
         for n in range(2):
             product(first_accs[n][:], 0, 0, node_halves[n])
-        dst, src = rounding_views(0, 1)
-        nc.vector.tensor_copy(out=dst[:, 0:VECTOR_RUNS], in_=src[:, 0:VECTOR_RUNS])
-        nc.scalar.copy(out=dst[:, VECTOR_RUNS:RUNS], in_=src[:, VECTOR_RUNS:RUNS])
+        nc.vector.tensor_copy(node_words[1][:], word_table[1][:].indirect(node_list[:]))
+        round_h(0, 1)
         quantize_h(0, 1)
         for n in range(2):
             product(first_accs[n][:], 0, 1, node_halves[n])
-        last_base = placed([P, U], F32, "last_base", RAW_0)
-        nc.scalar.activation(last_base[:], spread[1][:, 1, :], COPY, bias=0.5, scale=-0.5)
-        nc.scalar.copy(out=ys[0][:, node_halves[0]], in_=first_accs[0][:])
-        nc.vector.tensor_copy(out=ys[0][:, node_halves[1]], in_=first_accs[1][:])
-        gather_sigmoids(0)
-
-        for b, o in ((1, 0), (1, 1), (2, 0)):
-            round_h(b, o)
-            quantize_multiply(b, o)
-        nc.gpsimd.tensor_scalar(
-            last_bf16[0][:].rearrange("p (t j) -> p t j", j=PACK),
-            late_raw[:, 0, :, half(1)].rearrange("p j t -> p t j"),
-            1.0,
-            0.0,
-            MULT,
-            ADD,
-        )
-        empty(1)
-        gather_sigmoids(1)
-        round_h(2, 1)
-        nc.vector.tensor_copy(
-            out=last_bf16[1][:].rearrange("p (c i j) -> p c j i", i=RUN, j=PACK),
-            in_=late_raw[:, 1, :, half(1)].rearrange("p j (c i) -> p c j i", i=RUN),
-        )
-        quantize_multiply(2, 1)
-        link(0, 0)
-        nc.vector.quantize_mx(out=h_words[LAST, 0].bitcast(FP8X4), scales=h_scales[LAST, 0], in_=last_bf16[0][:])
-        nc.vector.quantize_mx(out=h_words[LAST, 1].bitcast(FP8X4), scales=h_scales[LAST, 1], in_=last_bf16[1][:])
+            nc.scalar.copy(out=ys[0][:, node_halves[n]], in_=first_accs[n][:])
         for o in range(PASSES):
-            product(accs[LAST], LAST, o, slice(0, S))
-        empty(2)
-        gather_sigmoids(2)
+            round_h(1, o)
+            quantize_h(1, o)
+            multiply(1, o)
+        for d in range(D):
+            gather(0, d)
+        nc.vector.tensor_scalar(base_cols[:], turned[:, 0:TURN_ROWS], -0.5, 0.5, MULT, ADD)
+        for d in range(LINKS):
+            flip(0, d)
 
-        link(0, 1)
+        round_h(2, 0)
+        round_h(3, 0)
+        quantize_h(2, 0)
+        multiply(2, 0)
+        empty(1)
+        for d in range(D):
+            gather(1, d)
+        quantize_h(3, 0)
+        round_h(2, 1)
+        round_h(3, 1)
+        quantize_h(2, 1)
+        multiply(2, 1)
+        quantize_h(3, 1)
         shift(0)
+        link(0, 0)
+        for o in range(PASSES):
+            multiply(3, o)
+        link(0, 1)
+        empty(2)
+        for d in range(LINKS):
+            gather(2, d)
+        flip(1, 0)
         link(0, 2)
-        link(1, 0)
-        empty(LAST)
-        gather_sigmoids(LAST)
-        link(1, 1)
+        flip(1, 1)
+        turn_back(0)
         shift(1)
-        link(1, 2)
-        link(2, 0)
+        empty(3)
+        gather(3, 0)
+        gather(3, 1)
+        flip(1, 2)
+        link(1, 0)
+        flip(2, 0)
+        link(1, 1)
+        gather(2, 3)
+        for d in range(2, D):
+            for h in range(HALVES):
+                gather(LAST, d, half(h))
+        flip(2, 1)
         finish(0)
+        link(1, 2)
+        turn_back(1)
+        flip(2, 2)
+        link(2, 0)
+        flip(3, 0)
         link(2, 1)
+        flip(3, 1)
         finish(1)
-        shift(2)
         link(2, 2)
-
-        centred_pairs = [
-            placed([P, 2, U], F32, "centred_pair0", CHAIN_2_0 + KIB // 2),
-            placed([P, 2, U], F32, "centred_pair1", CHAIN_2_1),
-        ]
-        centred = [centred_pairs[d // 2][:, d % 2, :] for d in range(D)]
-        so_far = [placed([P, U], F32, "so_far%d" % d) for d in range(D - 1)]
-
-        def centre(d, words):
-            nc.vector.scalar_tensor_tensor(
-                centred[d][:, words], sigmoids[LAST][:, d, words], -0.5, turns[d][:, words], ADD, MULT
-            )
-
-        def extend(target, d, words):
-            nc.vector.scalar_tensor_tensor(target[:, words], centred[d][:, words], 0.5, so_far[d - 1][:, words], ADD, MULT)
-
-        every = slice(0, U)
-        centre(0, every)
+        shift(2)
+        turn_back(2)
+        link(3, 0)
+        link(3, 1)
+        for h in range(HALVES):
+            nc.tensor.transpose(closing_flipped[h][:], sigmoids[LAST, 2][:, half(h)], identity[:])
+        link_half(LAST, 2, 0, closing_flipped[0][:])
         finish(2)
-        nc.vector.tensor_scalar_add(so_far[0][:], centred[0], 0.5)
-        centre(1, every)
-        extend(so_far[1], 1, every)
-        centre(2, half(0))
-        centre(3, half(0))
-        extend(so_far[2], 2, half(0))
-        centre(2, half(1))
-        extend(results[LAST], 3, half(0))
-        nc.sync.dma_start(out=out[half(LAST), half(0)], in_=results[LAST][:, half(0)])
-        extend(so_far[2], 2, half(1))
-        centre(3, half(1))
-        extend(results[LAST], 3, half(1))
-        nc.sync.dma_start(out=out[half(LAST), half(1)], in_=results[LAST][:, half(1)])
+        link_half(LAST, 2, 1, closing_flipped[1][:])
+        for h in range(HALVES):
+            nc.tensor.transpose(closing_back[h][:], chain[LAST, 2][:, h, :], identity[:])
+        for h in range(HALVES):
+            nc.vector.tensor_tensor(shifted[LAST][:, half(h)], sigmoids[LAST, 3][:, half(h)], last_base[:, half(h)], SUBTRACT)
+        for h in range(HALVES):
+            nc.vector.tensor_tensor(results[LAST][:, half(h)], shifted[LAST][:, half(h)], closing_back[h][:], MULT)
+            nc.sync.dma_start(out=out[half(LAST), half(h)], in_=results[LAST][:, half(h)])

@@ -34,11 +34,15 @@ KIB = 1024
 BANK = 2 * KIB
 
 WORDS_1 = 0
-SCALES = 8 * KIB
-ROUNDED_FIRST = 10 * KIB
 RAW_LATE = 12 * KIB
 CHAIN_1_0 = 16 * KIB
 FOURTH = 20 * KIB
+CLOSING = 24 * KIB
+WORDS_0 = 32 * KIB
+RAW_0 = 44 * KIB
+VECTOR_RUNS = 20
+RUNS = P // RUN
+SCALES = WORDS_0 + 8 * KIB + KIB // 2
 
 
 def tile_picked_yhs_prob_p_kernel(tc, x_words, x_scales, hT, turn, offs, pos1, pos2, pos3, pos4, out):
@@ -61,11 +65,11 @@ def tile_picked_yhs_prob_p_kernel(tc, x_words, x_scales, hT, turn, offs, pos1, p
 
         node_list = keep.tile([P, S // 16], U16, name="node_list")
         path_lists = [keep.tile([P, U // 16], U16, name="path_list%d" % d) for d in range(D)]
-        word_table = [placed([P, T], U32, "word_table0"), placed([P, T], U32, "word_table1", WORDS_1)]
+        word_table = [placed([P, T], U32, "word_table0", WORDS_0), placed([P, T], U32, "word_table1", WORDS_1)]
         scale_table = placed([P, T], U8, "scale_table", SCALES)
         identity = keep.tile([P, P], F32, name="identity")
         turn_rows = keep.tile([P, P], F32, name="turn_rows")
-        h_raw = {(b, o): placed([P, PACK, P], F32, "h_raw%d_%d" % (b, o))[:] for b in range(2) for o in range(PASSES)}
+        h_raw = {(b, o): placed([P, PACK, P], F32, "h_raw%d_%d" % (b, o), RAW_0 if (b, o) == (0, 0) else None)[:] for b in range(2) for o in range(PASSES)}
         late_raw = [placed([P, PACK, 2 * P], F32, "late_raw0", RAW_LATE), placed([P, PACK, 2 * P], F32, "late_raw1")]
         for o in range(PASSES):
             for b in range(2, BANDS):
@@ -91,11 +95,11 @@ def tile_picked_yhs_prob_p_kernel(tc, x_words, x_scales, hT, turn, offs, pos1, p
                 in_=x_scales[:, SCALE_ROWS * q : SCALE_ROWS * (q + 1), :].bitcast(I32),
             )
         load_words(0)
-        nc.sync.dma_start(out=turn_rows[0:TURN_ROWS, :], in_=turn[:, 0, :].rearrange("d (h c) -> d h c", c=P))
-        load_h(h_raw[0, 0], 0, half(0))
-        load_words(1)
         load_path(0)
-        load_h(h_raw[0, 1], 1, half(0))
+        nc.sync.dma_start(out=turn_rows[0:TURN_ROWS, :], in_=turn[:, 0, :].rearrange("d (h c) -> d h c", c=P))
+        load_words(1)
+        for o in range(PASSES):
+            load_h(h_raw[0, o], o, half(0))
         for o in range(PASSES):
             load_h(h_raw[1, o], o, half(1))
         load_path(1)
@@ -110,39 +114,53 @@ def tile_picked_yhs_prob_p_kernel(tc, x_words, x_scales, hT, turn, offs, pos1, p
         nc.vector.memset(warm_in[:], 0.0)
         nc.scalar.activation(warm_up[:], warm_in[:], SIGMOID)
 
-        turned_span = in_bank([P, LINKS, S], "turned_span", 2)
-        turned = turned_span[:, 0, 0:P]
+        node_words = [placed([P, S], U32, "node_words0"), placed([P, S], U32, "node_words1", SCALES)]
+        node_scales = placed([P, S], U8, "node_scales")
+        nc.vector.tensor_copy(node_words[0][:], word_table[0][:].indirect(node_list[:]))
+        nc.vector.tensor_copy(node_scales[:], scale_table[:].indirect(node_list[:]))
+        nc.vector.tensor_copy(node_words[1][:], word_table[1][:].indirect(node_list[:]))
+
+        turned = in_bank([P, P], "turned", 7)[:]
         nc.tensor.transpose(turned, turn_rows[:], identity[:])
-        turn_cols = keep.tile([P, TURN_ROWS], F32, name="turn_cols")
+        turn_cols = placed([P, TURN_ROWS], F32, "turn_cols")
         nc.scalar.copy(out=turn_cols[:], in_=turned[:, 0:TURN_ROWS])
+        base_cols = keep.tile([P, TURN_ROWS], F32, name="base_cols")
+        nc.scalar.activation(base_cols[:], turned[:, 0:TURN_ROWS], COPY, bias=0.5, scale=-0.5)
         pair_cols = keep.tile([P, 2 * HALVES], F32, name="pair_cols")
         nc.gpsimd.tensor_tensor(pair_cols[:], turn_cols[:, 0 : 2 * HALVES], turn_cols[:, 2 * HALVES : TURN_ROWS], MULT)
         sign_cols = keep.tile([P, HALVES], F32, name="sign_cols")
         nc.gpsimd.tensor_tensor(sign_cols[:], pair_cols[:, 0:HALVES], pair_cols[:, HALVES : 2 * HALVES], MULT)
-        spread = in_bank([P, U], "spread", 7)
-        for h in range(HALVES):
-            col = HALVES * LINKS + h
-            nc.tensor.transpose(spread[:, half(h)], turn_cols[:, col : col + 1].to_broadcast([P, P]), identity[:])
-        last_base = placed([P, U], F32, "last_base")
-        nc.scalar.activation(last_base[:], spread[:], COPY, bias=0.5, scale=-0.5)
+        spread = [in_bank([P, 2, U], "spread%d" % pair, 4 + pair)[:] for pair in range(D // 2)]
+        turn_pairs = [keep.tile([P, 2, U], F32, name="turn_pair%d" % pair) for pair in range(D // 2)]
+        for pair in range(D // 2):
+            flat = spread[pair].rearrange("p d u -> p (d u)")
+            for n in range(2 * HALVES):
+                col = 2 * HALVES * pair + n
+                nc.tensor.transpose(flat[:, half(n)], turn_cols[:, col : col + 1].to_broadcast([P, P]), identity[:])
+            nc.scalar.copy(out=turn_pairs[pair][:], in_=spread[pair])
+        turns = [turn_pairs[d // 2][:, d % 2, :] for d in range(D)]
 
-        node_words = [placed([P, S], U32, "node_words0"), placed([P, S], U32, "node_words1", SCALES + KIB)]
-        node_scales = placed([P, S], U8, "node_scales")
 
-        pieces = [(0, 1), (1, 0), (1, 1), (2, 0), (3, 0), (2, 1), (3, 1)]
+        pieces = [(1, 0), (1, 1), (2, 0), (3, 0), (2, 1), (3, 1)]
         rounded_start = {piece: WORDS_1 + n * KIB for n, piece in enumerate(pieces)}
-        rounded_start[0, 0] = ROUNDED_FIRST
+        rounded_start[0, 0] = None
+        rounded_start[0, 1] = WORDS_1 + 7 * KIB
+        words_start = {(0, 0): WORDS_1 + 6 * KIB}
         h_bf16, h_words, h_scales = {}, {}, {}
         for (b, o), start in rounded_start.items():
             h_bf16[b, o] = placed([P, P * PACK], BF16, "h_bf16_%d_%d" % (b, o), start)
-            h_words[b, o] = placed([P, P], U32, "h_words%d_%d" % (b, o))
+            h_words[b, o] = placed([P, P], U32, "h_words%d_%d" % (b, o), words_start.get((b, o)))
             h_scales[b, o] = placed([P, P], U8, "h_scales%d_%d" % (b, o))
 
-        def round_h(b, o):
-            nc.vector.tensor_copy(
-                out=h_bf16[b, o][:].rearrange("p (c i j) -> p c j i", i=RUN, j=PACK),
-                in_=h_raw[b, o].rearrange("p j (c i) -> p c j i", i=RUN),
+        def rounding_views(b, o):
+            return (
+                h_bf16[b, o][:].rearrange("p (c i j) -> p c j i", i=RUN, j=PACK),
+                h_raw[b, o].rearrange("p j (c i) -> p c j i", i=RUN),
             )
+
+        def round_h(b, o):
+            dst, src = rounding_views(b, o)
+            nc.vector.tensor_copy(out=dst, in_=src)
 
         def quantize_h(b, o):
             nc.vector.quantize_mx(out=h_words[b, o][:].bitcast(FP8X4), scales=h_scales[b, o][:], in_=h_bf16[b, o][:])
@@ -158,9 +176,9 @@ def tile_picked_yhs_prob_p_kernel(tc, x_words, x_scales, hT, turn, offs, pos1, p
                 stop=(o == PASSES - 1),
             )
 
-        node_halves = [slice(n * S // 2, (n + 1) * S // 2) for n in range(2)]
-        first_accs = [in_bank([P, S // 2], "first_acc%d" % n, n) for n in range(2)]
-        acc_banks = {1: 6, 2: 5, 3: 2}
+        node_parts = [slice(0, S // 2), slice(S // 2, S)]
+        first_accs = [in_bank([P, part.stop - part.start], "first_acc%d" % n, n) for n, part in enumerate(node_parts)]
+        acc_banks = {1: 6, 2: 7, 3: 4}
         accs = {b: in_bank([P, S], "acc%d" % b, bank) for b, bank in acc_banks.items()}
         ys = [placed([P, S], F32, "y%d" % b, RAW_LATE if b == 1 else None) for b in range(BANDS)]
 
@@ -170,36 +188,35 @@ def tile_picked_yhs_prob_p_kernel(tc, x_words, x_scales, hT, turn, offs, pos1, p
         def empty(b):
             nc.vector.tensor_copy(out=ys[b][:], in_=accs[b][:])
 
-        sigmoid_start = {(0, 3): FOURTH, (1, 3): FOURTH + KIB, (2, 3): CHAIN_1_0 - KIB // 2}
+        sigmoid_start = {(0, 3): FOURTH, (1, 3): FOURTH + KIB}
         sigmoids = {
             (b, d): placed([P, U], F32, "sigmoids%d_%d" % (b, d), sigmoid_start.get((b, d)))[:]
             for b in range(BANDS)
             for d in range(D)
-            if (b, d) < (LAST, 2)
         }
-        closing = placed([P, 2, U], F32, "closing", CHAIN_1_0 + KIB // 2)
-        for d in range(2, D):
-            sigmoids[LAST, d] = closing[:, d - 2, :]
 
-        flip_banks = ((2, 3, 4), (5, 4, 2), (5, 4, 2), (5, 4))
+        flip_banks = ((6, 3, 5), (0, 1, 2), (4, 0, 1))
         flipped = {
-            (b, d): in_bank([P, HALVES, P], "flipped%d_%d" % (b, d), bank)
-            for b in range(BANDS)
+            (b, d): in_bank([P, HALVES, P], "flipped%d_%d" % (b, d), bank)[:]
+            for b in range(LAST)
             for d, bank in enumerate(flip_banks[b])
+            if b > 0 or d == LINKS - 1
         }
-        closing_flipped = [in_bank([P, P], "closing_flipped%d" % h, bank) for h, bank in enumerate((2, 5))]
-        back = [in_bank([P, U], "back%d" % b, 3) for b in range(LAST)]
-        closing_back = [in_bank([P, P], "closing_back%d" % h, bank) for h, bank in enumerate((4, 6))]
-        chain_start = {(0, 0): rounded_start[2, 1], (1, 0): CHAIN_1_0}
+        first_span = in_bank([P, D, S], "first_span", 3)
+        flipped[0, 0] = first_span[:, D - 1, 0:U].rearrange("p (h t) -> p h t", h=HALVES)
+        second_span = in_bank([P, D, S], "second_span", 0)
+        flipped[0, 1] = second_span[:, D - 1, 0:U].rearrange("p (h t) -> p h t", h=HALVES)
+        back = [in_bank([P, U], "back%d" % b, bank) for b, bank in enumerate((5, 6, 7))]
+        chain_start = {(0, 0): rounded_start[2, 1], (0, 1): CHAIN_1_0, (1, 0): CHAIN_1_0, (2, 0): CLOSING + KIB // 2, (2, 1): CLOSING + 5 * KIB // 2}
+        centred_start = {0: CLOSING, 1: CLOSING + KIB, 2: CLOSING + 2 * KIB, 3: CLOSING + 3 * KIB}
         chain = {
             (b, d): placed([P, HALVES, P], F32, "chain%d_%d" % (b, d), chain_start.get((b, d)))
-            for b in range(BANDS)
+            for b in range(LAST)
             for d in range(LINKS)
         }
         shifted_start = {0: rounded_start[3, 1], 1: FOURTH, 2: FOURTH + KIB}
-        shifted = [placed([P, U], F32, "shifted%d" % b, shifted_start.get(b)) for b in range(BANDS)]
+        shifted = [placed([P, U], F32, "shifted%d" % b, shifted_start.get(b)) for b in range(LAST)]
         results = [placed([P, U], F32, "result%d" % b) for b in range(BANDS)]
-        base_cols = placed([P, TURN_ROWS], F32, "base_cols", rounded_start[1, 1])
 
         def gather(b, d, words=slice(0, U)):
             offsets = path_lists[d][:, words.start // 16 : words.stop // 16]
@@ -232,27 +249,27 @@ def tile_picked_yhs_prob_p_kernel(tc, x_words, x_scales, hT, turn, offs, pos1, p
             nc.vector.tensor_tensor(results[b][:], shifted[b][:], back[b][:], MULT)
             nc.sync.dma_start(out=out[half(b), :], in_=results[b][:])
 
-        nc.vector.tensor_copy(node_words[0][:], word_table[0][:].indirect(node_list[:]))
-        nc.vector.tensor_copy(node_scales[:], scale_table[:].indirect(node_list[:]))
-        round_h(0, 0)
+        dst, src = rounding_views(0, 0)
+        nc.scalar.copy(out=dst, in_=src)
         quantize_h(0, 0)
         for n in range(2):
-            product(first_accs[n][:], 0, 0, node_halves[n])
-        nc.vector.tensor_copy(node_words[1][:], word_table[1][:].indirect(node_list[:]))
-        round_h(0, 1)
+            product(first_accs[n][:], 0, 0, node_parts[n])
+        dst, src = rounding_views(0, 1)
+        nc.vector.tensor_copy(out=dst[:, 0:VECTOR_RUNS], in_=src[:, 0:VECTOR_RUNS])
+        nc.scalar.copy(out=dst[:, VECTOR_RUNS:RUNS], in_=src[:, VECTOR_RUNS:RUNS])
         quantize_h(0, 1)
         for n in range(2):
-            product(first_accs[n][:], 0, 1, node_halves[n])
-            nc.scalar.copy(out=ys[0][:, node_halves[n]], in_=first_accs[n][:])
+            product(first_accs[n][:], 0, 1, node_parts[n])
+        last_base = placed([P, U], F32, "last_base", RAW_0)
+        nc.scalar.activation(last_base[:], spread[1][:, 1, :], COPY, bias=0.5, scale=-0.5)
+        for n in range(2):
+            nc.scalar.copy(out=ys[0][:, node_parts[n]], in_=first_accs[n][:])
         for o in range(PASSES):
             round_h(1, o)
             quantize_h(1, o)
             multiply(1, o)
         for d in range(D):
             gather(0, d)
-        nc.vector.tensor_scalar(base_cols[:], turned[:, 0:TURN_ROWS], -0.5, 0.5, MULT, ADD)
-        for d in range(LINKS):
-            flip(0, d)
 
         round_h(2, 0)
         round_h(3, 0)
@@ -261,6 +278,7 @@ def tile_picked_yhs_prob_p_kernel(tc, x_words, x_scales, hT, turn, offs, pos1, p
         empty(1)
         for d in range(D):
             gather(1, d)
+        flip(0, 0)
         quantize_h(3, 0)
         round_h(2, 1)
         round_h(3, 1)
@@ -269,52 +287,64 @@ def tile_picked_yhs_prob_p_kernel(tc, x_words, x_scales, hT, turn, offs, pos1, p
         quantize_h(3, 1)
         shift(0)
         link(0, 0)
+        flip(0, 1)
+        flip(0, 2)
         for o in range(PASSES):
             multiply(3, o)
-        link(0, 1)
         empty(2)
-        for d in range(LINKS):
+        for d in range(D):
             gather(2, d)
-        flip(1, 0)
+        link(0, 1)
+        for d in range(LINKS):
+            flip(1, d)
         link(0, 2)
-        flip(1, 1)
         turn_back(0)
         shift(1)
         empty(3)
-        gather(3, 0)
-        gather(3, 1)
-        flip(1, 2)
-        link(1, 0)
-        flip(2, 0)
-        link(1, 1)
-        gather(2, 3)
-        for d in range(2, D):
-            for h in range(HALVES):
+        gather(LAST, 0)
+        gather(LAST, 1)
+        for h in range(HALVES):
+            for d in range(2, D):
                 gather(LAST, d, half(h))
+        flip(2, 0)
+        link(1, 0)
         flip(2, 1)
+        link(1, 1)
+        flip(2, 2)
         finish(0)
         link(1, 2)
         turn_back(1)
-        flip(2, 2)
         link(2, 0)
-        flip(3, 0)
         link(2, 1)
-        flip(3, 1)
         finish(1)
         link(2, 2)
         shift(2)
         turn_back(2)
-        link(3, 0)
-        link(3, 1)
-        for h in range(HALVES):
-            nc.tensor.transpose(closing_flipped[h][:], sigmoids[LAST, 2][:, half(h)], identity[:])
-        link_half(LAST, 2, 0, closing_flipped[0][:])
+
+        centred = [placed([P, U], F32, "centred%d" % d, centred_start.get(d)) for d in range(D)]
+        so_far = [placed([P, U], F32, "so_far%d" % d) for d in range(D - 1)]
+
+        def centre(d, words):
+            nc.vector.scalar_tensor_tensor(
+                centred[d][:, words], sigmoids[LAST, d][:, words], -0.5, turns[d][:, words], ADD, MULT
+            )
+
+        def extend(target, d, words):
+            nc.vector.scalar_tensor_tensor(target[:, words], centred[d][:, words], 0.5, so_far[d - 1][:, words], ADD, MULT)
+
+        every = slice(0, U)
+        centre(0, every)
         finish(2)
-        link_half(LAST, 2, 1, closing_flipped[1][:])
-        for h in range(HALVES):
-            nc.tensor.transpose(closing_back[h][:], chain[LAST, 2][:, h, :], identity[:])
-        for h in range(HALVES):
-            nc.vector.tensor_tensor(shifted[LAST][:, half(h)], sigmoids[LAST, 3][:, half(h)], last_base[:, half(h)], SUBTRACT)
-        for h in range(HALVES):
-            nc.vector.tensor_tensor(results[LAST][:, half(h)], shifted[LAST][:, half(h)], closing_back[h][:], MULT)
-            nc.sync.dma_start(out=out[half(LAST), half(h)], in_=results[LAST][:, half(h)])
+        nc.vector.tensor_scalar_add(so_far[0][:], centred[0][:], 0.5)
+        centre(1, every)
+        extend(so_far[1], 1, every)
+        centre(2, half(0))
+        centre(3, half(0))
+        extend(so_far[2], 2, half(0))
+        centre(2, half(1))
+        extend(results[LAST], 3, half(0))
+        nc.sync.dma_start(out=out[half(LAST), half(0)], in_=results[LAST][:, half(0)])
+        extend(so_far[2], 2, half(1))
+        centre(3, half(1))
+        extend(results[LAST], 3, half(1))
+        nc.sync.dma_start(out=out[half(LAST), half(1)], in_=results[LAST][:, half(1)])

@@ -40,6 +40,7 @@ FOURTH = 20 * KIB
 CLOSING = 24 * KIB
 WORDS_0 = 32 * KIB
 RAW_0 = 44 * KIB
+RAW_LAST = 48 * KIB
 VECTOR_RUNS = 20
 RUNS = P // RUN
 SCALES = WORDS_0 + 8 * KIB + KIB // 2
@@ -70,7 +71,7 @@ def tile_picked_yhs_prob_p_kernel(tc, x_words, x_scales, hT, turn, offs, pos1, p
         identity = keep.tile([P, P], F32, name="identity")
         turn_rows = keep.tile([P, P], F32, name="turn_rows")
         h_raw = {(b, o): placed([P, PACK, P], F32, "h_raw%d_%d" % (b, o), RAW_0 if (b, o) == (0, 0) else None)[:] for b in range(2) for o in range(PASSES)}
-        late_raw = [placed([P, PACK, 2 * P], F32, "late_raw0", RAW_LATE), placed([P, PACK, 2 * P], F32, "late_raw1")]
+        late_raw = [placed([P, PACK, 2 * P], F32, "late_raw0", RAW_LATE), placed([P, PACK, 2 * P], F32, "late_raw1", RAW_LAST)]
         for o in range(PASSES):
             for b in range(2, BANDS):
                 h_raw[b, o] = late_raw[o][:, :, half(b - 2)]
@@ -120,17 +121,16 @@ def tile_picked_yhs_prob_p_kernel(tc, x_words, x_scales, hT, turn, offs, pos1, p
         nc.vector.tensor_copy(node_scales[:], scale_table[:].indirect(node_list[:]))
         nc.vector.tensor_copy(node_words[1][:], word_table[1][:].indirect(node_list[:]))
 
-        turned = in_bank([P, P], "turned", 7)[:]
+        turned_span = in_bank([P, LINKS, S], "turned_span", 2)
+        turned = turned_span[:, 0, 0:P]
         nc.tensor.transpose(turned, turn_rows[:], identity[:])
         turn_cols = placed([P, TURN_ROWS], F32, "turn_cols")
         nc.scalar.copy(out=turn_cols[:], in_=turned[:, 0:TURN_ROWS])
-        base_cols = keep.tile([P, TURN_ROWS], F32, name="base_cols")
-        nc.scalar.activation(base_cols[:], turned[:, 0:TURN_ROWS], COPY, bias=0.5, scale=-0.5)
         pair_cols = keep.tile([P, 2 * HALVES], F32, name="pair_cols")
         nc.gpsimd.tensor_tensor(pair_cols[:], turn_cols[:, 0 : 2 * HALVES], turn_cols[:, 2 * HALVES : TURN_ROWS], MULT)
         sign_cols = keep.tile([P, HALVES], F32, name="sign_cols")
         nc.gpsimd.tensor_tensor(sign_cols[:], pair_cols[:, 0:HALVES], pair_cols[:, HALVES : 2 * HALVES], MULT)
-        spread = [in_bank([P, 2, U], "spread%d" % pair, 4 + pair)[:] for pair in range(D // 2)]
+        spread = [in_bank([P, 2, U], "spread%d" % pair, 6 + pair)[:] for pair in range(D // 2)]
         turn_pairs = [keep.tile([P, 2, U], F32, name="turn_pair%d" % pair) for pair in range(D // 2)]
         for pair in range(D // 2):
             flat = spread[pair].rearrange("p d u -> p (d u)")
@@ -138,14 +138,16 @@ def tile_picked_yhs_prob_p_kernel(tc, x_words, x_scales, hT, turn, offs, pos1, p
                 col = 2 * HALVES * pair + n
                 nc.tensor.transpose(flat[:, half(n)], turn_cols[:, col : col + 1].to_broadcast([P, P]), identity[:])
             nc.scalar.copy(out=turn_pairs[pair][:], in_=spread[pair])
+        bases = placed([P, 2, U], F32, "bases")
+        nc.gpsimd.tensor_scalar(bases[:], turn_pairs[1][:], -0.5, 0.5, MULT, ADD)
         turns = [turn_pairs[d // 2][:, d % 2, :] for d in range(D)]
 
 
-        pieces = [(1, 0), (1, 1), (2, 0), (3, 0), (2, 1), (3, 1)]
-        rounded_start = {piece: WORDS_1 + n * KIB for n, piece in enumerate(pieces)}
+        halves_in = {(1, 0): 0, (1, 1): 2, (2, 0): 6, (3, 0): 7, (2, 1): 9, (3, 1): 11}
+        rounded_start = {piece: WORDS_1 + n * KIB // 2 for piece, n in halves_in.items()}
         rounded_start[0, 0] = None
         rounded_start[0, 1] = WORDS_1 + 7 * KIB
-        words_start = {(0, 0): WORDS_1 + 6 * KIB}
+        words_start = {(3, 0): RAW_LAST, (0, 0): WORDS_1 + 13 * KIB // 2}
         h_bf16, h_words, h_scales = {}, {}, {}
         for (b, o), start in rounded_start.items():
             h_bf16[b, o] = placed([P, P * PACK], BF16, "h_bf16_%d_%d" % (b, o), start)
@@ -178,9 +180,9 @@ def tile_picked_yhs_prob_p_kernel(tc, x_words, x_scales, hT, turn, offs, pos1, p
 
         node_parts = [slice(0, S // 2), slice(S // 2, S)]
         first_accs = [in_bank([P, part.stop - part.start], "first_acc%d" % n, n) for n, part in enumerate(node_parts)]
-        acc_banks = {1: 6, 2: 7, 3: 4}
+        acc_banks = {1: 6, 2: 7, 3: 5}
         accs = {b: in_bank([P, S], "acc%d" % b, bank) for b, bank in acc_banks.items()}
-        ys = [placed([P, S], F32, "y%d" % b, RAW_LATE if b == 1 else None) for b in range(BANDS)]
+        ys = [placed([P, S], F32, "y%d" % b, WORDS_1 + 3 * KIB // 2 if b == 1 else None) for b in range(BANDS)]
 
         def multiply(b, o):
             product(accs[b][:], b, o, slice(0, S))
@@ -188,34 +190,32 @@ def tile_picked_yhs_prob_p_kernel(tc, x_words, x_scales, hT, turn, offs, pos1, p
         def empty(b):
             nc.vector.tensor_copy(out=ys[b][:], in_=accs[b][:])
 
-        sigmoid_start = {(0, 3): FOURTH, (1, 3): FOURTH + KIB}
-        sigmoids = {
-            (b, d): placed([P, U], F32, "sigmoids%d_%d" % (b, d), sigmoid_start.get((b, d)))[:]
-            for b in range(BANDS)
-            for d in range(D)
+        sigmoid_pairs = {
+            (b, pair): placed([P, 2, U], F32, "sigmoids%d_%d" % (b, pair)) for b in range(BANDS) for pair in range(D // 2)
         }
+        sigmoids = {(b, d): sigmoid_pairs[b, d // 2][:, d % 2, :] for b in range(BANDS) for d in range(D)}
+        links = (2, 2, 3)
 
-        flip_banks = ((6, 3, 5), (0, 1, 2), (4, 0, 1))
+        flip_banks = ((2, 3), (1, 0), (5, 1, 0))
         flipped = {
             (b, d): in_bank([P, HALVES, P], "flipped%d_%d" % (b, d), bank)[:]
             for b in range(LAST)
             for d, bank in enumerate(flip_banks[b])
-            if b > 0 or d == LINKS - 1
+            if (b, d) != (0, 0)
         }
-        first_span = in_bank([P, D, S], "first_span", 3)
-        flipped[0, 0] = first_span[:, D - 1, 0:U].rearrange("p (h t) -> p h t", h=HALVES)
-        second_span = in_bank([P, D, S], "second_span", 0)
-        flipped[0, 1] = second_span[:, D - 1, 0:U].rearrange("p (h t) -> p h t", h=HALVES)
-        back = [in_bank([P, U], "back%d" % b, bank) for b, bank in enumerate((5, 6, 7))]
-        chain_start = {(0, 0): rounded_start[2, 1], (0, 1): CHAIN_1_0, (1, 0): CHAIN_1_0, (2, 0): CLOSING + KIB // 2, (2, 1): CLOSING + 5 * KIB // 2}
+        first_span = in_bank([P, LINKS, S], "first_span", 0)
+        flipped[0, 0] = first_span[:, LINKS - 1, 0:U].rearrange("p (h t) -> p h t", h=HALVES)
+        base_cols = placed([P, TURN_ROWS], F32, "base_cols", rounded_start[1, 1])
+        back = [in_bank([P, U], "back%d" % b, bank) for b, bank in enumerate((2, 7, 3))]
+        chain_start = {(0, 0): rounded_start[2, 1], (1, 0): rounded_start[2, 1], (2, 0): CLOSING + KIB // 2, (2, 1): CLOSING + 5 * KIB // 2}
         centred_start = {0: CLOSING, 1: CLOSING + KIB, 2: CLOSING + 2 * KIB, 3: CLOSING + 3 * KIB}
         chain = {
             (b, d): placed([P, HALVES, P], F32, "chain%d_%d" % (b, d), chain_start.get((b, d)))
             for b in range(LAST)
-            for d in range(LINKS)
+            for d in range(links[b])
         }
-        shifted_start = {0: rounded_start[3, 1], 1: FOURTH, 2: FOURTH + KIB}
-        shifted = [placed([P, U], F32, "shifted%d" % b, shifted_start.get(b)) for b in range(LAST)]
+        shifted_pairs = [placed([P, 2, U], F32, "shifted_pair%d" % b, rounded_start[3, 1]) for b in range(2)]
+        shifted = [placed([P, U], F32, "shifted%d" % b, rounded_start[3, 1] if b == 2 else None) for b in range(LAST)]
         results = [placed([P, U], F32, "result%d" % b) for b in range(BANDS)]
 
         def gather(b, d, words=slice(0, U)):
@@ -240,10 +240,14 @@ def tile_picked_yhs_prob_p_kernel(tc, x_words, x_scales, hT, turn, offs, pos1, p
 
         def turn_back(b):
             for h in range(HALVES):
-                nc.tensor.transpose(back[b][:, half(h)], chain[b, LINKS - 1][:, h, :], identity[:])
+                nc.tensor.transpose(back[b][:, half(h)], chain[b, links[b] - 1][:, h, :], identity[:])
 
         def shift(b):
-            nc.gpsimd.tensor_tensor(shifted[b][:], sigmoids[b, D - 1], last_base[:], SUBTRACT)
+            if links[b] == LINKS:
+                nc.gpsimd.tensor_tensor(shifted[b][:], sigmoids[b, D - 1], bases[:, 1, :], SUBTRACT)
+            else:
+                nc.gpsimd.tensor_tensor(shifted_pairs[b][:], sigmoid_pairs[b, 1][:], bases[:], SUBTRACT)
+                nc.gpsimd.tensor_tensor(shifted[b][:], shifted_pairs[b][:, 0, :], shifted_pairs[b][:, 1, :], MULT)
 
         def finish(b):
             nc.vector.tensor_tensor(results[b][:], shifted[b][:], back[b][:], MULT)
@@ -260,44 +264,48 @@ def tile_picked_yhs_prob_p_kernel(tc, x_words, x_scales, hT, turn, offs, pos1, p
         quantize_h(0, 1)
         for n in range(2):
             product(first_accs[n][:], 0, 1, node_parts[n])
-        last_base = placed([P, U], F32, "last_base", RAW_0)
-        nc.scalar.activation(last_base[:], spread[1][:, 1, :], COPY, bias=0.5, scale=-0.5)
-        for n in range(2):
-            nc.scalar.copy(out=ys[0][:, node_parts[n]], in_=first_accs[n][:])
+
+        nc.scalar.copy(out=ys[0][:, node_parts[0]], in_=first_accs[0][:])
+        nc.vector.tensor_copy(out=ys[0][:, node_parts[1]], in_=first_accs[1][:])
         for o in range(PASSES):
             round_h(1, o)
             quantize_h(1, o)
             multiply(1, o)
         for d in range(D):
             gather(0, d)
+        nc.vector.tensor_scalar(base_cols[:], turned[:, 0:TURN_ROWS], -0.5, 0.5, MULT, ADD)
+        for d in range(links[0]):
+            flip(0, d)
 
         round_h(2, 0)
-        round_h(3, 0)
         quantize_h(2, 0)
         multiply(2, 0)
+        nc.gpsimd.tensor_scalar(
+            h_bf16[LAST, 0][:].rearrange("p (t j) -> p t j", j=PACK),
+            h_raw[LAST, 0].rearrange("p j t -> p t j"),
+            1.0,
+            0.0,
+            MULT,
+            ADD,
+        )
         empty(1)
         for d in range(D):
             gather(1, d)
-        flip(0, 0)
-        quantize_h(3, 0)
         round_h(2, 1)
         round_h(3, 1)
         quantize_h(2, 1)
         multiply(2, 1)
-        quantize_h(3, 1)
+        for o in range(PASSES):
+            quantize_h(3, o)
+            multiply(3, o)
         shift(0)
         link(0, 0)
-        flip(0, 1)
-        flip(0, 2)
-        for o in range(PASSES):
-            multiply(3, o)
+        flip(1, 0)
+        flip(1, 1)
         empty(2)
         for d in range(D):
             gather(2, d)
         link(0, 1)
-        for d in range(LINKS):
-            flip(1, d)
-        link(0, 2)
         turn_back(0)
         shift(1)
         empty(3)
@@ -310,10 +318,9 @@ def tile_picked_yhs_prob_p_kernel(tc, x_words, x_scales, hT, turn, offs, pos1, p
         link(1, 0)
         flip(2, 1)
         link(1, 1)
+        turn_back(1)
         flip(2, 2)
         finish(0)
-        link(1, 2)
-        turn_back(1)
         link(2, 0)
         link(2, 1)
         finish(1)

@@ -40,6 +40,7 @@ FOURTH = 20 * KIB
 CLOSING = 24 * KIB
 WORDS_0 = 32 * KIB
 RAW_0 = 44 * KIB
+TURN_3 = 52 * KIB
 RAW_LAST = 48 * KIB
 VECTOR_RUNS = 20
 RUNS = P // RUN
@@ -131,23 +132,23 @@ def tile_picked_yhs_prob_p_kernel(tc, x_words, x_scales, hT, turn, offs, pos1, p
         sign_cols = keep.tile([P, HALVES], F32, name="sign_cols")
         nc.gpsimd.tensor_tensor(sign_cols[:], pair_cols[:, 0:HALVES], pair_cols[:, HALVES : 2 * HALVES], MULT)
         spread = [in_bank([P, 2, U], "spread%d" % pair, 6 + pair)[:] for pair in range(D // 2)]
-        turn_pairs = [keep.tile([P, 2, U], F32, name="turn_pair%d" % pair) for pair in range(D // 2)]
+        first_turns = keep.tile([P, 2, U], F32, name="first_turns")
+        turns = [first_turns[:, 0, :], first_turns[:, 1, :], placed([P, U], F32, "turn2")[:], placed([P, U], F32, "turn3", TURN_3)[:]]
         for pair in range(D // 2):
             flat = spread[pair].rearrange("p d u -> p (d u)")
             for n in range(2 * HALVES):
                 col = 2 * HALVES * pair + n
                 nc.tensor.transpose(flat[:, half(n)], turn_cols[:, col : col + 1].to_broadcast([P, P]), identity[:])
-            nc.scalar.copy(out=turn_pairs[pair][:], in_=spread[pair])
-        bases = placed([P, 2, U], F32, "bases")
-        nc.gpsimd.tensor_scalar(bases[:], turn_pairs[1][:], -0.5, 0.5, MULT, ADD)
-        turns = [turn_pairs[d // 2][:, d % 2, :] for d in range(D)]
+        nc.scalar.copy(out=first_turns[:], in_=spread[0])
+        for d in range(2, D):
+            nc.scalar.copy(out=turns[d], in_=spread[1][:, d - 2, :])
 
 
         halves_in = {(1, 0): 0, (1, 1): 2, (2, 0): 6, (3, 0): 7, (2, 1): 9, (3, 1): 11}
         rounded_start = {piece: WORDS_1 + n * KIB // 2 for piece, n in halves_in.items()}
         rounded_start[0, 0] = None
         rounded_start[0, 1] = WORDS_1 + 7 * KIB
-        words_start = {(3, 0): RAW_LAST, (0, 0): WORDS_1 + 13 * KIB // 2}
+        words_start = {(0, 1): rounded_start[1, 1], (3, 0): RAW_LAST, (0, 0): WORDS_1 + 13 * KIB // 2}
         h_bf16, h_words, h_scales = {}, {}, {}
         for (b, o), start in rounded_start.items():
             h_bf16[b, o] = placed([P, P * PACK], BF16, "h_bf16_%d_%d" % (b, o), start)
@@ -191,12 +192,12 @@ def tile_picked_yhs_prob_p_kernel(tc, x_words, x_scales, hT, turn, offs, pos1, p
             nc.vector.tensor_copy(out=ys[b][:], in_=accs[b][:])
 
         sigmoid_pairs = {
-            (b, pair): placed([P, 2, U], F32, "sigmoids%d_%d" % (b, pair)) for b in range(BANDS) for pair in range(D // 2)
+            (b, pair): placed([P, 2, U], F32, "sigmoids%d_%d" % (b, pair), FOURTH if (b, pair) == (1, 1) else None) for b in range(BANDS) for pair in range(D // 2)
         }
         sigmoids = {(b, d): sigmoid_pairs[b, d // 2][:, d % 2, :] for b in range(BANDS) for d in range(D)}
-        links = (2, 2, 3)
+        links = (2, 3, 3)
 
-        flip_banks = ((2, 3), (1, 0), (5, 1, 0))
+        flip_banks = ((2, 3), (1, 0, 3), (5, 1, 0))
         flipped = {
             (b, d): in_bank([P, HALVES, P], "flipped%d_%d" % (b, d), bank)[:]
             for b in range(LAST)
@@ -206,17 +207,19 @@ def tile_picked_yhs_prob_p_kernel(tc, x_words, x_scales, hT, turn, offs, pos1, p
         first_span = in_bank([P, LINKS, S], "first_span", 0)
         flipped[0, 0] = first_span[:, LINKS - 1, 0:U].rearrange("p (h t) -> p h t", h=HALVES)
         base_cols = placed([P, TURN_ROWS], F32, "base_cols", rounded_start[1, 1])
-        back = [in_bank([P, U], "back%d" % b, bank) for b, bank in enumerate((2, 7, 3))]
-        chain_start = {(0, 0): rounded_start[2, 1], (1, 0): rounded_start[2, 1], (2, 0): CLOSING + KIB // 2, (2, 1): CLOSING + 5 * KIB // 2}
-        centred_start = {0: CLOSING, 1: CLOSING + KIB, 2: CLOSING + 2 * KIB, 3: CLOSING + 3 * KIB}
+        back = [in_bank([P, U], "back%d" % b, bank) for b, bank in enumerate((2, 7, 6))]
+        chain_start = {(0, 0): rounded_start[2, 1], (1, 0): rounded_start[2, 1], (1, 1): CHAIN_1_0, (2, 0): CLOSING + KIB, (2, 1): CLOSING + 4 * KIB}
+        result_start = {0: CHAIN_1_0, 1: CLOSING + KIB // 2}
         chain = {
             (b, d): placed([P, HALVES, P], F32, "chain%d_%d" % (b, d), chain_start.get((b, d)))
             for b in range(LAST)
             for d in range(links[b])
         }
-        shifted_pairs = [placed([P, 2, U], F32, "shifted_pair%d" % b, rounded_start[3, 1]) for b in range(2)]
-        shifted = [placed([P, U], F32, "shifted%d" % b, rounded_start[3, 1] if b == 2 else None) for b in range(LAST)]
-        results = [placed([P, U], F32, "result%d" % b) for b in range(BANDS)]
+        shifted_pairs = [placed([P, 2, U], F32, "shifted_pair%d" % b, rounded_start[3, 1]) for b in range(1)]
+        shifted_start = {1: TURN_3, 2: FOURTH + KIB}
+        shifted = [placed([P, U], F32, "shifted%d" % b, shifted_start.get(b)) for b in range(LAST)]
+        signed = placed([P, U], F32, "signed", rounded_start[3, 1])
+        results = [placed([P, U], F32, "result%d" % b, result_start.get(b)) for b in range(BANDS)]
 
         def gather(b, d, words=slice(0, U)):
             offsets = path_lists[d][:, words.start // 16 : words.stop // 16]
@@ -265,6 +268,8 @@ def tile_picked_yhs_prob_p_kernel(tc, x_words, x_scales, hT, turn, offs, pos1, p
         for n in range(2):
             product(first_accs[n][:], 0, 1, node_parts[n])
 
+        bases = placed([P, 2, U], F32, "bases", RAW_0)
+        nc.scalar.activation(bases[:], spread[1], COPY, bias=0.5, scale=-0.5)
         nc.scalar.copy(out=ys[0][:, node_parts[0]], in_=first_accs[0][:])
         nc.vector.tensor_copy(out=ys[0][:, node_parts[1]], in_=first_accs[1][:])
         for o in range(PASSES):
@@ -306,20 +311,23 @@ def tile_picked_yhs_prob_p_kernel(tc, x_words, x_scales, hT, turn, offs, pos1, p
         for d in range(D):
             gather(2, d)
         link(0, 1)
+        flip(1, 2)
         turn_back(0)
-        shift(1)
         empty(3)
+        flip(2, 0)
+        link(1, 0)
+        nc.vector.tensor_tensor(signed[:], ys[LAST][:].indirect(path_lists[D - 1][:]), turns[D - 1], MULT)
+        nc.scalar.activation(sigmoids[LAST, D - 1], signed[:], SIGMOID)
         gather(LAST, 0)
         gather(LAST, 1)
         for h in range(HALVES):
-            for d in range(2, D):
-                gather(LAST, d, half(h))
-        flip(2, 0)
-        link(1, 0)
+            gather(LAST, 2, half(h))
+        shift(1)
         flip(2, 1)
         link(1, 1)
-        turn_back(1)
         flip(2, 2)
+        link(1, 2)
+        turn_back(1)
         finish(0)
         link(2, 0)
         link(2, 1)
@@ -328,8 +336,10 @@ def tile_picked_yhs_prob_p_kernel(tc, x_words, x_scales, hT, turn, offs, pos1, p
         shift(2)
         turn_back(2)
 
-        centred = [placed([P, U], F32, "centred%d" % d, centred_start.get(d)) for d in range(D)]
-        so_far = [placed([P, U], F32, "so_far%d" % d) for d in range(D - 1)]
+        centred_pair = placed([P, 2, U], F32, "centred_pair", CLOSING + 3 * KIB // 2)
+        centred = [centred_pair[:, 0, :], centred_pair[:, 1, :], placed([P, U], F32, "centred2", CLOSING + 4 * KIB)[:]]
+        so_far = [placed([P, U], F32, "so_far%d" % d)[:] for d in range(2)]
+        before = [sigmoids[LAST, D - 1]] + so_far
 
         def centre(d, words):
             nc.vector.scalar_tensor_tensor(
@@ -337,21 +347,16 @@ def tile_picked_yhs_prob_p_kernel(tc, x_words, x_scales, hT, turn, offs, pos1, p
             )
 
         def extend(target, d, words):
-            nc.vector.scalar_tensor_tensor(target[:, words], centred[d][:, words], 0.5, so_far[d - 1][:, words], ADD, MULT)
+            nc.vector.scalar_tensor_tensor(target[:, words], centred[d][:, words], 0.5, before[d][:, words], ADD, MULT)
 
         every = slice(0, U)
         centre(0, every)
         finish(2)
-        nc.vector.tensor_scalar_add(so_far[0][:], centred[0][:], 0.5)
+        extend(so_far[0], 0, every)
         centre(1, every)
         extend(so_far[1], 1, every)
-        centre(2, half(0))
-        centre(3, half(0))
-        extend(so_far[2], 2, half(0))
-        centre(2, half(1))
-        extend(results[LAST], 3, half(0))
-        nc.sync.dma_start(out=out[half(LAST), half(0)], in_=results[LAST][:, half(0)])
-        extend(so_far[2], 2, half(1))
-        centre(3, half(1))
-        extend(results[LAST], 3, half(1))
-        nc.sync.dma_start(out=out[half(LAST), half(1)], in_=results[LAST][:, half(1)])
+        for h in range(HALVES):
+            centre(2, half(h))
+        for h in range(HALVES):
+            extend(results[LAST], 2, half(h))
+            nc.sync.dma_start(out=out[half(LAST), half(h)], in_=results[LAST][:, half(h)])

@@ -40,6 +40,7 @@ FOURTH = 20 * KIB
 CLOSING = 24 * KIB
 WORDS_0 = 32 * KIB
 RAW_0 = 44 * KIB
+PAIR_0 = 56 * KIB
 TURN_3 = 52 * KIB
 RAW_LAST = 48 * KIB
 VECTOR_RUNS = 20
@@ -90,18 +91,18 @@ def tile_picked_yhs_prob_p_kernel(tc, x_words, x_scales, hT, turn, offs, pos1, p
 
         nc.vector.memset(scale_table[:].bitcast(I32), 0)
         nc.gpsimd.memset(turn_rows[:], 0.0)
+        load_words(0)
         nc.sync.dma_start(node_list[:], offs)
         for q in range(QUADRANTS):
             nc.sync.dma_start(
                 out=scale_table[32 * q : 32 * q + SCALE_ROWS * PASSES, :].bitcast(I32),
                 in_=x_scales[:, SCALE_ROWS * q : SCALE_ROWS * (q + 1), :].bitcast(I32),
             )
-        load_words(0)
-        load_path(0)
         nc.sync.dma_start(out=turn_rows[0:TURN_ROWS, :], in_=turn[:, 0, :].rearrange("d (h c) -> d h c", c=P))
         load_words(1)
         for o in range(PASSES):
             load_h(h_raw[0, o], o, half(0))
+        load_path(0)
         for o in range(PASSES):
             load_h(h_raw[1, o], o, half(1))
         load_path(1)
@@ -122,24 +123,23 @@ def tile_picked_yhs_prob_p_kernel(tc, x_words, x_scales, hT, turn, offs, pos1, p
         nc.vector.tensor_copy(node_scales[:], scale_table[:].indirect(node_list[:]))
         nc.vector.tensor_copy(node_words[1][:], word_table[1][:].indirect(node_list[:]))
 
-        turned_span = in_bank([P, LINKS, S], "turned_span", 2)
-        turned = turned_span[:, 0, 0:P]
+        turned = in_bank([P, P], "turned", 2)[:]
         nc.tensor.transpose(turned, turn_rows[:], identity[:])
         turn_cols = placed([P, TURN_ROWS], F32, "turn_cols")
         nc.scalar.copy(out=turn_cols[:], in_=turned[:, 0:TURN_ROWS])
+        base_cols = keep.tile([P, TURN_ROWS], F32, name="base_cols")
+        nc.scalar.activation(base_cols[:], turned[:, 0:TURN_ROWS], COPY, bias=0.5, scale=-0.5)
         pair_cols = keep.tile([P, 2 * HALVES], F32, name="pair_cols")
         nc.gpsimd.tensor_tensor(pair_cols[:], turn_cols[:, 0 : 2 * HALVES], turn_cols[:, 2 * HALVES : TURN_ROWS], MULT)
         sign_cols = keep.tile([P, HALVES], F32, name="sign_cols")
         nc.gpsimd.tensor_tensor(sign_cols[:], pair_cols[:, 0:HALVES], pair_cols[:, HALVES : 2 * HALVES], MULT)
         spread = [in_bank([P, 2, U], "spread%d" % pair, 6 + pair)[:] for pair in range(D // 2)]
-        first_turns = keep.tile([P, 2, U], F32, name="first_turns")
-        turns = [first_turns[:, 0, :], first_turns[:, 1, :], placed([P, U], F32, "turn2")[:], placed([P, U], F32, "turn3", TURN_3)[:]]
+        turns = [spread[0][:, 0, :], spread[0][:, 1, :], placed([P, U], F32, "turn2")[:], placed([P, U], F32, "turn3", TURN_3)[:]]
         for pair in range(D // 2):
             flat = spread[pair].rearrange("p d u -> p (d u)")
             for n in range(2 * HALVES):
                 col = 2 * HALVES * pair + n
                 nc.tensor.transpose(flat[:, half(n)], turn_cols[:, col : col + 1].to_broadcast([P, P]), identity[:])
-        nc.scalar.copy(out=first_turns[:], in_=spread[0])
         for d in range(2, D):
             nc.scalar.copy(out=turns[d], in_=spread[1][:, d - 2, :])
 
@@ -181,18 +181,21 @@ def tile_picked_yhs_prob_p_kernel(tc, x_words, x_scales, hT, turn, offs, pos1, p
 
         node_parts = [slice(0, S // 2), slice(S // 2, S)]
         first_accs = [in_bank([P, part.stop - part.start], "first_acc%d" % n, n) for n, part in enumerate(node_parts)]
-        acc_banks = {1: 6, 2: 7, 3: 5}
-        accs = {b: in_bank([P, S], "acc%d" % b, bank) for b, bank in acc_banks.items()}
+        accs = {
+            1: in_bank([P, LINKS, S], "acc1", 2)[:, LINKS - 1, :],
+            2: in_bank([P, S], "acc2", 7)[:],
+            3: in_bank([P, S], "acc3", 5)[:],
+        }
         ys = [placed([P, S], F32, "y%d" % b, WORDS_1 + 3 * KIB // 2 if b == 1 else None) for b in range(BANDS)]
 
         def multiply(b, o):
-            product(accs[b][:], b, o, slice(0, S))
+            product(accs[b], b, o, slice(0, S))
 
         def empty(b):
-            nc.vector.tensor_copy(out=ys[b][:], in_=accs[b][:])
+            nc.vector.tensor_copy(out=ys[b][:], in_=accs[b])
 
         sigmoid_pairs = {
-            (b, pair): placed([P, 2, U], F32, "sigmoids%d_%d" % (b, pair), FOURTH if (b, pair) == (1, 1) else None) for b in range(BANDS) for pair in range(D // 2)
+            (b, pair): placed([P, 2, U], F32, "sigmoids%d_%d" % (b, pair), {(0, 1): PAIR_0, (1, 1): FOURTH}.get((b, pair))) for b in range(BANDS) for pair in range(D // 2)
         }
         sigmoids = {(b, d): sigmoid_pairs[b, d // 2][:, d % 2, :] for b in range(BANDS) for d in range(D)}
         links = (2, 3, 3)
@@ -206,8 +209,7 @@ def tile_picked_yhs_prob_p_kernel(tc, x_words, x_scales, hT, turn, offs, pos1, p
         }
         first_span = in_bank([P, LINKS, S], "first_span", 0)
         flipped[0, 0] = first_span[:, LINKS - 1, 0:U].rearrange("p (h t) -> p h t", h=HALVES)
-        base_cols = placed([P, TURN_ROWS], F32, "base_cols", rounded_start[1, 1])
-        back = [in_bank([P, U], "back%d" % b, bank) for b, bank in enumerate((2, 7, 6))]
+        back = [in_bank([P, U], "back%d" % b, bank) for b, bank in enumerate((2, 7, 4))]
         chain_start = {(0, 0): rounded_start[2, 1], (1, 0): rounded_start[2, 1], (1, 1): CHAIN_1_0, (2, 0): CLOSING + KIB, (2, 1): CLOSING + 4 * KIB}
         result_start = {0: CHAIN_1_0, 1: CLOSING + KIB // 2}
         chain = {
@@ -216,9 +218,9 @@ def tile_picked_yhs_prob_p_kernel(tc, x_words, x_scales, hT, turn, offs, pos1, p
             for d in range(links[b])
         }
         shifted_pairs = [placed([P, 2, U], F32, "shifted_pair%d" % b, rounded_start[3, 1]) for b in range(1)]
-        shifted_start = {1: TURN_3, 2: FOURTH + KIB}
+        shifted_start = {0: TURN_3, 1: rounded_start[3, 1], 2: FOURTH + KIB}
         shifted = [placed([P, U], F32, "shifted%d" % b, shifted_start.get(b)) for b in range(LAST)]
-        signed = placed([P, U], F32, "signed", rounded_start[3, 1])
+        signed = placed([P, U], F32, "signed", PAIR_0)
         results = [placed([P, U], F32, "result%d" % b, result_start.get(b)) for b in range(BANDS)]
 
         def gather(b, d, words=slice(0, U)):
@@ -250,7 +252,6 @@ def tile_picked_yhs_prob_p_kernel(tc, x_words, x_scales, hT, turn, offs, pos1, p
                 nc.gpsimd.tensor_tensor(shifted[b][:], sigmoids[b, D - 1], bases[:, 1, :], SUBTRACT)
             else:
                 nc.gpsimd.tensor_tensor(shifted_pairs[b][:], sigmoid_pairs[b, 1][:], bases[:], SUBTRACT)
-                nc.gpsimd.tensor_tensor(shifted[b][:], shifted_pairs[b][:, 0, :], shifted_pairs[b][:, 1, :], MULT)
 
         def finish(b):
             nc.vector.tensor_tensor(results[b][:], shifted[b][:], back[b][:], MULT)
@@ -278,9 +279,6 @@ def tile_picked_yhs_prob_p_kernel(tc, x_words, x_scales, hT, turn, offs, pos1, p
             multiply(1, o)
         for d in range(D):
             gather(0, d)
-        nc.vector.tensor_scalar(base_cols[:], turned[:, 0:TURN_ROWS], -0.5, 0.5, MULT, ADD)
-        for d in range(links[0]):
-            flip(0, d)
 
         round_h(2, 0)
         quantize_h(2, 0)
@@ -294,6 +292,8 @@ def tile_picked_yhs_prob_p_kernel(tc, x_words, x_scales, hT, turn, offs, pos1, p
             ADD,
         )
         empty(1)
+        for d in range(links[0]):
+            flip(0, d)
         for d in range(D):
             gather(1, d)
         round_h(2, 1)
@@ -318,6 +318,7 @@ def tile_picked_yhs_prob_p_kernel(tc, x_words, x_scales, hT, turn, offs, pos1, p
         link(1, 0)
         nc.vector.tensor_tensor(signed[:], ys[LAST][:].indirect(path_lists[D - 1][:]), turns[D - 1], MULT)
         nc.scalar.activation(sigmoids[LAST, D - 1], signed[:], SIGMOID)
+        nc.gpsimd.tensor_tensor(shifted[0][:], shifted_pairs[0][:, 0, :], shifted_pairs[0][:, 1, :], MULT)
         gather(LAST, 0)
         gather(LAST, 1)
         for h in range(HALVES):

@@ -182,17 +182,28 @@ def tile_picked_yhs_prob_p_kernel(tc, x_words, x_scales, hT, turn, offs, pos1, p
         node_parts = [slice(0, S // 2), slice(S // 2, S)]
         first_accs = [in_bank([P, part.stop - part.start], "first_acc%d" % n, n) for n, part in enumerate(node_parts)]
         accs = {
-            1: in_bank([P, LINKS, S], "acc1", 2)[:, LINKS - 1, :],
-            2: in_bank([P, S], "acc2", 7)[:],
             3: in_bank([P, S], "acc3", 5)[:],
         }
         ys = [placed([P, S], F32, "y%d" % b, WORDS_1 + 3 * KIB // 2 if b == 1 else None) for b in range(BANDS)]
 
+        split_accs = {
+            1: [in_bank([P, S // 2], "acc1_0", 4)[:], in_bank([P, 2, S], "acc1_1", 2)[:, 1, 0 : S // 2]],
+            2: [in_bank([P, S // 2], "acc2_%d" % n, bank)[:] for n, bank in enumerate((0, 7))],
+        }
+
         def multiply(b, o):
-            product(accs[b], b, o, slice(0, S))
+            if b in split_accs:
+                for n in range(2):
+                    product(split_accs[b][n], b, o, node_parts[n])
+            else:
+                product(accs[b], b, o, slice(0, S))
 
         def empty(b):
-            nc.vector.tensor_copy(out=ys[b][:], in_=accs[b])
+            if b in split_accs:
+                for n in range(2):
+                    nc.vector.tensor_copy(out=ys[b][:, node_parts[n]], in_=split_accs[b][n])
+            else:
+                nc.vector.tensor_copy(out=ys[b][:], in_=accs[b])
 
         sigmoid_pairs = {
             (b, pair): placed([P, 2, U], F32, "sigmoids%d_%d" % (b, pair), {(0, 1): PAIR_0, (1, 1): FOURTH}.get((b, pair))) for b in range(BANDS) for pair in range(D // 2)
@@ -207,8 +218,8 @@ def tile_picked_yhs_prob_p_kernel(tc, x_words, x_scales, hT, turn, offs, pos1, p
             for d, bank in enumerate(flip_banks[b])
             if (b, d) != (0, 0)
         }
-        first_span = in_bank([P, LINKS, S], "first_span", 0)
-        flipped[0, 0] = first_span[:, LINKS - 1, 0:U].rearrange("p (h t) -> p h t", h=HALVES)
+        first_span = in_bank([P, 2, S], "first_span", 1)
+        flipped[0, 0] = first_span[:, 1, 0:U].rearrange("p (h t) -> p h t", h=HALVES)
         back = [in_bank([P, U], "back%d" % b, bank) for b, bank in enumerate((2, 7, 4))]
         chain_start = {(0, 0): rounded_start[2, 1], (1, 0): rounded_start[2, 1], (1, 1): CHAIN_1_0, (2, 0): CLOSING + KIB, (2, 1): CLOSING + 4 * KIB}
         result_start = {0: CHAIN_1_0, 1: CLOSING + KIB // 2}
@@ -306,8 +317,8 @@ def tile_picked_yhs_prob_p_kernel(tc, x_words, x_scales, hT, turn, offs, pos1, p
         shift(0)
         link(0, 0)
         flip(1, 0)
-        flip(1, 1)
         empty(2)
+        flip(1, 1)
         for d in range(D):
             gather(2, d)
         link(0, 1)

from contextlib import ExitStack

import concourse.mybir as mybir
from concourse.masks import make_identity

K, T, S, V, U, D = 1024, 2048, 512, 512, 256, 4
FLOPS = 2 * K * V * S

F32 = mybir.dt.float32
BF16 = mybir.dt.bfloat16
I32 = mybir.dt.int32
U32 = mybir.dt.uint32
U16 = mybir.dt.uint16
U8 = mybir.dt.uint8
FP8X4 = mybir.dt.float8_e4m3fn_x4
MULT = mybir.AluOpType.mult
ADD = mybir.AluOpType.add
SUBTRACT = mybir.AluOpType.subtract
COPY = mybir.ActivationFunctionType.Copy
SIGMOID = mybir.ActivationFunctionType.Sigmoid

P = 128
PACK = 4
PASSES = K // (P * PACK)
QUADRANTS = 4
SCALE_ROWS = 4
BANDS = V // P
LAST = BANDS - 1
HALVES = U // P
TURN_ROWS = D * HALVES
LINKS = D - 1
RUN = 4
KIB = 1024
BANK = 2 * KIB

WORDS_1 = 0
RAW_LATE = 12 * KIB
CHAIN_1_0 = 16 * KIB
FOURTH = 20 * KIB
CLOSING = 24 * KIB
WORDS_0 = 32 * KIB
RAW_0 = 44 * KIB
PAIR_0 = 56 * KIB
TURN_3 = 52 * KIB
RAW_LAST = 48 * KIB
VECTOR_RUNS = 20
RUNS = P // RUN
SCALES = WORDS_0 + 8 * KIB + KIB // 2


def tile_picked_yhs_prob_p_kernel(tc, x_words, x_scales, hT, turn, offs, pos1, pos2, pos3, pos4, out):
    nc = tc.nc
    with ExitStack() as ctx:
        keep = ctx.enter_context(tc.tile_pool(name="keep", bufs=1))
        reused = ctx.enter_context(tc.tile_pool(name="reused", bufs=1))
        psum = ctx.enter_context(tc.psum_pool(name="psum", bufs=1))

        def placed(shape, dtype, name, start=None):
            if start is None:
                return keep.tile(shape, dtype, name=name, align_bytes=64)
            return reused.tile(shape, dtype, name=name, offset=start, align_bytes=64)

        def in_bank(shape, name, bank):
            return psum.tile(shape, F32, name=name, offset=bank * BANK)

        def half(n):
            return slice(n * P, (n + 1) * P)

        node_list = keep.tile([P, S // 16], U16, name="node_list")
        path_lists = [keep.tile([P, U // 16], U16, name="path_list%d" % d) for d in range(D)]
        word_table = [placed([P, T], U32, "word_table0", WORDS_0), placed([P, T], U32, "word_table1", WORDS_1)]
        scale_table = placed([P, T], U8, "scale_table", SCALES)
        identity = keep.tile([P, P], F32, name="identity")
        turn_rows = keep.tile([P, P], F32, name="turn_rows")
        h_raw = {(b, o): placed([P, PACK, P], F32, "h_raw%d_%d" % (b, o), RAW_0 if (b, o) == (0, 0) else None)[:] for b in range(2) for o in range(PASSES)}
        late_raw = [placed([P, PACK, 2 * P], F32, "late_raw0", RAW_LATE), placed([P, PACK, 2 * P], F32, "late_raw1", RAW_LAST)]
        for o in range(PASSES):
            for b in range(2, BANDS):
                h_raw[b, o] = late_raw[o][:, :, half(b - 2)]

        def load_words(o):
            words = x_words[o].rearrange("p n r -> p (n r)").bitcast(I32)
            nc.sync.dma_start(out=word_table[o][:].bitcast(I32), in_=words)

        def load_h(target, o, positions):
            rows = hT[o * P * PACK : (o + 1) * P * PACK, positions]
            nc.sync.dma_start(out=target, in_=rows.rearrange("(p j) t -> p j t", j=PACK))

        def load_path(d):
            nc.sync.dma_start(path_lists[d][:], (pos1, pos2, pos3, pos4)[d])

        nc.vector.memset(scale_table[:].bitcast(I32), 0)
        nc.gpsimd.memset(turn_rows[:], 0.0)
        load_words(0)
        nc.sync.dma_start(node_list[:], offs)
        for q in range(QUADRANTS):
            nc.sync.dma_start(
                out=scale_table[32 * q : 32 * q + SCALE_ROWS * PASSES, :].bitcast(I32),
                in_=x_scales[:, SCALE_ROWS * q : SCALE_ROWS * (q + 1), :].bitcast(I32),
            )
        nc.sync.dma_start(out=turn_rows[0:TURN_ROWS, :], in_=turn[:, 0, :].rearrange("d (h c) -> d h c", c=P))
        load_words(1)
        for o in range(PASSES):
            load_h(h_raw[0, o], o, half(0))
        load_path(0)
        for o in range(PASSES):
            load_h(h_raw[1, o], o, half(1))
        load_path(1)
        load_path(2)
        load_h(late_raw[0][:], 0, slice(2 * P, V))
        load_path(3)
        load_h(late_raw[1][:], 1, slice(2 * P, V))

        make_identity(nc, identity[:])
        warm_in = keep.tile([P, 1], F32, name="warm_in")
        warm_up = keep.tile([P, 1], F32, name="warm_up")
        nc.vector.memset(warm_in[:], 0.0)
        nc.scalar.activation(warm_up[:], warm_in[:], SIGMOID)

        node_words = [placed([P, S], U32, "node_words0"), placed([P, S], U32, "node_words1", SCALES)]
        node_scales = placed([P, S], U8, "node_scales")
        nc.vector.tensor_copy(node_words[0][:], word_table[0][:].indirect(node_list[:]))
        nc.vector.tensor_copy(node_scales[:], scale_table[:].indirect(node_list[:]))
        nc.vector.tensor_copy(node_words[1][:], word_table[1][:].indirect(node_list[:]))

        turned = in_bank([P, P], "turned", 2)[:]
        nc.tensor.transpose(turned, turn_rows[:], identity[:])
        turn_cols = placed([P, TURN_ROWS], F32, "turn_cols")
        nc.scalar.copy(out=turn_cols[:], in_=turned[:, 0:TURN_ROWS])
        base_cols = keep.tile([P, TURN_ROWS], F32, name="base_cols")
        nc.scalar.activation(base_cols[:], turned[:, 0:TURN_ROWS], COPY, bias=0.5, scale=-0.5)
        pair_cols = keep.tile([P, 2 * HALVES], F32, name="pair_cols")
        nc.gpsimd.tensor_tensor(pair_cols[:], turn_cols[:, 0 : 2 * HALVES], turn_cols[:, 2 * HALVES : TURN_ROWS], MULT)
        sign_cols = keep.tile([P, HALVES], F32, name="sign_cols")
        nc.gpsimd.tensor_tensor(sign_cols[:], pair_cols[:, 0:HALVES], pair_cols[:, HALVES : 2 * HALVES], MULT)
        spread = [in_bank([P, 2, U], "spread%d" % pair, 6 + pair)[:] for pair in range(D // 2)]
        turns = [spread[0][:, 0, :], spread[0][:, 1, :], placed([P, U], F32, "turn2")[:], placed([P, U], F32, "turn3", TURN_3)[:]]
        for pair in range(D // 2):
            flat = spread[pair].rearrange("p d u -> p (d u)")
            for n in range(2 * HALVES):
                col = 2 * HALVES * pair + n
                nc.tensor.transpose(flat[:, half(n)], turn_cols[:, col : col + 1].to_broadcast([P, P]), identity[:])
        for d in range(2, D):
            nc.scalar.copy(out=turns[d], in_=spread[1][:, d - 2, :])


        halves_in = {(1, 0): 0, (1, 1): 2, (2, 0): 6, (3, 0): 7, (2, 1): 9, (3, 1): 11}
        rounded_start = {piece: WORDS_1 + n * KIB // 2 for piece, n in halves_in.items()}
        rounded_start[0, 0] = None
        rounded_start[0, 1] = WORDS_1 + 7 * KIB
        words_start = {(0, 1): rounded_start[1, 1], (3, 0): RAW_LAST, (0, 0): WORDS_1 + 13 * KIB // 2}
        h_bf16, h_words, h_scales = {}, {}, {}
        for (b, o), start in rounded_start.items():
            h_bf16[b, o] = placed([P, P * PACK], BF16, "h_bf16_%d_%d" % (b, o), start)
            h_words[b, o] = placed([P, P], U32, "h_words%d_%d" % (b, o), words_start.get((b, o)))
            h_scales[b, o] = placed([P, P], U8, "h_scales%d_%d" % (b, o))

        def rounding_views(b, o):
            return (
                h_bf16[b, o][:].rearrange("p (c i j) -> p c j i", i=RUN, j=PACK),
                h_raw[b, o].rearrange("p j (c i) -> p c j i", i=RUN),
            )

        def round_h(b, o):
            dst, src = rounding_views(b, o)
            nc.vector.tensor_copy(out=dst, in_=src)

        def quantize_h(b, o):
            nc.vector.quantize_mx(out=h_words[b, o][:].bitcast(FP8X4), scales=h_scales[b, o][:], in_=h_bf16[b, o][:])

        def product(acc, b, o, cols):
            nc.tensor.matmul_mx(
                out=acc,
                lhsT=h_words[b, o][:].bitcast(FP8X4),
                lhsT_scale=h_scales[b, o][:],
                rhs=node_words[o][:, cols].bitcast(FP8X4),
                rhs_scale=node_scales[SCALE_ROWS * o : P, cols],
                start=(o == 0),
                stop=(o == PASSES - 1),
            )

        node_parts = [slice(0, S // 2), slice(S // 2, S)]
        first_accs = [in_bank([P, part.stop - part.start], "first_acc%d" % n, n) for n, part in enumerate(node_parts)]
        accs = {
            3: in_bank([P, S], "acc3", 5)[:],
        }
        ys = [placed([P, S], F32, "y%d" % b, WORDS_1 + 3 * KIB // 2 if b == 1 else None) for b in range(BANDS)]

        split_accs = {
            1: [in_bank([P, S // 2], "acc1_0", 4)[:], in_bank([P, 2, S], "acc1_1", 2)[:, 1, 0 : S // 2]],
            2: [in_bank([P, S // 2], "acc2_%d" % n, bank)[:] for n, bank in enumerate((0, 7))],
        }

        def multiply(b, o):
            if b in split_accs:
                for n in range(2):
                    product(split_accs[b][n], b, o, node_parts[n])
            else:
                product(accs[b], b, o, slice(0, S))

        def empty(b):
            if b in split_accs:
                for n in range(2):
                    nc.vector.tensor_copy(out=ys[b][:, node_parts[n]], in_=split_accs[b][n])
            else:
                nc.vector.tensor_copy(out=ys[b][:], in_=accs[b])

        sigmoid_pairs = {
            (b, pair): placed([P, 2, U], F32, "sigmoids%d_%d" % (b, pair), {(0, 1): PAIR_0, (1, 1): FOURTH}.get((b, pair))) for b in range(BANDS) for pair in range(D // 2)
        }
        sigmoids = {(b, d): sigmoid_pairs[b, d // 2][:, d % 2, :] for b in range(BANDS) for d in range(D)}
        links = (2, 3, 3)

        flip_banks = ((2, 3), (1, 0, 3), (5, 1, 0))
        flipped = {
            (b, d): in_bank([P, HALVES, P], "flipped%d_%d" % (b, d), bank)[:]
            for b in range(LAST)
            for d, bank in enumerate(flip_banks[b])
            if (b, d) != (0, 0)
        }
        first_span = in_bank([P, 2, S], "first_span", 1)
        flipped[0, 0] = first_span[:, 1, 0:U].rearrange("p (h t) -> p h t", h=HALVES)
        back = [in_bank([P, U], "back%d" % b, bank) for b, bank in enumerate((2, 7, 4))]
        chain_start = {(0, 0): rounded_start[2, 1], (1, 0): rounded_start[2, 1], (1, 1): CHAIN_1_0, (2, 0): CLOSING + KIB, (2, 1): CLOSING + 4 * KIB}
        result_start = {0: CHAIN_1_0, 1: CLOSING + KIB // 2}
        chain = {
            (b, d): placed([P, HALVES, P], F32, "chain%d_%d" % (b, d), chain_start.get((b, d)))
            for b in range(LAST)
            for d in range(links[b])
        }
        shifted_pairs = [placed([P, 2, U], F32, "shifted_pair%d" % b, rounded_start[3, 1]) for b in range(1)]
        shifted_start = {0: TURN_3, 1: rounded_start[3, 1], 2: FOURTH + KIB}
        shifted = [placed([P, U], F32, "shifted%d" % b, shifted_start.get(b)) for b in range(LAST)]
        signed = placed([P, U], F32, "signed", PAIR_0)
        results = [placed([P, U], F32, "result%d" % b, result_start.get(b)) for b in range(BANDS)]

        def gather(b, d, words=slice(0, U)):
            offsets = path_lists[d][:, words.start // 16 : words.stop // 16]
            nc.scalar.activation(sigmoids[b, d][:, words], ys[b][:].indirect(offsets), SIGMOID)

        def flip(b, d):
            for h in range(HALVES):
                nc.tensor.transpose(flipped[b, d][:, h, :], sigmoids[b, d][:, half(h)], identity[:])

        def link_half(b, d, h, source):
            base = base_cols[:, HALVES * d + h : HALVES * d + h + 1]
            target = chain[b, d][:, h, :]
            if d == 0:
                nc.vector.tensor_scalar(target, source, base, sign_cols[:, h : h + 1], SUBTRACT, MULT)
            else:
                nc.vector.scalar_tensor_tensor(target, source, base, chain[b, d - 1][:, h, :], SUBTRACT, MULT)

        def link(b, d):
            for h in range(HALVES):
                link_half(b, d, h, flipped[b, d][:, h, :])

        def turn_back(b):
            for h in range(HALVES):
                nc.tensor.transpose(back[b][:, half(h)], chain[b, links[b] - 1][:, h, :], identity[:])

        def shift(b):
            if links[b] == LINKS:
                nc.gpsimd.tensor_tensor(shifted[b][:], sigmoids[b, D - 1], bases[:, 1, :], SUBTRACT)
            else:
                nc.gpsimd.tensor_tensor(shifted_pairs[b][:], sigmoid_pairs[b, 1][:], bases[:], SUBTRACT)

        def finish(b):
            nc.vector.tensor_tensor(results[b][:], shifted[b][:], back[b][:], MULT)
            nc.sync.dma_start(out=out[half(b), :], in_=results[b][:])

        dst, src = rounding_views(0, 0)
        nc.scalar.copy(out=dst, in_=src)
        quantize_h(0, 0)
        for n in range(2):
            product(first_accs[n][:], 0, 0, node_parts[n])
        dst, src = rounding_views(0, 1)
        nc.vector.tensor_copy(out=dst[:, 0:VECTOR_RUNS], in_=src[:, 0:VECTOR_RUNS])
        nc.scalar.copy(out=dst[:, VECTOR_RUNS:RUNS], in_=src[:, VECTOR_RUNS:RUNS])
        quantize_h(0, 1)
        for n in range(2):
            product(first_accs[n][:], 0, 1, node_parts[n])

        bases = placed([P, 2, U], F32, "bases", RAW_0)
        nc.scalar.activation(bases[:], spread[1], COPY, bias=0.5, scale=-0.5)
        nc.scalar.copy(out=ys[0][:, node_parts[0]], in_=first_accs[0][:])
        nc.vector.tensor_copy(out=ys[0][:, node_parts[1]], in_=first_accs[1][:])
        for o in range(PASSES):
            round_h(1, o)
            quantize_h(1, o)
            multiply(1, o)
        for d in range(D):
            gather(0, d)

        round_h(2, 0)
        quantize_h(2, 0)
        multiply(2, 0)
        nc.gpsimd.tensor_scalar(
            h_bf16[LAST, 0][:].rearrange("p (t j) -> p t j", j=PACK),
            h_raw[LAST, 0].rearrange("p j t -> p t j"),
            1.0,
            0.0,
            MULT,
            ADD,
        )
        empty(1)
        for d in range(links[0]):
            flip(0, d)
        for d in range(D):
            gather(1, d)
        round_h(2, 1)
        round_h(3, 1)
        quantize_h(2, 1)
        multiply(2, 1)
        for o in range(PASSES):
            quantize_h(3, o)
            multiply(3, o)
        shift(0)
        link(0, 0)
        flip(1, 0)
        empty(2)
        flip(1, 1)
        for d in range(D):
            gather(2, d)
        link(0, 1)
        flip(1, 2)
        turn_back(0)
        empty(3)
        flip(2, 0)
        link(1, 0)
        nc.vector.tensor_tensor(signed[:], ys[LAST][:].indirect(path_lists[D - 1][:]), turns[D - 1], MULT)
        nc.scalar.activation(sigmoids[LAST, D - 1], signed[:], SIGMOID)
        nc.gpsimd.tensor_tensor(shifted[0][:], shifted_pairs[0][:, 0, :], shifted_pairs[0][:, 1, :], MULT)
        gather(LAST, 0)
        gather(LAST, 1)
        for h in range(HALVES):
            gather(LAST, 2, half(h))
        shift(1)
        flip(2, 1)
        link(1, 1)
        flip(2, 2)
        link(1, 2)
        turn_back(1)
        finish(0)
        link(2, 0)
        link(2, 1)
        finish(1)
        link(2, 2)
        shift(2)
        turn_back(2)

        centred_pair = placed([P, 2, U], F32, "centred_pair", CLOSING + 3 * KIB // 2)
        centred = [centred_pair[:, 0, :], centred_pair[:, 1, :], placed([P, U], F32, "centred2", CLOSING + 4 * KIB)[:]]
        so_far = [placed([P, U], F32, "so_far%d" % d)[:] for d in range(2)]
        before = [sigmoids[LAST, D - 1]] + so_far

        def centre(d, words):
            nc.vector.scalar_tensor_tensor(
                centred[d][:, words], sigmoids[LAST, d][:, words], -0.5, turns[d][:, words], ADD, MULT
            )

        def extend(target, d, words):
            nc.vector.scalar_tensor_tensor(target[:, words], centred[d][:, words], 0.5, before[d][:, words], ADD, MULT)

        every = slice(0, U)
        centre(0, every)
        finish(2)
        extend(so_far[0], 0, every)
        centre(1, every)
        extend(so_far[1], 1, every)
        for h in range(HALVES):
            centre(2, half(h))
        for h in range(HALVES):
            extend(results[LAST], 2, half(h))
            nc.sync.dma_start(out=out[half(LAST), half(h)], in_=results[LAST][:, half(h)])
